import numpy as np
import ml_dtypes


def mxq(x, axis, fmt="e4m3"):
    dtype, down = {"e4m3": (ml_dtypes.float8_e4m3fn, 7), "e5m2": (ml_dtypes.float8_e5m2, 14)}[fmt]
    v = np.moveaxis(np.asarray(x, np.float32).astype(ml_dtypes.bfloat16).astype(np.float64), axis, -1)
    blocks = v.reshape(v.shape[:-1] + (-1, 32))
    amax = np.abs(blocks).max(-1, keepdims=True)
    byte = np.maximum(np.where(amax > 0, np.frexp(amax)[1] - 1 + 127, 0) - down, 1)
    scale = np.exp2(byte - 127.0)
    codes = (blocks / scale).astype(np.float32).astype(dtype).astype(np.float64)
    return np.moveaxis((codes * scale).reshape(v.shape), -1, axis)


WIDE = False


def mx_kscale(k):
    if not WIDE:
        return np.ones(k)
    levels = np.array([10, -10, 5, -5, 0])
    if k % 512:
        return np.exp2(np.random.permutation(np.resize(levels, k // 32))).repeat(32)
    a = np.empty((k // 512, 16))
    for p in range(k // 512):
        a[p, :8] = np.random.permutation(np.resize(levels, 8))
        for g in range(8):
            far = levels[np.abs(levels - a[p, g]) >= 10]
            a[p, g + 8] = far[np.random.randint(len(far))]
    return np.exp2(a.ravel()).repeat(32)


def f64(x):
    return np.asarray(x).astype(np.float64)


def striped(idx):
    return np.tile(idx.reshape(-1, 16).T, (8, 1)).astype(np.uint16)


def unstriped(offs):
    return offs[:16].T.reshape(-1).astype(np.int64)


def pack_weight(w):
    k, n = w.shape
    w = f64(np.asarray(w, np.float32).astype(ml_dtypes.bfloat16)).reshape(k // 32, 32, n)
    amax = np.abs(w).max(1)
    byte = np.clip(np.where(amax > 0, np.frexp(amax)[1] - 1 + 127 - 7, 1), 1, 254)
    scaled = (w * np.exp2(127.0 - byte)[:, None, :]).reshape(k, n).astype(np.float32)
    words = np.ascontiguousarray(scaled.reshape(k // 512, 128, 4, n).transpose(0, 1, 3, 2)).astype(ml_dtypes.float8_e4m3fn).view(np.uint8)
    return words, np.ascontiguousarray(byte.astype(np.uint8).reshape(k // 512, 16, n))


def unpack_weight(words, scales):
    g, p, n, _ = words.shape
    vals = np.ascontiguousarray(words).view(ml_dtypes.float8_e4m3fn).astype(np.float64) * np.repeat(np.exp2(scales.astype(np.float64) - 127.0), 8, axis=1)[..., None]
    return vals.transpose(0, 1, 3, 2).reshape(g * 512, n)


E2M1 = np.array([0.0, 0.5, 1.0, 1.5, 2.0, 3.0, 4.0, 6.0, -0.0, -0.5, -1.0, -1.5, -2.0, -3.0, -4.0, -6.0])


def pack_fp4(w):
    k, n = w.shape
    w = f64(np.asarray(w, np.float32).astype(ml_dtypes.bfloat16)).reshape(k // 32, 32, n)
    amax = np.abs(w).max(1)
    mant, ex = np.frexp(amax / 6.0)
    byte = np.clip(np.where(amax > 0, np.where(mant > 0.5, ex, ex - 1) + 127, 1), 1, 254)
    scaled = (w * np.exp2(127.0 - byte)[:, None, :]).reshape(k, n).astype(np.float32)
    c = np.ascontiguousarray(scaled.reshape(k // 512, 128, 4, n).transpose(0, 1, 3, 2)).astype(ml_dtypes.float4_e2m1fn).view(np.uint8) & 0xF
    words = (c[..., 0::2] | (c[..., 1::2] << 4)).reshape(k // 512, 128, 2 * n)
    return np.ascontiguousarray(words), np.ascontiguousarray(byte.astype(np.uint8).reshape(k // 512, 16, n))


def unpack_fp4(words, scales):
    g, _, n = scales.shape
    words = np.ascontiguousarray(words).reshape(g, 128, n, 2)
    nib = np.empty((g, 128, n, 4), np.uint8)
    nib[..., 0::2] = words & 0xF
    nib[..., 1::2] = words >> 4
    vals = E2M1[nib] * np.repeat(np.exp2(scales.astype(np.float64) - 127.0), 8, axis=1)[..., None]
    return vals.transpose(0, 1, 3, 2).reshape(g * 512, n)


def relu(v):
    return np.maximum(v, 0.0)


K, T, H, N = 1024, 512, 512, 256


def setup_inputs():
    n = np.random.standard_normal
    s = mx_kscale(K)[:, None]
    u = mx_kscale(H)
    packed_xT = pack_weight(n((K, T)) * s)
    packed_w2 = pack_fp4(n((H, N)) / np.sqrt(2 * H) / u[:, None])
    packed_w3 = pack_fp4(n((H, N)) / np.sqrt(2 * H) / u[:, None])
    return {
        "x_words": packed_xT[0],
        "x_scales": packed_xT[1],
        "w1": (n((K, H)) / np.sqrt(K) / s * u).astype(np.float32),
        "w2_words": packed_w2[0],
        "w2_scales": packed_w2[1],
        "w3_words": packed_w3[0],
        "w3_scales": packed_w3[1],
        "pos1": striped(np.random.permutation(T)),
        "pos2": striped(np.random.permutation(T)),
        "pos3": striped(np.random.permutation(T)),
    }


def reference(x_words, x_scales, w1, w2_words, w2_scales, w3_words, w3_scales, pos1, pos2, pos3):
    xq = unpack_weight(x_words, x_scales)
    h = relu(mxq(f64(w1), 0, "e4m3").T @ xq)
    z = np.maximum(np.maximum(h[:, unstriped(pos1)], h[:, unstriped(pos2)]), h[:, unstriped(pos3)])
    return relu(unpack_fp4(w2_words, w2_scales).T @ mxq(h, 0, "e4m3") + unpack_fp4(w3_words, w3_scales).T @ mxq(z, 0, "e4m3"))

@@ -1,0 +1,211 @@
+from contextlib import ExitStack
+
+import concourse.mybir as mybir
+
+K, T, H, N = 1024, 512, 512, 256
+FLOPS = 2 * K * H * T + 2 * 2 * H * N * T
+
+F32 = mybir.dt.float32
+BF16 = mybir.dt.bfloat16
+I32 = mybir.dt.int32
+U32 = mybir.dt.uint32
+U16 = mybir.dt.uint16
+U8 = mybir.dt.uint8
+FP8X4 = mybir.dt.float8_e4m3fn_x4
+FP4X4 = mybir.dt.float4_e2m1fn_x4
+ACT = mybir.ActivationFunctionType
+ALU = mybir.AluOpType
+
+P = 128
+PACK = 4
+PASSES = K // (P * PACK)
+WIN = 704
+QW = 128
+NQ = T // QW
+LISTS = 3
+
+
+def tile_picked_wsagecat_maxrelu_l_kernel(
+    tc, x_words, x_scales, w1, w2_words, w2_scales, w3_words, w3_scales, pos1, pos2, pos3, out
+):
+    nc = tc.nc
+    with ExitStack() as ctx:
+        keep = ctx.enter_context(tc.tile_pool(name="keep", bufs=1))
+        psum = ctx.enter_context(tc.psum_pool(name="psum", bufs=1))
+
+        lists = [keep.tile([P, T // 16], U16, name=f"list{d}") for d in range(LISTS)]
+        x_sc = keep.tile([P, PASSES, T], U8, name="x_sc", align_bytes=64)
+        w_sc = keep.tile([P, 2, N], U8, name="w_sc", align_bytes=64)
+        hs = keep.tile([P, PACK, WIN], F32, name="hs", align_bytes=64)
+        nc.vector.memset(x_sc[:].rearrange("p z c -> p (z c)").bitcast(I32), 0)
+        nc.gpsimd.memset(w_sc[:].rearrange("p z c -> p (z c)").bitcast(I32), 0)
+        nc.gpsimd.memset(hs[:, 0 : PACK - 1, T:WIN], 0.0)
+
+        HALF = H // 2
+        raw = {}
+        x_w = []
+        w1v = w1.rearrange("(z p j) c -> z p j c", z=PASSES, j=PACK)
+        for z in range(PASSES):
+            for c in range(2):
+                raw[z, c] = keep.tile([P, PACK, HALF], F32, name=f"raw{z}{c}", align_bytes=64)
+                nc.sync.dma_start(out=raw[z, c][:], in_=w1v[z, :, :, c * HALF : (c + 1) * HALF])
+            x_w.append(keep.tile([P, T], U32, name=f"x_w{z}", align_bytes=64))
+            nc.sync.dma_start(out=x_w[z][:].bitcast(I32), in_=x_words[z].rearrange("p c r -> p (c r)").bitcast(I32))
+            if z == 0:
+                xs_v = x_scales.bitcast(I32).rearrange("z (q r) c -> r q z c", r=PACK)
+                for r in range(PACK):
+                    nc.scalar.dma_start(out=x_sc[r:P:32, :, :].bitcast(I32), in_=xs_v[r])
+        for d, pos in enumerate((pos1, pos2, pos3)):
+            nc.sync.dma_start(lists[d][:], pos)
+        w_w = []
+        for a, (words, scales) in enumerate(((w2_words, w2_scales), (w3_words, w3_scales))):
+            sv = scales[0].bitcast(I32).rearrange("(q r) c -> r q c", r=PACK)
+            for r in range(PACK):
+                nc.sync.dma_start(out=w_sc[r:P:32, a, :].bitcast(I32), in_=sv[r])
+        for a, words in enumerate((w2_words, w3_words)):
+            w_w.append(keep.tile([P, 2 * N], U8, name=f"w_w{a}", align_bytes=64))
+            nc.sync.dma_start(out=w_w[a][:].bitcast(I32), in_=words[0].bitcast(I32))
+
+        MH = HALF // PACK
+        wq = [keep.tile([P, PACK, P, PACK], BF16, name=f"wq{z}", align_bytes=64) for z in range(PASSES)]
+        w1c = [keep.tile([P, H], U32, name=f"w1c{z}", align_bytes=64) for z in range(PASSES)]
+        w1s = [keep.tile([P, H], U8, name=f"w1s{z}", align_bytes=64) for z in range(PASSES)]
+
+        def cast_views(z, c, t0, t1):
+            src = raw[z, c][:].rearrange("p j (m t) -> p m j t", t=PACK)[:, :, :, t0:t1]
+            dst = wq[z][:, t0:t1, c * MH : (c + 1) * MH, :].rearrange("p t m j -> p m j t")
+            return dst, src
+
+        def quant_w1(z, t0, t1):
+            nc.vector.quantize_mx(
+                out=w1c[z][:, t0 * P : t1 * P].bitcast(FP8X4),
+                scales=w1s[z][:, t0 * P : t1 * P],
+                in_=wq[z][:, t0:t1, :, :].rearrange("p t m j -> p (t m j)"),
+            )
+
+        hb = [psum.tile([P, T], F32, name=f"hb{t}") for t in range(PACK)]
+
+        def first(t, z):
+            nc.tensor.matmul_mx(
+                out=hb[t][:],
+                lhsT=w1c[z][:, t * P : (t + 1) * P].bitcast(FP8X4),
+                lhsT_scale=w1s[z][:, t * P : (t + 1) * P],
+                rhs=x_w[z][:].bitcast(FP8X4),
+                rhs_scale=x_sc[:, z, :],
+                start=(z == 0),
+                stop=(z == PASSES - 1),
+            )
+
+        dst, src = cast_views(0, 0, 0, PACK)
+        nc.scalar.activation(dst, src, ACT.Copy)
+        nc.vector.tensor_copy(*cast_views(0, 1, 0, PACK))
+        quant_w1(0, 0, PACK)
+        for t in range(PACK):
+            first(t, 0)
+        nc.vector.tensor_copy(*cast_views(1, 0, 0, PACK))
+        nc.vector.tensor_copy(*cast_views(1, 1, 0, 1))
+        quant_w1(1, 0, 1)
+        first(0, 1)
+        nc.scalar.activation(hs[:, 0, 0:T], hb[0][:], ACT.Relu)
+        nc.vector.tensor_copy(*cast_views(1, 1, 1, PACK))
+        quant_w1(1, 1, 2)
+        quant_w1(1, 2, PACK)
+        for t in range(1, PACK):
+            first(t, 1)
+            nc.scalar.activation(hs[:, t, 0:T], hb[t][:], ACT.Relu)
+
+        h4 = keep.tile([P, T, PACK], BF16, name="h4", align_bytes=64)
+        nc.scalar.copy(
+            h4[:].rearrange("p (c i) t -> p c t i", i=4), hs[:, :, 0:T].rearrange("p t (c i) -> p c t i", i=4)
+        )
+        hc = keep.tile([P, T], U32, name="hc", align_bytes=64)
+        hsc = keep.tile([P, T], U8, name="hsc", align_bytes=64)
+
+        zp = keep.tile([P, NQ, PACK, QW], BF16, name="zp", align_bytes=64)
+        pending = []
+        for t in range(PACK - 1):
+            g = keep.tile([P, NQ, LISTS, QW], BF16, name=f"g{t}", align_bytes=64)
+            m = keep.tile([P, NQ, QW], BF16, name=f"m{t}", align_bytes=64)
+            for d in range(LISTS):
+                nc.vector.tensor_copy(g[:, :, d, :], hs[:, t, :].indirect(lists[d][:]))
+                if pending:
+                    nc.vector.tensor_tensor(*pending[0], ALU.max)
+                    pending.clear()
+            nc.vector.tensor_tensor(m[:], g[:, :, 0, :], g[:, :, 1, :], ALU.max)
+            pending.append((zp[:, :, t, :], m[:], g[:, :, 2, :]))
+
+        outv = out.rearrange("(b p) v -> p b v", p=P)
+        zc = keep.tile([P, T], U32, name="zc", align_bytes=64)
+        zsc = keep.tile([P, T], U8, name="zsc", align_bytes=64)
+        z4 = {}
+
+        def second(dst, b, q, a):
+            codes, scales = ((hc, hsc), (zc, zsc))[a]
+            nc.tensor.matmul_mx(
+                out=dst,
+                lhsT=w_w[a][:, 2 * P * b : 2 * P * (b + 1)].bitcast(FP4X4),
+                lhsT_scale=w_sc[:, a, P * b : P * (b + 1)],
+                rhs=codes[:, q * QW : (q + 1) * QW].bitcast(FP8X4),
+                rhs_scale=scales[:, q * QW : (q + 1) * QW],
+                start=(a == 0),
+                stop=(a == 1),
+            )
+
+        def quant_z(q):
+            nc.vector.quantize_mx(
+                out=zc[:, q * QW : (q + 1) * QW].bitcast(FP8X4),
+                scales=zsc[:, q * QW : (q + 1) * QW],
+                in_=z4[q][:].rearrange("p v t -> p (v t)"),
+            )
+
+        def finish(q):
+            quant_z(q)
+            ob = psum.tile([P, 2, QW], F32, name="ob", bufs=2)
+            for b in range(2):
+                second(ob[:, b, :], b, q, 0)
+                second(ob[:, b, :], b, q, 1)
+            res = keep.tile([P, 2, QW], F32, name=f"res{q}")
+            nc.scalar.activation(res[:], ob[:], ACT.Relu)
+            nc.sync.dma_start(out=outv[:, :, q * QW : (q + 1) * QW], in_=res[:])
+
+        t = PACK - 1
+        last = [psum.tile([P, QW], F32, name=f"last{b}") for b in range(2)]
+        for q in range(NQ):
+            if q >= 2:
+                finish(q - 2)
+            g = keep.tile([P, 2, LISTS, QW // 2], BF16, name=f"gq{q}", tag=f"hold{q % 2}", align_bytes=64)
+            m = keep.tile([P, 2, QW // 2], BF16, name=f"mq{q}", align_bytes=64)
+            cols = slice(q * QW // 16, (q + 1) * QW // 16)
+            for d in range(LISTS):
+                nc.vector.tensor_copy(g[:, :, d, :], hs[:, t, 0:T].indirect(lists[d][:, cols]))
+                if pending:
+                    nc.vector.tensor_tensor(*pending[0], ALU.max)
+                    pending.clear()
+            if q == 0:
+                nc.vector.quantize_mx(out=hc[:].bitcast(FP8X4), scales=hsc[:], in_=h4[:].rearrange("p v t -> p (v t)"))
+                for b in range(2):
+                    second(last[b][:], b, NQ - 1, 0)
+            nc.vector.tensor_tensor(m[:], g[:, :, 0, :], g[:, :, 1, :], ALU.max)
+            nc.vector.tensor_tensor(
+                zp[:, q, t, :].rearrange("p (a b) -> p a b", a=2), m[:], g[:, :, 2, :], ALU.max
+            )
+            tag = f"hold{q % 2}" if q < 2 else f"z4_{q}"
+            z4[q] = keep.tile([P, QW, PACK], BF16, name=f"z4_{q}", tag=tag, align_bytes=64)
+            dst = z4[q][:].rearrange("p (c i) t -> p c t i", i=4)
+            src = zp[:, q, :, :].rearrange("p t (c i) -> p c t i", i=4)
+            if q < NQ - 1:
+                nc.scalar.copy(dst, src)
+            else:
+                nc.vector.tensor_copy(dst, src)
+        finish(NQ - 2)
+        q = NQ - 1
+        quant_z(q)
+        for b in range(2):
+            second(last[b][:], b, q, 1)
+            res = keep.tile([P, QW], F32, name=f"resl{b}")
+            if b == 0:
+                nc.scalar.activation(res[:], last[b][:], ACT.Relu)
+                nc.scalar.dma_start(out=outv[:, b, q * QW : (q + 1) * QW], in_=res[:])
+            else:
+                nc.vector.tensor_scalar_max(res[:], last[b][:], 0.0)
+                nc.sync.dma_start(out=outv[:, b, q * QW : (q + 1) * QW], in_=res[:])

@@ -37,26 +37,32 @@ def tile_picked_wsagecat_maxrelu_l_kernel(
         x_sc = keep.tile([P, PASSES, T], U8, name="x_sc", align_bytes=64)
         w_sc = keep.tile([P, 2, N], U8, name="w_sc", align_bytes=64)
         hs = keep.tile([P, PACK, WIN], F32, name="hs", align_bytes=64)
-        nc.vector.memset(x_sc[:].rearrange("p z c -> p (z c)").bitcast(I32), 0)
-        nc.gpsimd.memset(w_sc[:].rearrange("p z c -> p (z c)").bitcast(I32), 0)
-        nc.gpsimd.memset(hs[:, 0 : PACK - 1, T:WIN], 0.0)
+        hh = [keep.tile([P, WIN], F32, name=f"hh{c}", align_bytes=64) for c in range(2)]
 
         HALF = H // 2
+        MH = HALF // PACK
         raw = {}
         x_w = []
         w1v = w1.rearrange("(z p j) c -> z p j c", z=PASSES, j=PACK)
+        poss = (pos1, pos2, pos3)
+
+        def load_w1(z, c):
+            raw[z, c] = keep.tile([P, PACK, HALF], F32, name=f"raw{z}{c}", align_bytes=64)
+            nc.sync.dma_start(out=raw[z, c][:], in_=w1v[z, :, :, c * HALF : (c + 1) * HALF])
+
+        xs_v = x_scales.bitcast(I32).rearrange("z (q r) c -> r q z c", r=PACK)
+        for r in range(PACK):
+            nc.scalar.dma_start(out=x_sc[r:P:32, :, :].bitcast(I32), in_=xs_v[r])
         for z in range(PASSES):
-            for c in range(2):
-                raw[z, c] = keep.tile([P, PACK, HALF], F32, name=f"raw{z}{c}", align_bytes=64)
-                nc.sync.dma_start(out=raw[z, c][:], in_=w1v[z, :, :, c * HALF : (c + 1) * HALF])
+            load_w1(z, 0)
+        for z in range(PASSES):
             x_w.append(keep.tile([P, T], U32, name=f"x_w{z}", align_bytes=64))
             nc.sync.dma_start(out=x_w[z][:].bitcast(I32), in_=x_words[z].rearrange("p c r -> p (c r)").bitcast(I32))
-            if z == 0:
-                xs_v = x_scales.bitcast(I32).rearrange("z (q r) c -> r q z c", r=PACK)
-                for r in range(PACK):
-                    nc.scalar.dma_start(out=x_sc[r:P:32, :, :].bitcast(I32), in_=xs_v[r])
-        for d, pos in enumerate((pos1, pos2, pos3)):
-            nc.sync.dma_start(lists[d][:], pos)
+        nc.sync.dma_start(lists[0][:], pos1)
+        for z in range(PASSES):
+            load_w1(z, 1)
+        for d in range(1, LISTS):
+            nc.sync.dma_start(lists[d][:], poss[d])
         w_w = []
         for a, (words, scales) in enumerate(((w2_words, w2_scales), (w3_words, w3_scales))):
             sv = scales[0].bitcast(I32).rearrange("(q r) c -> r q c", r=PACK)
@@ -66,53 +72,123 @@ def tile_picked_wsagecat_maxrelu_l_kernel(
             w_w.append(keep.tile([P, 2 * N], U8, name=f"w_w{a}", align_bytes=64))
             nc.sync.dma_start(out=w_w[a][:].bitcast(I32), in_=words[0].bitcast(I32))
 
-        MH = HALF // PACK
-        wq = [keep.tile([P, PACK, P, PACK], BF16, name=f"wq{z}", align_bytes=64) for z in range(PASSES)]
-        w1c = [keep.tile([P, H], U32, name=f"w1c{z}", align_bytes=64) for z in range(PASSES)]
-        w1s = [keep.tile([P, H], U8, name=f"w1s{z}", align_bytes=64) for z in range(PASSES)]
+        w1c = {}
+        w1s = {}
+        for z in range(PASSES):
+            for k in range(PACK):
+                w1c[z, k] = keep.tile([P, P], U32, name=f"w1c{z}{k}", align_bytes=64)
+                w1s[z, k] = keep.tile([P, P], U8, name=f"w1s{z}{k}", align_bytes=64)
+        wq = {}
 
-        def cast_views(z, c, t0, t1):
-            src = raw[z, c][:].rearrange("p j (m t) -> p m j t", t=PACK)[:, :, :, t0:t1]
-            dst = wq[z][:, t0:t1, c * MH : (c + 1) * MH, :].rearrange("p t m j -> p m j t")
-            return dst, src
+        def cast(eng, z, c, u, tag):
+            wq[z, c, u] = keep.tile([P, 2, MH, PACK], BF16, name=f"wq{z}{c}{u}", tag=tag, align_bytes=64)
+            src = raw[z, c][:].rearrange("p j (m t) -> p m j t", t=PACK)[:, :, :, 2 * u : 2 * u + 2]
+            dst = wq[z, c, u][:].rearrange("p t m j -> p m j t")
+            if eng == "s":
+                nc.scalar.activation(dst, src, ACT.Copy)
+            else:
+                nc.vector.tensor_copy(dst, src)
 
-        def quant_w1(z, t0, t1):
-            nc.vector.quantize_mx(
-                out=w1c[z][:, t0 * P : t1 * P].bitcast(FP8X4),
-                scales=w1s[z][:, t0 * P : t1 * P],
-                in_=wq[z][:, t0:t1, :, :].rearrange("p t m j -> p (t m j)"),
-            )
+        def quant_w1(z, c, u):
+            if u == 0:
+                nc.vector.quantize_mx(
+                    out=w1c[z, c][:].bitcast(FP8X4),
+                    scales=w1s[z, c][:],
+                    in_=wq[z, c, u][:].rearrange("p t m j -> p (t m j)"),
+                )
+            else:
+                for t in range(2):
+                    nc.vector.quantize_mx(
+                        out=w1c[z, 2 + t][:, c * MH : (c + 1) * MH].bitcast(FP8X4),
+                        scales=w1s[z, 2 + t][:, c * MH : (c + 1) * MH],
+                        in_=wq[z, c, u][:, t, :, :].rearrange("p m j -> p (m j)"),
+                    )
 
-        hb = [psum.tile([P, T], F32, name=f"hb{t}") for t in range(PACK)]
+        TH = T // 2
+        hb = {(k, 0): psum.tile([P, T], F32, name=f"hb{k}", tag=f"bank{k}") for k in range(1, PACK)}
+        hb[0, 0] = psum.tile([P, TH], F32, name="hb0", tag="bank0")
+        hb[0, 1] = psum.tile([P, TH], F32, name="hb4", tag="bank4")
 
-        def first(t, z):
-            nc.tensor.matmul_mx(
-                out=hb[t][:],
-                lhsT=w1c[z][:, t * P : (t + 1) * P].bitcast(FP8X4),
-                lhsT_scale=w1s[z][:, t * P : (t + 1) * P],
-                rhs=x_w[z][:].bitcast(FP8X4),
-                rhs_scale=x_sc[:, z, :],
-                start=(z == 0),
-                stop=(z == PASSES - 1),
-            )
+        def first(k, z):
+            parts = 2 if k == 0 else 1
+            width = T // parts
+            for s in range(parts):
+                nc.tensor.matmul_mx(
+                    out=hb[k, s][:],
+                    lhsT=w1c[z, k][:].bitcast(FP8X4),
+                    lhsT_scale=w1s[z, k][:],
+                    rhs=x_w[z][:, s * width : (s + 1) * width].bitcast(FP8X4),
+                    rhs_scale=x_sc[:, z, s * width : (s + 1) * width],
+                    start=(z == 0),
+                    stop=(z == PASSES - 1),
+                )
 
-        dst, src = cast_views(0, 0, 0, PACK)
-        nc.scalar.activation(dst, src, ACT.Copy)
-        nc.vector.tensor_copy(*cast_views(0, 1, 0, PACK))
-        quant_w1(0, 0, PACK)
-        for t in range(PACK):
-            first(t, 0)
-        nc.vector.tensor_copy(*cast_views(1, 0, 0, PACK))
-        nc.vector.tensor_copy(*cast_views(1, 1, 0, 1))
-        quant_w1(1, 0, 1)
+        zp = keep.tile([P, NQ, PACK, QW], BF16, name="zp", align_bytes=64)
+        zt = keep.tile([P, NQ, QW], BF16, name="zt", align_bytes=64)
+        HP = P // 2
+        lo, hi = slice(0, HP), slice(HP, P)
+
+        def gather(k, d, window, tag):
+            g = keep.tile([P, NQ, QW + 32], BF16, name=f"g{k}{d}", tag=tag, align_bytes=64)
+            nc.vector.tensor_copy(g[:, :, 0:QW], window.indirect(lists[d][:]))
+            return g[:, :, 0:QW]
+
+        def evacuate(c):
+            parts = 2 if c == 0 else 1
+            width = T // parts
+            for s in range(parts):
+                nc.scalar.activation(hh[c][:, s * width : (s + 1) * width], hb[c, s][:], ACT.Relu)
+            own = (lo, hi)[c]
+            nc.sync.dma_start(out=hs[own, 0, 0:T], in_=hh[c][lo, 0:T])
+            nc.sync.dma_start(out=hs[own, 1, 0:T], in_=hh[c][hi, 0:T])
+
+        cast("s", 0, 0, 1, "wq001")
+        cast("v", 0, 0, 0, "wq000")
+        quant_w1(0, 0, 0)
+        cast("v", 1, 0, 0, "wq100")
+        cast("s", 1, 0, 1, "wq101")
+        quant_w1(1, 0, 0)
+        first(0, 0)
         first(0, 1)
-        nc.scalar.activation(hs[:, 0, 0:T], hb[0][:], ACT.Relu)
-        nc.vector.tensor_copy(*cast_views(1, 1, 1, PACK))
-        quant_w1(1, 1, 2)
-        quant_w1(1, 2, PACK)
-        for t in range(1, PACK):
-            first(t, 1)
-            nc.scalar.activation(hs[:, t, 0:T], hb[t][:], ACT.Relu)
+        evacuate(0)
+        quant_w1(0, 0, 1)
+        quant_w1(1, 0, 1)
+
+        m = [keep.tile([P, NQ, QW], BF16, name=f"m{k}", align_bytes=64) for k in range(PACK - 1)]
+        cast("s", 0, 1, 0, "wait0")
+        cast("s", 1, 1, 0, "wait1")
+        g0 = gather(0, 0, hh[0][:], "g00")
+        quant_w1(0, 1, 0)
+        first(1, 0)
+        g1 = gather(0, 1, hh[0][:], "wait0")
+        quant_w1(1, 1, 0)
+        first(1, 1)
+        cast("s", 0, 1, 1, "wait2")
+        evacuate(1)
+        cast("s", 1, 1, 1, "wait3")
+        g2 = gather(0, 2, hh[0][:], "wait1")
+        nc.vector.tensor_tensor(m[0][:], g0, g1, ALU.max)
+        quant_w1(0, 1, 1)
+        first(2, 0)
+        first(3, 0)
+        g0 = gather(1, 0, hh[1][:], "wait2")
+        nc.vector.tensor_tensor(zp[:, :, 0, :], m[0][:], g2, ALU.max)
+        nc.sync.dma_start(out=zp[lo, :, 1, :], in_=zp[hi, :, 0, :])
+        quant_w1(1, 1, 1)
+        for k in range(2, PACK):
+            first(k, 1)
+            nc.scalar.activation(hs[:, k, 0:T], hb[k, 0][:], ACT.Relu)
+        g1 = gather(1, 1, hh[1][:], "wait3")
+        g2 = gather(1, 2, hh[1][:], "g12")
+        nc.vector.tensor_tensor(m[1][:], g0, g1, ALU.max)
+        g0 = gather(2, 0, hs[:, 2, :], "g20")
+        nc.vector.tensor_tensor(zt[:], m[1][:], g2, ALU.max)
+        nc.sync.dma_start(out=zp[hi, :, 0, :], in_=zt[lo, :, :])
+        nc.sync.dma_start(out=zp[hi, :, 1, :], in_=zt[hi, :, :])
+        g1 = gather(2, 1, hs[:, 2, :], "g21")
+        g2 = gather(2, 2, hs[:, 2, :], "g22")
+        nc.vector.tensor_tensor(m[2][:], g0, g1, ALU.max)
+        pending = [(zp[:, :, 2, :], m[2][:], g2)]
 
         h4 = keep.tile([P, T, PACK], BF16, name="h4", align_bytes=64)
         nc.scalar.copy(
@@ -120,19 +196,6 @@ def tile_picked_wsagecat_maxrelu_l_kernel(
         )
         hc = keep.tile([P, T], U32, name="hc", align_bytes=64)
         hsc = keep.tile([P, T], U8, name="hsc", align_bytes=64)
-
-        zp = keep.tile([P, NQ, PACK, QW], BF16, name="zp", align_bytes=64)
-        pending = []
-        for t in range(PACK - 1):
-            g = keep.tile([P, NQ, LISTS, QW], BF16, name=f"g{t}", align_bytes=64)
-            m = keep.tile([P, NQ, QW], BF16, name=f"m{t}", align_bytes=64)
-            for d in range(LISTS):
-                nc.vector.tensor_copy(g[:, :, d, :], hs[:, t, :].indirect(lists[d][:]))
-                if pending:
-                    nc.vector.tensor_tensor(*pending[0], ALU.max)
-                    pending.clear()
-            nc.vector.tensor_tensor(m[:], g[:, :, 0, :], g[:, :, 1, :], ALU.max)
-            pending.append((zp[:, :, t, :], m[:], g[:, :, 2, :]))
 
         outv = out.rearrange("(b p) v -> p b v", p=P)
         zc = keep.tile([P, T], U32, name="zc", align_bytes=64)
@@ -158,54 +221,61 @@ def tile_picked_wsagecat_maxrelu_l_kernel(
                 in_=z4[q][:].rearrange("p v t -> p (v t)"),
             )
 
+        ob = {}
+
         def finish(q):
             quant_z(q)
-            ob = psum.tile([P, 2, QW], F32, name="ob", bufs=2)
-            for b in range(2):
-                second(ob[:, b, :], b, q, 0)
-                second(ob[:, b, :], b, q, 1)
             res = keep.tile([P, 2, QW], F32, name=f"res{q}")
-            nc.scalar.activation(res[:], ob[:], ACT.Relu)
+            for b in range(2):
+                second(ob[q, b][:], b, q, 1)
+                nc.scalar.activation(res[:, b, :], ob[q, b][:], ACT.Relu)
             nc.sync.dma_start(out=outv[:, :, q * QW : (q + 1) * QW], in_=res[:])
 
-        t = PACK - 1
-        last = [psum.tile([P, QW], F32, name=f"last{b}") for b in range(2)]
-        for q in range(NQ):
-            if q >= 2:
-                finish(q - 2)
-            g = keep.tile([P, 2, LISTS, QW // 2], BF16, name=f"gq{q}", tag=f"hold{q % 2}", align_bytes=64)
-            m = keep.tile([P, 2, QW // 2], BF16, name=f"mq{q}", align_bytes=64)
-            cols = slice(q * QW // 16, (q + 1) * QW // 16)
-            for d in range(LISTS):
-                nc.vector.tensor_copy(g[:, :, d, :], hs[:, t, 0:T].indirect(lists[d][:, cols]))
-                if pending:
-                    nc.vector.tensor_tensor(*pending[0], ALU.max)
-                    pending.clear()
-            if q == 0:
-                nc.vector.quantize_mx(out=hc[:].bitcast(FP8X4), scales=hsc[:], in_=h4[:].rearrange("p v t -> p (v t)"))
-                for b in range(2):
-                    second(last[b][:], b, NQ - 1, 0)
-            nc.vector.tensor_tensor(m[:], g[:, :, 0, :], g[:, :, 1, :], ALU.max)
-            nc.vector.tensor_tensor(
-                zp[:, q, t, :].rearrange("p (a b) -> p a b", a=2), m[:], g[:, :, 2, :], ALU.max
-            )
-            tag = f"hold{q % 2}" if q < 2 else f"z4_{q}"
-            z4[q] = keep.tile([P, QW, PACK], BF16, name=f"z4_{q}", tag=tag, align_bytes=64)
+        def interleave(q):
+            z4[q] = keep.tile([P, QW, PACK], BF16, name=f"z4_{q}", tag=f"hold{q}", align_bytes=64)
             dst = z4[q][:].rearrange("p (c i) t -> p c t i", i=4)
             src = zp[:, q, :, :].rearrange("p t (c i) -> p c t i", i=4)
             if q < NQ - 1:
                 nc.scalar.copy(dst, src)
             else:
                 nc.vector.tensor_copy(dst, src)
-        finish(NQ - 2)
+
+        t = PACK - 1
+        for q in range(NQ):
+            g = []
+            cols = slice(q * QW // 16, (q + 1) * QW // 16)
+            for d in range(LISTS):
+                if d == 1 and q >= 2:
+                    finish(q - 2)
+                tag = f"hold{q - 2}" if d == 1 and q >= 2 else f"gq{q}{d}"
+                gt = keep.tile([P, 2, QW // 2 + 32], BF16, name=f"gq{q}{d}", tag=tag, align_bytes=64)
+                g.append(gt[:, :, 0 : QW // 2])
+                nc.vector.tensor_copy(g[d], hs[:, t, 0:T].indirect(lists[d][:, cols]))
+                if d == 0:
+                    nc.vector.tensor_tensor(*pending[0], ALU.max)
+                    pending.clear()
+                    if q > 0:
+                        interleave(q - 1)
+            if q == 0:
+                nc.vector.quantize_mx(out=hc[:].bitcast(FP8X4), scales=hsc[:], in_=h4[:].rearrange("p v t -> p (v t)"))
+                for qq in range(NQ):
+                    for b in range(2):
+                        ob[qq, b] = psum.tile([P, QW], F32, name=f"ob{qq}{b}", tag=f"bank{2 * qq + b}")
+                        second(ob[qq, b][:], b, qq, 0)
+            mq = keep.tile([P, 2, QW // 2], BF16, name=f"mq{q}", align_bytes=64)
+            nc.vector.tensor_tensor(mq[:], g[0], g[1], ALU.max)
+            pending.append((zp[:, q, t, :].rearrange("p (a b) -> p a b", a=2), mq[:], g[2]))
+        nc.vector.tensor_tensor(*pending[0], ALU.max)
         q = NQ - 1
+        interleave(q)
+        finish(NQ - 2)
         quant_z(q)
         for b in range(2):
-            second(last[b][:], b, q, 1)
+            second(ob[q, b][:], b, q, 1)
             res = keep.tile([P, QW], F32, name=f"resl{b}")
             if b == 0:
-                nc.scalar.activation(res[:], last[b][:], ACT.Relu)
+                nc.scalar.activation(res[:], ob[q, b][:], ACT.Relu)
                 nc.scalar.dma_start(out=outv[:, b, q * QW : (q + 1) * QW], in_=res[:])
             else:
-                nc.vector.tensor_scalar_max(res[:], last[b][:], 0.0)
+                nc.vector.tensor_scalar_max(res[:], ob[q, b][:], 0.0)
                 nc.sync.dma_start(out=outv[:, b, q * QW : (q + 1) * QW], in_=res[:])

@@ -19,7 +19,7 @@ ALU = mybir.AluOpType
 P = 128
 PACK = 4
 PASSES = K // (P * PACK)
-WIN = 704
+WIN = 1024
 QW = 128
 NQ = T // QW
 LISTS = 3
@@ -36,8 +36,8 @@ def tile_picked_wsagecat_maxrelu_l_kernel(
         lists = [keep.tile([P, T // 16], U16, name=f"list{d}") for d in range(LISTS)]
         x_sc = keep.tile([P, PASSES, T], U8, name="x_sc", align_bytes=64)
         w_sc = keep.tile([P, 2, N], U8, name="w_sc", align_bytes=64)
-        hs = keep.tile([P, PACK, WIN], F32, name="hs", align_bytes=64)
-        hh = [keep.tile([P, WIN], F32, name=f"hh{c}", align_bytes=64) for c in range(2)]
+        hs = keep.tile([P, PACK, T], F32, name="hs", tag="hs", align_bytes=64)
+        hh = [keep.tile([P, WIN if k < PACK - 1 else T], F32, name=f"hh{k}", align_bytes=64) for k in range(PACK)]
 
         HALF = H // 2
         MH = HALF // PACK
@@ -47,22 +47,26 @@ def tile_picked_wsagecat_maxrelu_l_kernel(
         poss = (pos1, pos2, pos3)
 
         def load_w1(z, c):
-            raw[z, c] = keep.tile([P, PACK, HALF], F32, name=f"raw{z}{c}", align_bytes=64)
+            raw[z, c] = keep.tile([P, PACK, HALF], F32, name=f"raw{z}{c}", tag=f"raw{z}{c}", align_bytes=64)
             nc.sync.dma_start(out=raw[z, c][:], in_=w1v[z, :, :, c * HALF : (c + 1) * HALF])
 
         xs_v = x_scales.bitcast(I32).rearrange("z (q r) c -> r q z c", r=PACK)
+        load_w1(0, 0)
         for r in range(PACK):
-            nc.scalar.dma_start(out=x_sc[r:P:32, :, :].bitcast(I32), in_=xs_v[r])
-        for z in range(PASSES):
-            load_w1(z, 0)
+            nc.sync.dma_start(out=x_sc[r:P:32, :, :].bitcast(I32), in_=xs_v[r])
+        load_w1(1, 0)
         for z in range(PASSES):
             x_w.append(keep.tile([P, T], U32, name=f"x_w{z}", align_bytes=64))
-            nc.sync.dma_start(out=x_w[z][:].bitcast(I32), in_=x_words[z].rearrange("p c r -> p (c r)").bitcast(I32))
+            src = x_words[z].rearrange("p c r -> p (c r)").bitcast(I32)
+            width = T // (z + 1)
+            for s in range(z + 1):
+                cols = slice(s * width, (s + 1) * width)
+                nc.sync.dma_start(out=x_w[z][:, cols].bitcast(I32), in_=src[:, cols])
         nc.sync.dma_start(lists[0][:], pos1)
-        for z in range(PASSES):
-            load_w1(z, 1)
+        load_w1(0, 1)
         for d in range(1, LISTS):
             nc.sync.dma_start(lists[d][:], poss[d])
+        load_w1(1, 1)
         w_w = []
         for a, (words, scales) in enumerate(((w2_words, w2_scales), (w3_words, w3_scales))):
             sv = scales[0].bitcast(I32).rearrange("(q r) c -> r q c", r=PACK)
@@ -80,10 +84,12 @@ def tile_picked_wsagecat_maxrelu_l_kernel(
                 w1s[z, k] = keep.tile([P, P], U8, name=f"w1s{z}{k}", align_bytes=64)
         wq = {}
 
-        def cast(eng, z, c, u, tag):
-            wq[z, c, u] = keep.tile([P, 2, MH, PACK], BF16, name=f"wq{z}{c}{u}", tag=tag, align_bytes=64)
-            src = raw[z, c][:].rearrange("p j (m t) -> p m j t", t=PACK)[:, :, :, 2 * u : 2 * u + 2]
-            dst = wq[z, c, u][:].rearrange("p t m j -> p m j t")
+        def cast(eng, z, c, t0, t1):
+            tile = keep.tile([P, t1 - t0, MH, PACK], BF16, name=f"wq{z}{c}{t0}", align_bytes=64)
+            for u in range(t0 // 2, t1 // 2):
+                wq[z, c, u] = tile[:, 2 * u - t0 : 2 * u - t0 + 2, :, :]
+            src = raw[z, c][:].rearrange("p j (m t) -> p m j t", t=PACK)[:, :, :, t0:t1]
+            dst = tile[:].rearrange("p t m j -> p m j t")
             if eng == "s":
                 nc.scalar.activation(dst, src, ACT.Copy)
             else:
@@ -94,7 +100,7 @@ def tile_picked_wsagecat_maxrelu_l_kernel(
                 nc.vector.quantize_mx(
                     out=w1c[z, c][:].bitcast(FP8X4),
                     scales=w1s[z, c][:],
-                    in_=wq[z, c, u][:].rearrange("p t m j -> p (t m j)"),
+                    in_=wq[z, c, u].rearrange("p t m j -> p (t m j)"),
                 )
             else:
                 for t in range(2):
@@ -105,12 +111,13 @@ def tile_picked_wsagecat_maxrelu_l_kernel(
                     )
 
         TH = T // 2
-        hb = {(k, 0): psum.tile([P, T], F32, name=f"hb{k}", tag=f"bank{k}") for k in range(1, PACK)}
-        hb[0, 0] = psum.tile([P, TH], F32, name="hb0", tag="bank0")
-        hb[0, 1] = psum.tile([P, TH], F32, name="hb4", tag="bank4")
+        hb = {(k, 0): psum.tile([P, T], F32, name=f"hb{k}", tag=f"bank{k}") for k in range(2, PACK)}
+        for k in range(2):
+            for s in range(2):
+                hb[k, s] = psum.tile([P, TH], F32, name=f"hb{k}{s}", tag=f"bank{k + PACK * s}")
 
         def first(k, z):
-            parts = 2 if k == 0 else 1
+            parts = 2 if k < 2 else 1
             width = T // parts
             for s in range(parts):
                 nc.tensor.matmul_mx(
@@ -119,8 +126,8 @@ def tile_picked_wsagecat_maxrelu_l_kernel(
                     lhsT_scale=w1s[z, k][:],
                     rhs=x_w[z][:, s * width : (s + 1) * width].bitcast(FP8X4),
                     rhs_scale=x_sc[:, z, s * width : (s + 1) * width],
-                    start=(z == 0),
-                    stop=(z == PASSES - 1),
+                    start=(z == (0 if k < 2 else 1)),
+                    stop=(z == (1 if k < 2 else 0)),
                 )
 
         zp = keep.tile([P, NQ, PACK, QW], BF16, name="zp", align_bytes=64)
@@ -128,13 +135,11 @@ def tile_picked_wsagecat_maxrelu_l_kernel(
         HP = P // 2
         lo, hi = slice(0, HP), slice(HP, P)
 
-        def gather(k, d, window, tag):
-            g = keep.tile([P, NQ, QW + 32], BF16, name=f"g{k}{d}", tag=tag, align_bytes=64)
-            nc.vector.tensor_copy(g[:, :, 0:QW], window.indirect(lists[d][:]))
-            return g[:, :, 0:QW]
+        def gather(k, d, dst):
+            nc.vector.tensor_copy(dst, hh[k][:].indirect(lists[d][:]))
 
         def evacuate(c):
-            parts = 2 if c == 0 else 1
+            parts = 2
             width = T // parts
             for s in range(parts):
                 nc.scalar.activation(hh[c][:, s * width : (s + 1) * width], hb[c, s][:], ACT.Relu)
@@ -142,57 +147,61 @@ def tile_picked_wsagecat_maxrelu_l_kernel(
             nc.sync.dma_start(out=hs[own, 0, 0:T], in_=hh[c][lo, 0:T])
             nc.sync.dma_start(out=hs[own, 1, 0:T], in_=hh[c][hi, 0:T])
 
-        cast("s", 0, 0, 1, "wq001")
-        cast("v", 0, 0, 0, "wq000")
-        quant_w1(0, 0, 0)
-        cast("v", 1, 0, 0, "wq100")
-        cast("s", 1, 0, 1, "wq101")
-        quant_w1(1, 0, 0)
+        for z in range(PASSES):
+            cast("v", z, 0, 0, 2)
+            quant_w1(z, 0, 0)
+            cast("s", z, 0, 2, PACK)
         first(0, 0)
         first(0, 1)
         evacuate(0)
-        quant_w1(0, 0, 1)
-        quant_w1(1, 0, 1)
+        for z in range(PASSES):
+            quant_w1(z, 0, 1)
 
-        m = [keep.tile([P, NQ, QW], BF16, name=f"m{k}", align_bytes=64) for k in range(PACK - 1)]
-        cast("s", 0, 1, 0, "wait0")
-        cast("s", 1, 1, 0, "wait1")
-        g0 = gather(0, 0, hh[0][:], "g00")
+        early = keep.tile([P, 2, T], BF16, name="early", align_bytes=64)
+        gather(0, 0, early[:, 0, :])
+        gather(0, 1, early[:, 1, :])
+        cast("s", 0, 1, 0, 2)
         quant_w1(0, 1, 0)
         first(1, 0)
-        g1 = gather(0, 1, hh[0][:], "wait0")
+        cast("s", 0, 1, 2, PACK)
+        quant_w1(0, 1, 1)
+        cast("s", 1, 1, 0, PACK)
         quant_w1(1, 1, 0)
         first(1, 1)
-        cast("s", 0, 1, 1, "wait2")
         evacuate(1)
-        cast("s", 1, 1, 1, "wait3")
-        g2 = gather(0, 2, hh[0][:], "wait1")
-        nc.vector.tensor_tensor(m[0][:], g0, g1, ALU.max)
-        quant_w1(0, 1, 1)
-        first(2, 0)
-        first(3, 0)
-        g0 = gather(1, 0, hh[1][:], "wait2")
-        nc.vector.tensor_tensor(zp[:, :, 0, :], m[0][:], g2, ALU.max)
-        nc.sync.dma_start(out=zp[lo, :, 1, :], in_=zp[hi, :, 0, :])
         quant_w1(1, 1, 1)
         for k in range(2, PACK):
             first(k, 1)
-            nc.scalar.activation(hs[:, k, 0:T], hb[k, 0][:], ACT.Relu)
-        g1 = gather(1, 1, hh[1][:], "wait3")
-        g2 = gather(1, 2, hh[1][:], "g12")
-        nc.vector.tensor_tensor(m[1][:], g0, g1, ALU.max)
-        g0 = gather(2, 0, hs[:, 2, :], "g20")
-        nc.vector.tensor_tensor(zt[:], m[1][:], g2, ALU.max)
-        nc.sync.dma_start(out=zp[hi, :, 0, :], in_=zt[lo, :, :])
-        nc.sync.dma_start(out=zp[hi, :, 1, :], in_=zt[hi, :, :])
-        g1 = gather(2, 1, hs[:, 2, :], "g21")
-        g2 = gather(2, 2, hs[:, 2, :], "g22")
-        nc.vector.tensor_tensor(m[2][:], g0, g1, ALU.max)
-        pending = [(zp[:, :, 2, :], m[2][:], g2)]
+            first(k, 0)
+            nc.scalar.activation(hh[k][:, 0:T], hb[k, 0][:], ACT.Relu)
+        for k in range(2, PACK):
+            nc.scalar.activation(hs[:, k, :], hb[k, 0][:], ACT.Relu)
+        late = keep.tile([P, 2, T], BF16, name="late", tag="raw11", align_bytes=64)
+        gather(0, 2, late[:, 0, :])
+        quarters = lambda ap: ap.rearrange("p (q v) -> p q v", q=NQ)
+
+        def largest2(dst, a, b, c, m):
+            for s in range(2):
+                qs = slice(2 * s, 2 * s + 2)
+                nc.vector.tensor_tensor(quarters(m)[:, qs, :], quarters(a)[:, qs, :], quarters(b)[:, qs, :], ALU.max)
+            for s in range(2):
+                qs = slice(2 * s, 2 * s + 2)
+                nc.vector.tensor_tensor(dst[:, qs, :], quarters(m)[:, qs, :], quarters(c)[:, qs, :], ALU.max)
+
+        largest2(zp[:, :, 0, :], early[:, 0, :], early[:, 1, :], late[:, 0, :], late[:, 1, :])
+        nc.sync.dma_start(out=zp[lo, :, 1, :], in_=zp[hi, :, 0, :])
+        for k in range(1, PACK - 1):
+            work = keep.tile([P, 4, T], BF16, name=f"work{k}", align_bytes=64)
+            for d in range(LISTS):
+                gather(k, d, work[:, d, :])
+            largest2(zt[:] if k == 1 else zp[:, :, k, :], work[:, 0, :], work[:, 1, :], work[:, 2, :], work[:, 3, :])
+            if k == 1:
+                nc.sync.dma_start(out=zp[hi, :, 0, :], in_=zt[lo, :, :])
+                nc.sync.dma_start(out=zp[hi, :, 1, :], in_=zt[hi, :, :])
 
         h4 = keep.tile([P, T, PACK], BF16, name="h4", align_bytes=64)
         nc.scalar.copy(
-            h4[:].rearrange("p (c i) t -> p c t i", i=4), hs[:, :, 0:T].rearrange("p t (c i) -> p c t i", i=4)
+            h4[:].rearrange("p (c i) t -> p c t i", i=4), hs[:].rearrange("p t (c i) -> p c t i", i=4)
         )
         hc = keep.tile([P, T], U32, name="hc", align_bytes=64)
         hsc = keep.tile([P, T], U8, name="hsc", align_bytes=64)
@@ -232,7 +241,7 @@ def tile_picked_wsagecat_maxrelu_l_kernel(
             nc.sync.dma_start(out=outv[:, :, q * QW : (q + 1) * QW], in_=res[:])
 
         def interleave(q):
-            z4[q] = keep.tile([P, QW, PACK], BF16, name=f"z4_{q}", tag=f"hold{q}", align_bytes=64)
+            z4[q] = keep.tile([P, QW, PACK], BF16, name=f"z4_{q}", align_bytes=64)
             dst = z4[q][:].rearrange("p (c i) t -> p c t i", i=4)
             src = zp[:, q, :, :].rearrange("p t (c i) -> p c t i", i=4)
             if q < NQ - 1:
@@ -241,31 +250,39 @@ def tile_picked_wsagecat_maxrelu_l_kernel(
                 nc.vector.tensor_copy(dst, src)
 
         t = PACK - 1
-        for q in range(NQ):
-            g = []
+        nc.vector.quantize_mx(out=hc[:].bitcast(FP8X4), scales=hsc[:], in_=h4[:].rearrange("p v t -> p (v t)"))
+        for qq in range(NQ):
+            for b in range(2):
+                ob[qq, b] = psum.tile([P, QW], F32, name=f"ob{qq}{b}", tag=f"bank{2 * qq + b}")
+                second(ob[qq, b][:], b, qq, 0)
+        free = keep.tile([P, QW], BF16, name="free", align_bytes=64)
+        afterh = keep.tile([P, 6, QW], BF16, name="afterh", tag="hs", align_bytes=64)
+        mq = keep.tile([P, NQ, QW], BF16, name="mq", align_bytes=64)
+
+        def slot(q, d):
+            n = LISTS * q + d
+            if n == 0:
+                return free[:]
+            if n < 7:
+                return afterh[:, n - 1, :]
+            return zp[:, (n - 7) // LISTS, (n - 7) % LISTS, :]
+
+        def gather_q(q, d):
             cols = slice(q * QW // 16, (q + 1) * QW // 16)
-            for d in range(LISTS):
-                if d == 1 and q >= 2:
-                    finish(q - 2)
-                tag = f"hold{q - 2}" if d == 1 and q >= 2 else f"gq{q}{d}"
-                gt = keep.tile([P, 2, QW // 2 + 32], BF16, name=f"gq{q}{d}", tag=tag, align_bytes=64)
-                g.append(gt[:, :, 0 : QW // 2])
-                nc.vector.tensor_copy(g[d], hs[:, t, 0:T].indirect(lists[d][:, cols]))
-                if d == 0:
-                    nc.vector.tensor_tensor(*pending[0], ALU.max)
-                    pending.clear()
-                    if q > 0:
-                        interleave(q - 1)
-            if q == 0:
-                nc.vector.quantize_mx(out=hc[:].bitcast(FP8X4), scales=hsc[:], in_=h4[:].rearrange("p v t -> p (v t)"))
-                for qq in range(NQ):
-                    for b in range(2):
-                        ob[qq, b] = psum.tile([P, QW], F32, name=f"ob{qq}{b}", tag=f"bank{2 * qq + b}")
-                        second(ob[qq, b][:], b, qq, 0)
-            mq = keep.tile([P, 2, QW // 2], BF16, name=f"mq{q}", align_bytes=64)
-            nc.vector.tensor_tensor(mq[:], g[0], g[1], ALU.max)
-            pending.append((zp[:, q, t, :].rearrange("p (a b) -> p a b", a=2), mq[:], g[2]))
-        nc.vector.tensor_tensor(*pending[0], ALU.max)
+            nc.vector.tensor_copy(slot(q, d), hh[t][:].indirect(lists[d][:, cols]))
+
+        gather_q(0, 0)
+        for q in range(NQ):
+            if q >= 2:
+                finish(q - 2)
+            gather_q(q, 1)
+            gather_q(q, 2)
+            nc.vector.tensor_tensor(mq[:, q, :], slot(q, 0), slot(q, 1), ALU.max)
+            if q + 1 < NQ:
+                gather_q(q + 1, 0)
+            nc.vector.tensor_tensor(zp[:, q, t, :], mq[:, q, :], slot(q, 2), ALU.max)
+            if q + 1 < NQ:
+                interleave(q)
         q = NQ - 1
         interleave(q)
         finish(NQ - 2)

@@ -57,11 +57,7 @@ def tile_picked_wsagecat_maxrelu_l_kernel(
         load_w1(1, 0)
         for z in range(PASSES):
             x_w.append(keep.tile([P, T], U32, name=f"x_w{z}", align_bytes=64))
-            src = x_words[z].rearrange("p c r -> p (c r)").bitcast(I32)
-            width = T // (z + 1)
-            for s in range(z + 1):
-                cols = slice(s * width, (s + 1) * width)
-                nc.sync.dma_start(out=x_w[z][:, cols].bitcast(I32), in_=src[:, cols])
+            nc.sync.dma_start(out=x_w[z][:].bitcast(I32), in_=x_words[z].rearrange("p c r -> p (c r)").bitcast(I32))
         nc.sync.dma_start(lists[0][:], pos1)
         load_w1(0, 1)
         for d in range(1, LISTS):
@@ -85,7 +81,7 @@ def tile_picked_wsagecat_maxrelu_l_kernel(
         wq = {}
 
         def cast(eng, z, c, t0, t1):
-            tile = keep.tile([P, t1 - t0, MH, PACK], BF16, name=f"wq{z}{c}{t0}", align_bytes=64)
+            tile = keep.tile([P, t1 - t0, MH, PACK], BF16, name=f"wq{z}{c}{t0}", tag=f"wq{z}{c}{t0}", align_bytes=64)
             for u in range(t0 // 2, t1 // 2):
                 wq[z, c, u] = tile[:, 2 * u - t0 : 2 * u - t0 + 2, :, :]
             src = raw[z, c][:].rearrange("p j (m t) -> p m j t", t=PACK)[:, :, :, t0:t1]
@@ -165,18 +161,12 @@ def tile_picked_wsagecat_maxrelu_l_kernel(
         first(1, 0)
         cast("s", 0, 1, 2, PACK)
         quant_w1(0, 1, 1)
-        cast("s", 1, 1, 0, PACK)
+        cast("s", 1, 1, 0, 2)
         quant_w1(1, 1, 0)
         first(1, 1)
+        cast("s", 1, 1, 2, PACK)
         evacuate(1)
-        quant_w1(1, 1, 1)
-        for k in range(2, PACK):
-            first(k, 1)
-            first(k, 0)
-            nc.scalar.activation(hh[k][:, 0:T], hb[k, 0][:], ACT.Relu)
-        for k in range(2, PACK):
-            nc.scalar.activation(hs[:, k, :], hb[k, 0][:], ACT.Relu)
-        late = keep.tile([P, 2, T], BF16, name="late", tag="raw11", align_bytes=64)
+        late = keep.tile([P, 2, T], BF16, name="late", tag="wq110", align_bytes=64)
         gather(0, 2, late[:, 0, :])
         quarters = lambda ap: ap.rearrange("p (q v) -> p q v", q=NQ)
 
@@ -190,8 +180,15 @@ def tile_picked_wsagecat_maxrelu_l_kernel(
 
         largest2(zp[:, :, 0, :], early[:, 0, :], early[:, 1, :], late[:, 0, :], late[:, 1, :])
         nc.sync.dma_start(out=zp[lo, :, 1, :], in_=zp[hi, :, 0, :])
+        quant_w1(1, 1, 1)
+        for k in range(2, PACK):
+            first(k, 1)
+            first(k, 0)
+            nc.scalar.activation(hh[k][:, 0:T], hb[k, 0][:], ACT.Relu)
+        for k in range(2, PACK):
+            nc.scalar.activation(hs[:, k, :], hb[k, 0][:], ACT.Relu)
         for k in range(1, PACK - 1):
-            work = keep.tile([P, 4, T], BF16, name=f"work{k}", align_bytes=64)
+            work = keep.tile([P, 4, T], BF16, name=f"work{k}", tag="raw11" if k == 1 else "work2", align_bytes=64)
             for d in range(LISTS):
                 gather(k, d, work[:, d, :])
             largest2(zt[:] if k == 1 else zp[:, :, k, :], work[:, 0, :], work[:, 1, :], work[:, 2, :], work[:, 3, :])
@@ -255,16 +252,16 @@ def tile_picked_wsagecat_maxrelu_l_kernel(
             for b in range(2):
                 ob[qq, b] = psum.tile([P, QW], F32, name=f"ob{qq}{b}", tag=f"bank{2 * qq + b}")
                 second(ob[qq, b][:], b, qq, 0)
-        free = keep.tile([P, QW], BF16, name="free", align_bytes=64)
-        afterh = keep.tile([P, 6, QW], BF16, name="afterh", tag="hs", align_bytes=64)
+        free = keep.tile([P, 4, QW], BF16, name="free", align_bytes=64)
+        afterh = keep.tile([P, 3, QW], BF16, name="afterh", tag="hs", align_bytes=64)
         mq = keep.tile([P, NQ, QW], BF16, name="mq", align_bytes=64)
 
         def slot(q, d):
             n = LISTS * q + d
-            if n == 0:
-                return free[:]
+            if n < 4:
+                return free[:, n, :]
             if n < 7:
-                return afterh[:, n - 1, :]
+                return afterh[:, n - 4, :]
             return zp[:, (n - 7) // LISTS, (n - 7) % LISTS, :]
 
         def gather_q(q, d):

@@ -23,6 +23,8 @@ WIN = 1024
 QW = 128
 NQ = T // QW
 LISTS = 3
+UNHELD = [(0, 0), (0, 1), (0, 2), (1, 0), (1, 2)]
+AFTER_H = [(1, 1), (2, 0), (3, 0)]
 
 
 def tile_picked_wsagecat_maxrelu_l_kernel(
@@ -36,7 +38,6 @@ def tile_picked_wsagecat_maxrelu_l_kernel(
         lists = [keep.tile([P, T // 16], U16, name=f"list{d}") for d in range(LISTS)]
         x_sc = keep.tile([P, PASSES, T], U8, name="x_sc", align_bytes=64)
         w_sc = keep.tile([P, 2, N], U8, name="w_sc", align_bytes=64)
-        hs = keep.tile([P, PACK, T], F32, name="hs", tag="hs", align_bytes=64)
         hh = [keep.tile([P, WIN if k < PACK - 1 else T], F32, name=f"hh{k}", align_bytes=64) for k in range(PACK)]
 
         HALF = H // 2
@@ -56,7 +57,7 @@ def tile_picked_wsagecat_maxrelu_l_kernel(
             nc.sync.dma_start(out=x_sc[r:P:32, :, :].bitcast(I32), in_=xs_v[r])
         load_w1(1, 0)
         for z in range(PASSES):
-            x_w.append(keep.tile([P, T], U32, name=f"x_w{z}", align_bytes=64))
+            x_w.append(keep.tile([P, T], U32, name=f"x_w{z}", tag=f"x_w{z}", align_bytes=64))
             nc.sync.dma_start(out=x_w[z][:].bitcast(I32), in_=x_words[z].rearrange("p c r -> p (c r)").bitcast(I32))
         nc.sync.dma_start(lists[0][:], pos1)
         load_w1(0, 1)
@@ -72,39 +73,40 @@ def tile_picked_wsagecat_maxrelu_l_kernel(
             w_w.append(keep.tile([P, 2 * N], U8, name=f"w_w{a}", align_bytes=64))
             nc.sync.dma_start(out=w_w[a][:].bitcast(I32), in_=words[0].bitcast(I32))
 
-        w1c = {}
-        w1s = {}
+        lowq = {}
+        lowc = {}
+        lows = {}
         for z in range(PASSES):
-            for k in range(PACK):
-                w1c[z, k] = keep.tile([P, P], U32, name=f"w1c{z}{k}", align_bytes=64)
-                w1s[z, k] = keep.tile([P, P], U8, name=f"w1s{z}{k}", align_bytes=64)
-        wq = {}
+            for c in range(2):
+                lowq[z, c] = keep.tile([P, 2, MH, PACK], BF16, name=f"lowq{z}{c}", tag=f"lowq{z}{c}", align_bytes=64)
+                lowc[z, c] = keep.tile([P, P], U32, name=f"lowc{z}{c}", align_bytes=64)
+                lows[z, c] = keep.tile([P, P], U8, name=f"lows{z}{c}", align_bytes=64)
+        highq = keep.tile([P, PASSES, 2, 2, MH, PACK], BF16, name="highq", align_bytes=64)
+        highc = keep.tile([P, PASSES, 2, P], U32, name="highc", tag="highc", align_bytes=64)
+        highs = keep.tile([P, PASSES, 2, P], U8, name="highs", align_bytes=64)
 
-        def cast(eng, z, c, t0, t1):
-            tile = keep.tile([P, t1 - t0, MH, PACK], BF16, name=f"wq{z}{c}{t0}", tag=f"wq{z}{c}{t0}", align_bytes=64)
-            for u in range(t0 // 2, t1 // 2):
-                wq[z, c, u] = tile[:, 2 * u - t0 : 2 * u - t0 + 2, :, :]
-            src = raw[z, c][:].rearrange("p j (m t) -> p m j t", t=PACK)[:, :, :, t0:t1]
-            dst = tile[:].rearrange("p t m j -> p m j t")
-            if eng == "s":
+        def cast(z, c, u):
+            src = raw[z, c][:].rearrange("p j (m t) -> p m j t", t=PACK)[:, :, :, 2 * u : 2 * u + 2]
+            dst = (lowq[z, c][:] if u == 0 else highq[:, z, :, c, :, :]).rearrange("p t m j -> p m j t")
+            if c == 1 or u == 1:
                 nc.scalar.activation(dst, src, ACT.Copy)
             else:
                 nc.vector.tensor_copy(dst, src)
 
-        def quant_w1(z, c, u):
-            if u == 0:
+        def quant_low(z, c):
+            nc.vector.quantize_mx(
+                out=lowc[z, c][:].bitcast(FP8X4),
+                scales=lows[z, c][:],
+                in_=lowq[z, c][:].rearrange("p t m j -> p (t m j)"),
+            )
+
+        def quant_high(z, c):
+            for t in range(2):
                 nc.vector.quantize_mx(
-                    out=w1c[z, c][:].bitcast(FP8X4),
-                    scales=w1s[z, c][:],
-                    in_=wq[z, c, u].rearrange("p t m j -> p (t m j)"),
+                    out=highc[:, z, t, c * MH : (c + 1) * MH].bitcast(FP8X4),
+                    scales=highs[:, z, t, c * MH : (c + 1) * MH],
+                    in_=highq[:, z, t, c, :, :].rearrange("p m j -> p (m j)"),
                 )
-            else:
-                for t in range(2):
-                    nc.vector.quantize_mx(
-                        out=w1c[z, 2 + t][:, c * MH : (c + 1) * MH].bitcast(FP8X4),
-                        scales=w1s[z, 2 + t][:, c * MH : (c + 1) * MH],
-                        in_=wq[z, c, u][:, t, :, :].rearrange("p m j -> p (m j)"),
-                    )
 
         TH = T // 2
         hb = {(k, 0): psum.tile([P, T], F32, name=f"hb{k}", tag=f"bank{k}") for k in range(2, PACK)}
@@ -115,62 +117,39 @@ def tile_picked_wsagecat_maxrelu_l_kernel(
         def first(k, z):
             parts = 2 if k < 2 else 1
             width = T // parts
+            codes = lowc[z, k][:] if k < 2 else highc[:, z, k - 2, :]
+            scales = lows[z, k][:] if k < 2 else highs[:, z, k - 2, :]
             for s in range(parts):
                 nc.tensor.matmul_mx(
                     out=hb[k, s][:],
-                    lhsT=w1c[z, k][:].bitcast(FP8X4),
-                    lhsT_scale=w1s[z, k][:],
+                    lhsT=codes.bitcast(FP8X4),
+                    lhsT_scale=scales,
                     rhs=x_w[z][:, s * width : (s + 1) * width].bitcast(FP8X4),
                     rhs_scale=x_sc[:, z, s * width : (s + 1) * width],
                     start=(z == (0 if k < 2 else 1)),
                     stop=(z == (1 if k < 2 else 0)),
                 )
 
-        zp = keep.tile([P, NQ, PACK, QW], BF16, name="zp", align_bytes=64)
-        zt = keep.tile([P, NQ, QW], BF16, name="zt", align_bytes=64)
+        zp = keep.tile([P, NQ, PACK, QW], BF16, name="zp", tag="zp", align_bytes=64)
         HP = P // 2
         lo, hi = slice(0, HP), slice(HP, P)
 
-        def gather(k, d, dst):
-            nc.vector.tensor_copy(dst, hh[k][:].indirect(lists[d][:]))
-
-        def evacuate(c):
-            parts = 2
-            width = T // parts
-            for s in range(parts):
-                nc.scalar.activation(hh[c][:, s * width : (s + 1) * width], hb[c, s][:], ACT.Relu)
-            own = (lo, hi)[c]
-            nc.sync.dma_start(out=hs[own, 0, 0:T], in_=hh[c][lo, 0:T])
-            nc.sync.dma_start(out=hs[own, 1, 0:T], in_=hh[c][hi, 0:T])
+        def gather(k, d, dst, c0=0, c1=T):
+            nc.vector.tensor_copy(dst, hh[k][:].indirect(lists[d][:, c0 // 16 : c1 // 16]))
 
         for z in range(PASSES):
-            cast("v", z, 0, 0, 2)
-            quant_w1(z, 0, 0)
-            cast("s", z, 0, 2, PACK)
-        first(0, 0)
-        first(0, 1)
-        evacuate(0)
+            cast(z, 0, 0)
+            quant_low(z, 0)
+            cast(z, 0, 1)
+            first(0, z)
+        for s in range(2):
+            nc.scalar.activation(hh[0][:, s * TH : (s + 1) * TH], hb[0, s][:], ACT.Relu)
         for z in range(PASSES):
-            quant_w1(z, 0, 1)
+            quant_high(z, 0)
 
-        early = keep.tile([P, 2, T], BF16, name="early", align_bytes=64)
-        gather(0, 0, early[:, 0, :])
-        gather(0, 1, early[:, 1, :])
-        cast("s", 0, 1, 0, 2)
-        quant_w1(0, 1, 0)
-        first(1, 0)
-        cast("s", 0, 1, 2, PACK)
-        quant_w1(0, 1, 1)
-        cast("s", 1, 1, 0, 2)
-        quant_w1(1, 1, 0)
-        first(1, 1)
-        cast("s", 1, 1, 2, PACK)
-        evacuate(1)
-        late = keep.tile([P, 2, T], BF16, name="late", tag="wq110", align_bytes=64)
-        gather(0, 2, late[:, 0, :])
         quarters = lambda ap: ap.rearrange("p (q v) -> p q v", q=NQ)
 
-        def largest2(dst, a, b, c, m):
+        def largest(dst, a, b, c, m):
             for s in range(2):
                 qs = slice(2 * s, 2 * s + 2)
                 nc.vector.tensor_tensor(quarters(m)[:, qs, :], quarters(a)[:, qs, :], quarters(b)[:, qs, :], ALU.max)
@@ -178,118 +157,186 @@ def tile_picked_wsagecat_maxrelu_l_kernel(
                 qs = slice(2 * s, 2 * s + 2)
                 nc.vector.tensor_tensor(dst[:, qs, :], quarters(m)[:, qs, :], quarters(c)[:, qs, :], ALU.max)
 
-        largest2(zp[:, :, 0, :], early[:, 0, :], early[:, 1, :], late[:, 0, :], late[:, 1, :])
+        early = keep.tile([P, 2, T], BF16, name="early", align_bytes=64)
+        gather(0, 0, early[:, 0, :])
+        cast(0, 1, 0)
+        quant_low(0, 1)
+        first(1, 0)
+        cast(0, 1, 1)
+        quant_high(0, 1)
+        gather(0, 1, early[:, 1, :])
+        cast(1, 1, 0)
+        quant_low(1, 1)
+        first(1, 1)
+        cast(1, 1, 1)
+        for s in range(2):
+            nc.scalar.activation(hh[1][:, s * TH : (s + 1) * TH], hb[1, s][:], ACT.Relu)
+        late = keep.tile([P, 2, T], BF16, name="late", tag="lowq11", align_bytes=64)
+        gather(0, 2, late[:, 0, :])
+        largest(zp[:, :, 0, :], early[:, 0, :], early[:, 1, :], late[:, 0, :], late[:, 1, :])
         nc.sync.dma_start(out=zp[lo, :, 1, :], in_=zp[hi, :, 0, :])
-        quant_w1(1, 1, 1)
+        quant_high(1, 1)
+        hs = keep.tile([P, PACK, T], F32, name="hs", tag="raw11", align_bytes=64)
+        for c in range(2):
+            own = (lo, hi)[c]
+            nc.sync.dma_start(out=hs[own, 0, :], in_=hh[c][lo, 0:T])
+            nc.sync.dma_start(out=hs[own, 1, :], in_=hh[c][hi, 0:T])
         for k in range(2, PACK):
-            first(k, 1)
-            first(k, 0)
+            for z in reversed(range(PASSES)):
+                first(k, z)
             nc.scalar.activation(hh[k][:, 0:T], hb[k, 0][:], ACT.Relu)
         for k in range(2, PACK):
             nc.scalar.activation(hs[:, k, :], hb[k, 0][:], ACT.Relu)
-        for k in range(1, PACK - 1):
-            work = keep.tile([P, 4, T], BF16, name=f"work{k}", tag="raw11" if k == 1 else "work2", align_bytes=64)
-            for d in range(LISTS):
-                gather(k, d, work[:, d, :])
-            largest2(zt[:] if k == 1 else zp[:, :, k, :], work[:, 0, :], work[:, 1, :], work[:, 2, :], work[:, 3, :])
-            if k == 1:
-                nc.sync.dma_start(out=zp[hi, :, 0, :], in_=zt[lo, :, :])
-                nc.sync.dma_start(out=zp[hi, :, 1, :], in_=zt[hi, :, :])
+
+        zt = keep.tile([P, NQ, QW], BF16, name="zt", tag="x_w0", align_bytes=64)
+        work1 = keep.tile([P, 4, T], BF16, name="work1", align_bytes=64)
+        for d in range(LISTS):
+            gather(1, d, work1[:, d, :])
+        largest(zt[:], work1[:, 0, :], work1[:, 1, :], work1[:, 2, :], work1[:, 3, :])
+        nc.sync.dma_start(out=zp[hi, :, 1, :], in_=zt[hi, :, :])
+        nc.sync.dma_start(out=zp[hi, :, 0, :], in_=zt[lo, :, :])
+
+        work = keep.tile([P, 2, T], BF16, name="work", align_bytes=64)
+        held = keep.tile([P, 2, T], BF16, name="held", tag="highc", align_bytes=64)
+        for d in range(LISTS):
+            gather(2, d, work[:, d, :] if d < 2 else held[:, 0, :])
 
         h4 = keep.tile([P, T, PACK], BF16, name="h4", align_bytes=64)
         nc.scalar.copy(
             h4[:].rearrange("p (c i) t -> p c t i", i=4), hs[:].rearrange("p t (c i) -> p c t i", i=4)
         )
-        hc = keep.tile([P, T], U32, name="hc", align_bytes=64)
+        hc = {}
         hsc = keep.tile([P, T], U8, name="hsc", align_bytes=64)
 
         outv = out.rearrange("(b p) v -> p b v", p=P)
-        zc = keep.tile([P, T], U32, name="zc", align_bytes=64)
+        zc = keep.tile([P, T - QW], U32, name="zc", align_bytes=64)
         zsc = keep.tile([P, T], U8, name="zsc", align_bytes=64)
         z4 = {}
+        last = NQ - 1
+
+        last_codes = []
+
+        def z_codes(q):
+            if q < last:
+                return zc[:, q * QW : (q + 1) * QW]
+            return last_codes[0][:]
 
         def second(dst, b, q, a):
-            codes, scales = ((hc, hsc), (zc, zsc))[a]
+            cols = slice(q * QW, (q + 1) * QW)
+            codes = z_codes(q) if a == 1 else hc[q // 2][:, (q % 2) * QW : (q % 2 + 1) * QW]
+            scales = (hsc, zsc)[a][:, cols]
+            shared = q < last
             nc.tensor.matmul_mx(
                 out=dst,
                 lhsT=w_w[a][:, 2 * P * b : 2 * P * (b + 1)].bitcast(FP4X4),
                 lhsT_scale=w_sc[:, a, P * b : P * (b + 1)],
-                rhs=codes[:, q * QW : (q + 1) * QW].bitcast(FP8X4),
-                rhs_scale=scales[:, q * QW : (q + 1) * QW],
-                start=(a == 0),
-                stop=(a == 1),
+                rhs=codes.bitcast(FP8X4),
+                rhs_scale=scales,
+                start=(a == 0 and (b == 0 or not shared)),
+                stop=(a == 1 and (b == 1 or not shared)),
             )
 
         def quant_z(q):
+            if q == last:
+                last_codes.append(keep.tile([P, QW], U32, name="zc_last", tag="zp", align_bytes=64))
             nc.vector.quantize_mx(
-                out=zc[:, q * QW : (q + 1) * QW].bitcast(FP8X4),
+                out=z_codes(q).bitcast(FP8X4),
                 scales=zsc[:, q * QW : (q + 1) * QW],
                 in_=z4[q][:].rearrange("p v t -> p (v t)"),
             )
 
-        ob = {}
+        pair = {q: psum.tile([P, 2, QW], F32, name=f"pair{q}", tag=f"bank{(0, 1, 4)[q]}") for q in range(last)}
+        lone = [psum.tile([P, QW], F32, name=f"lone{b}", tag=f"bank{6 + b}") for b in range(2)]
+
+        def sums(q, b):
+            return pair[q][:, b, :] if q < last else lone[b][:]
 
         def finish(q):
             quant_z(q)
-            res = keep.tile([P, 2, QW], F32, name=f"res{q}")
             for b in range(2):
-                second(ob[q, b][:], b, q, 1)
-                nc.scalar.activation(res[:, b, :], ob[q, b][:], ACT.Relu)
-            nc.sync.dma_start(out=outv[:, :, q * QW : (q + 1) * QW], in_=res[:])
+                second(sums(q, b), b, q, 1)
+            if q < last:
+                res = keep.tile([P, 2, QW], F32, name=f"res{q}")
+                nc.scalar.activation(res[:], pair[q][:], ACT.Relu)
+                nc.sync.dma_start(out=outv[:, :, q * QW : (q + 1) * QW], in_=res[:])
+            else:
+                for b in range(2):
+                    res = keep.tile([P, QW], F32, name=f"res{q}{b}")
+                    nc.vector.tensor_scalar_max(res[:], lone[b][:], 0.0)
+                    (nc.sync, nc.scalar)[b].dma_start(out=outv[:, b, q * QW : (q + 1) * QW], in_=res[:])
 
         def interleave(q):
-            z4[q] = keep.tile([P, QW, PACK], BF16, name=f"z4_{q}", align_bytes=64)
+            z4[q] = keep.tile([P, QW, PACK], BF16, name=f"z4_{q}", tag=f"z4_{q}", align_bytes=64)
             dst = z4[q][:].rearrange("p (c i) t -> p c t i", i=4)
             src = zp[:, q, :, :].rearrange("p t (c i) -> p c t i", i=4)
-            if q < NQ - 1:
+            if q < last:
                 nc.scalar.copy(dst, src)
             else:
                 nc.vector.tensor_copy(dst, src)
 
         t = PACK - 1
-        nc.vector.quantize_mx(out=hc[:].bitcast(FP8X4), scales=hsc[:], in_=h4[:].rearrange("p v t -> p (v t)"))
-        for qq in range(NQ):
-            for b in range(2):
-                ob[qq, b] = psum.tile([P, QW], F32, name=f"ob{qq}{b}", tag=f"bank{2 * qq + b}")
-                second(ob[qq, b][:], b, qq, 0)
-        free = keep.tile([P, 4, QW], BF16, name="free", align_bytes=64)
-        afterh = keep.tile([P, 3, QW], BF16, name="afterh", tag="hs", align_bytes=64)
+        free = keep.tile([P, len(UNHELD), QW], BF16, name="free", align_bytes=64)
+        afterh = keep.tile([P, 3, QW], BF16, name="afterh", tag="raw11", align_bytes=64)
         mq = keep.tile([P, NQ, QW], BF16, name="mq", align_bytes=64)
 
         def slot(q, d):
-            n = LISTS * q + d
-            if n < 4:
-                return free[:, n, :]
-            if n < 7:
-                return afterh[:, n - 4, :]
-            return zp[:, (n - 7) // LISTS, (n - 7) % LISTS, :]
+            if (q, d) in UNHELD:
+                return free[:, UNHELD.index((q, d)), :]
+            if (q, d) in AFTER_H:
+                return afterh[:, AFTER_H.index((q, d)), :]
+            if d == 1:
+                return zp[:, 0, q - 2, :]
+            if q == 2:
+                return z4[0][:].rearrange("p v t -> p (v t)")[:, 0:QW]
+            return slot(2, 0)
 
         def gather_q(q, d):
-            cols = slice(q * QW // 16, (q + 1) * QW // 16)
-            nc.vector.tensor_copy(slot(q, d), hh[t][:].indirect(lists[d][:, cols]))
+            gather(t, d, slot(q, d), q * QW, (q + 1) * QW)
+
+        def quant_h(s):
+            hc[s] = keep.tile([P, TH], U32, name=f"hc{s}", tag=("hc0", "z4_0")[s], align_bytes=64)
+            nc.vector.quantize_mx(
+                out=hc[s][:].bitcast(FP8X4),
+                scales=hsc[:, s * TH : (s + 1) * TH],
+                in_=h4[:, s * TH : (s + 1) * TH, :].rearrange("p v t -> p (v t)"),
+            )
+            for q in (2 * s, 2 * s + 1):
+                for b in range(2):
+                    second(sums(q, b), b, q, 0)
+
+        def first_max(q):
+            nc.vector.tensor_tensor(mq[:, q, :], slot(q, 0), slot(q, 1), ALU.max)
+
+        def second_max(q):
+            nc.vector.tensor_tensor(zp[:, q, t, :], mq[:, q, :], slot(q, 2), ALU.max)
+            if q == last:
+                quant_h(1)
+            interleave(q)
 
         gather_q(0, 0)
-        for q in range(NQ):
-            if q >= 2:
-                finish(q - 2)
-            gather_q(q, 1)
-            gather_q(q, 2)
-            nc.vector.tensor_tensor(mq[:, q, :], slot(q, 0), slot(q, 1), ALU.max)
-            if q + 1 < NQ:
-                gather_q(q + 1, 0)
-            nc.vector.tensor_tensor(zp[:, q, t, :], mq[:, q, :], slot(q, 2), ALU.max)
-            if q + 1 < NQ:
-                interleave(q)
-        q = NQ - 1
-        interleave(q)
-        finish(NQ - 2)
-        quant_z(q)
-        for b in range(2):
-            second(ob[q, b][:], b, q, 1)
-            res = keep.tile([P, QW], F32, name=f"resl{b}")
-            if b == 0:
-                nc.scalar.activation(res[:], ob[q, b][:], ACT.Relu)
-                nc.scalar.dma_start(out=outv[:, b, q * QW : (q + 1) * QW], in_=res[:])
-            else:
-                nc.vector.tensor_scalar_max(res[:], ob[q, b][:], 0.0)
-                nc.sync.dma_start(out=outv[:, b, q * QW : (q + 1) * QW], in_=res[:])
+        gather_q(0, 1)
+        nc.vector.tensor_tensor(held[:, 1, :], work[:, 0, :], work[:, 1, :], ALU.max)
+        gather_q(0, 2)
+        gather_q(1, 0)
+        first_max(0)
+        nc.vector.tensor_tensor(zp[:, :, 2, :], quarters(held[:, 1, :]), quarters(held[:, 0, :]), ALU.max)
+        gather_q(1, 2)
+        second_max(0)
+        gather_q(1, 1)
+        quant_h(0)
+        first_max(1)
+        gather_q(2, 0)
+        gather_q(3, 0)
+        second_max(1)
+        gather_q(2, 1)
+        finish(0)
+        gather_q(3, 1)
+        first_max(2)
+        gather_q(2, 2)
+        first_max(3)
+        gather_q(3, 2)
+        second_max(2)
+        finish(1)
+        second_max(3)
+        finish(2)
+        finish(3)

@@ -23,8 +23,6 @@ WIN = 1024
 QW = 128
 NQ = T // QW
 LISTS = 3
-UNHELD = [(0, 0), (0, 1), (0, 2), (1, 0), (1, 2)]
-AFTER_H = [(1, 1), (2, 0), (3, 0)]
 
 
 def tile_picked_wsagecat_maxrelu_l_kernel(
@@ -149,13 +147,8 @@ def tile_picked_wsagecat_maxrelu_l_kernel(
 
         quarters = lambda ap: ap.rearrange("p (q v) -> p q v", q=NQ)
 
-        def largest(dst, a, b, c, m):
-            for s in range(2):
-                qs = slice(2 * s, 2 * s + 2)
-                nc.vector.tensor_tensor(quarters(m)[:, qs, :], quarters(a)[:, qs, :], quarters(b)[:, qs, :], ALU.max)
-            for s in range(2):
-                qs = slice(2 * s, 2 * s + 2)
-                nc.vector.tensor_tensor(dst[:, qs, :], quarters(m)[:, qs, :], quarters(c)[:, qs, :], ALU.max)
+        def largest(dst, a, b):
+            nc.vector.tensor_tensor(dst, a, b, ALU.max)
 
         early = keep.tile([P, 2, T], BF16, name="early", align_bytes=64)
         gather(0, 0, early[:, 0, :])
@@ -173,9 +166,10 @@ def tile_picked_wsagecat_maxrelu_l_kernel(
             nc.scalar.activation(hh[1][:, s * TH : (s + 1) * TH], hb[1, s][:], ACT.Relu)
         late = keep.tile([P, 2, T], BF16, name="late", tag="lowq11", align_bytes=64)
         gather(0, 2, late[:, 0, :])
-        largest(zp[:, :, 0, :], early[:, 0, :], early[:, 1, :], late[:, 0, :], late[:, 1, :])
-        nc.sync.dma_start(out=zp[lo, :, 1, :], in_=zp[hi, :, 0, :])
+        largest(late[:, 1, :], early[:, 0, :], early[:, 1, :])
         quant_high(1, 1)
+        largest(zp[:, :, 0, :], quarters(late[:, 1, :]), quarters(late[:, 0, :]))
+        nc.sync.dma_start(out=zp[lo, :, 1, :], in_=zp[hi, :, 0, :])
         hs = keep.tile([P, PACK, T], F32, name="hs", tag="raw11", align_bytes=64)
         for c in range(2):
             own = (lo, hi)[c]
@@ -192,14 +186,16 @@ def tile_picked_wsagecat_maxrelu_l_kernel(
         work1 = keep.tile([P, 4, T], BF16, name="work1", align_bytes=64)
         for d in range(LISTS):
             gather(1, d, work1[:, d, :])
-        largest(zt[:], work1[:, 0, :], work1[:, 1, :], work1[:, 2, :], work1[:, 3, :])
-        nc.sync.dma_start(out=zp[hi, :, 1, :], in_=zt[hi, :, :])
-        nc.sync.dma_start(out=zp[hi, :, 0, :], in_=zt[lo, :, :])
+        largest(work1[:, 3, :], work1[:, 0, :], work1[:, 1, :])
 
         work = keep.tile([P, 2, T], BF16, name="work", align_bytes=64)
         held = keep.tile([P, 2, T], BF16, name="held", tag="highc", align_bytes=64)
-        for d in range(LISTS):
-            gather(2, d, work[:, d, :] if d < 2 else held[:, 0, :])
+        gather(2, 0, work[:, 0, :])
+        largest(zt[:], quarters(work1[:, 3, :]), quarters(work1[:, 2, :]))
+        nc.sync.dma_start(out=zp[hi, :, 1, :], in_=zt[hi, :, :])
+        nc.sync.dma_start(out=zp[hi, :, 0, :], in_=zt[lo, :, :])
+        gather(2, 1, work[:, 1, :])
+        gather(2, 2, held[:, 0, :])
 
         h4 = keep.tile([P, T, PACK], BF16, name="h4", align_bytes=64)
         nc.scalar.copy(
@@ -275,26 +271,16 @@ def tile_picked_wsagecat_maxrelu_l_kernel(
                 nc.vector.tensor_copy(dst, src)
 
         t = PACK - 1
-        free = keep.tile([P, len(UNHELD), QW], BF16, name="free", align_bytes=64)
+        free = keep.tile([P, 5, QW], BF16, name="free", align_bytes=64)
         afterh = keep.tile([P, 3, QW], BF16, name="afterh", tag="raw11", align_bytes=64)
         mq = keep.tile([P, NQ, QW], BF16, name="mq", align_bytes=64)
+        flat = lambda ap: ap.rearrange("p a v -> p (a v)")
 
-        def slot(q, d):
-            if (q, d) in UNHELD:
-                return free[:, UNHELD.index((q, d)), :]
-            if (q, d) in AFTER_H:
-                return afterh[:, AFTER_H.index((q, d)), :]
-            if d == 1:
-                return zp[:, 0, q - 2, :]
-            if q == 2:
-                return z4[0][:].rearrange("p v t -> p (v t)")[:, 0:QW]
-            return slot(2, 0)
-
-        def gather_q(q, d):
-            gather(t, d, slot(q, d), q * QW, (q + 1) * QW)
+        def gather_q(d, q0, q1, dst):
+            gather(t, d, dst, q0 * QW, q1 * QW)
 
         def quant_h(s):
-            hc[s] = keep.tile([P, TH], U32, name=f"hc{s}", tag=("hc0", "z4_0")[s], align_bytes=64)
+            hc[s] = keep.tile([P, TH], U32, name=f"hc{s}", tag=("hc0", "raw11")[s], align_bytes=64)
             nc.vector.quantize_mx(
                 out=hc[s][:].bitcast(FP8X4),
                 scales=hsc[:, s * TH : (s + 1) * TH],
@@ -304,39 +290,31 @@ def tile_picked_wsagecat_maxrelu_l_kernel(
                 for b in range(2):
                     second(sums(q, b), b, q, 0)
 
-        def first_max(q):
-            nc.vector.tensor_tensor(mq[:, q, :], slot(q, 0), slot(q, 1), ALU.max)
-
-        def second_max(q):
-            nc.vector.tensor_tensor(zp[:, q, t, :], mq[:, q, :], slot(q, 2), ALU.max)
-            if q == last:
-                quant_h(1)
-            interleave(q)
-
-        gather_q(0, 0)
-        gather_q(0, 1)
-        nc.vector.tensor_tensor(held[:, 1, :], work[:, 0, :], work[:, 1, :], ALU.max)
-        gather_q(0, 2)
-        gather_q(1, 0)
-        first_max(0)
-        nc.vector.tensor_tensor(zp[:, :, 2, :], quarters(held[:, 1, :]), quarters(held[:, 0, :]), ALU.max)
-        gather_q(1, 2)
-        second_max(0)
-        gather_q(1, 1)
+        gather_q(0, 0, 2, flat(free[:, 0:2, :]))
+        gather_q(1, 0, 1, free[:, 4, :])
+        largest(held[:, 1, :], work[:, 0, :], work[:, 1, :])
+        gather_q(2, 0, 2, flat(free[:, 2:4, :]))
+        largest(mq[:, 0, :], free[:, 0, :], free[:, 4, :])
+        largest(zp[:, :, 2, :], quarters(held[:, 1, :]), quarters(held[:, 0, :]))
+        largest(zp[:, 0, t, :], mq[:, 0, :], free[:, 2, :])
+        interleave(0)
+        gather_q(1, 1, 2, afterh[:, 2, :])
         quant_h(0)
-        first_max(1)
-        gather_q(2, 0)
-        gather_q(3, 0)
-        second_max(1)
-        gather_q(2, 1)
+        largest(mq[:, 1, :], free[:, 1, :], afterh[:, 2, :])
+        gather_q(0, 2, 4, flat(afterh[:, 0:2, :]))
+        largest(zp[:, 1, t, :], mq[:, 1, :], free[:, 3, :])
+        interleave(1)
+        gather_q(1, 2, 4, flat(zp[:, 0, 0:2, :]))
         finish(0)
-        gather_q(3, 1)
-        first_max(2)
-        gather_q(2, 2)
-        first_max(3)
-        gather_q(3, 2)
-        second_max(2)
+        gather_q(2, 2, 3, zp[:, 0, 2, :])
+        largest(mq[:, 2:4, :], afterh[:, 0:2, :], zp[:, 0, 0:2, :])
+        end = z4[0][:].rearrange("p v t -> p (v t)")[:, 0:QW]
+        gather_q(2, 3, 4, end)
+        largest(zp[:, 2, t, :], mq[:, 2, :], zp[:, 0, 2, :])
+        interleave(2)
+        quant_h(1)
+        largest(zp[:, 3, t, :], mq[:, 3, :], end)
         finish(1)
-        second_max(3)
+        interleave(3)
         finish(2)
         finish(3)

@@ -168,8 +168,6 @@ def tile_picked_wsagecat_maxrelu_l_kernel(
         gather(0, 2, late[:, 0, :])
         largest(late[:, 1, :], early[:, 0, :], early[:, 1, :])
         quant_high(1, 1)
-        largest(zp[:, :, 0, :], quarters(late[:, 1, :]), quarters(late[:, 0, :]))
-        nc.sync.dma_start(out=zp[lo, :, 1, :], in_=zp[hi, :, 0, :])
         hs = keep.tile([P, PACK, T], F32, name="hs", tag="raw11", align_bytes=64)
         for c in range(2):
             own = (lo, hi)[c]
@@ -182,22 +180,31 @@ def tile_picked_wsagecat_maxrelu_l_kernel(
         for k in range(2, PACK):
             nc.scalar.activation(hs[:, k, :], hb[k, 0][:], ACT.Relu)
 
-        zt = keep.tile([P, NQ, QW], BF16, name="zt", tag="x_w0", align_bytes=64)
-        work1 = keep.tile([P, 4, T], BF16, name="work1", align_bytes=64)
+        zt = keep.tile([P, NQ, QW], BF16, name="zt", align_bytes=64)
+        got1 = [keep.tile([P, T], BF16, name=f"got1{d}", tag=f"got1{d}", align_bytes=64) for d in range(LISTS)]
+        two1 = keep.tile([P, T], BF16, name="two1", align_bytes=64)
         for d in range(LISTS):
-            gather(1, d, work1[:, d, :])
-        largest(work1[:, 3, :], work1[:, 0, :], work1[:, 1, :])
+            gather(1, d, got1[d][:])
+        sides = ((late[:, 1, :], late[:, 0, :]), (got1[0][:], got1[1][:]))
+        ahead = []
+        for n, (a, b) in enumerate(sides):
+            diff = keep.tile([P, T], F32, name=f"diff{n}", align_bytes=64)
+            nc.gpsimd.tensor_tensor(diff[:], a, b, ALU.subtract)
+            ahead.append(keep.tile([P, T], F32, name=f"ahead{n}", tag=f"ahead{n}", align_bytes=64))
+            nc.scalar.activation(ahead[n][:], diff[:], ACT.Relu)
+        nc.gpsimd.tensor_tensor(zp[:, :, 0, :], quarters(ahead[0][:]), quarters(sides[0][1]), ALU.add)
+        nc.sync.dma_start(out=zp[lo, :, 1, :], in_=zp[hi, :, 0, :])
+        nc.gpsimd.tensor_tensor(two1[:], ahead[1][:], sides[1][1], ALU.add)
 
-        work = keep.tile([P, 2, T], BF16, name="work", align_bytes=64)
-        held = keep.tile([P, 2, T], BF16, name="held", tag="highc", align_bytes=64)
-        gather(2, 0, work[:, 0, :])
-        largest(zt[:], quarters(work1[:, 3, :]), quarters(work1[:, 2, :]))
+        work = keep.tile([P, 3, T], BF16, name="work", align_bytes=64)
+        two2 = keep.tile([P, T], BF16, name="two2", tag="ahead1", align_bytes=64)
+        for d in range(LISTS):
+            gather(2, d, work[:, d, :])
+        largest(zt[:], quarters(two1[:]), quarters(got1[2][:]))
         nc.sync.dma_start(out=zp[hi, :, 1, :], in_=zt[hi, :, :])
         nc.sync.dma_start(out=zp[hi, :, 0, :], in_=zt[lo, :, :])
-        gather(2, 1, work[:, 1, :])
-        gather(2, 2, held[:, 0, :])
 
-        h4 = keep.tile([P, T, PACK], BF16, name="h4", align_bytes=64)
+        h4 = keep.tile([P, T, PACK], BF16, name="h4", tag="got10", align_bytes=64)
         nc.scalar.copy(
             h4[:].rearrange("p (c i) t -> p c t i", i=4), hs[:].rearrange("p t (c i) -> p c t i", i=4)
         )
@@ -271,7 +278,7 @@ def tile_picked_wsagecat_maxrelu_l_kernel(
                 nc.vector.tensor_copy(dst, src)
 
         t = PACK - 1
-        free = keep.tile([P, 5, QW], BF16, name="free", align_bytes=64)
+        free = keep.tile([P, 5, QW], BF16, name="free", tag="got11", align_bytes=64)
         afterh = keep.tile([P, 3, QW], BF16, name="afterh", tag="raw11", align_bytes=64)
         mq = keep.tile([P, NQ, QW], BF16, name="mq", align_bytes=64)
         flat = lambda ap: ap.rearrange("p a v -> p (a v)")
@@ -290,12 +297,12 @@ def tile_picked_wsagecat_maxrelu_l_kernel(
                 for b in range(2):
                     second(sums(q, b), b, q, 0)
 
+        largest(two2[:], work[:, 0, :], work[:, 1, :])
         gather_q(0, 0, 2, flat(free[:, 0:2, :]))
         gather_q(1, 0, 1, free[:, 4, :])
-        largest(held[:, 1, :], work[:, 0, :], work[:, 1, :])
         gather_q(2, 0, 2, flat(free[:, 2:4, :]))
         largest(mq[:, 0, :], free[:, 0, :], free[:, 4, :])
-        largest(zp[:, :, 2, :], quarters(held[:, 1, :]), quarters(held[:, 0, :]))
+        largest(zp[:, :, 2, :], quarters(two2[:]), quarters(work[:, 2, :]))
         largest(zp[:, 0, t, :], mq[:, 0, :], free[:, 2, :])
         interleave(0)
         gather_q(1, 1, 2, afterh[:, 2, :])

@@ -150,14 +150,15 @@ def tile_picked_wsagecat_maxrelu_l_kernel(
         def largest(dst, a, b):
             nc.vector.tensor_tensor(dst, a, b, ALU.max)
 
-        early = keep.tile([P, 2, T], BF16, name="early", align_bytes=64)
-        gather(0, 0, early[:, 0, :])
+        early = keep.tile([P, T], BF16, name="early", align_bytes=64)
+        gather(0, 0, early[:])
         cast(0, 1, 0)
         quant_low(0, 1)
         first(1, 0)
         cast(0, 1, 1)
         quant_high(0, 1)
-        gather(0, 1, early[:, 1, :])
+        middle = keep.tile([P, T], BF16, name="middle", tag="raw01", align_bytes=64)
+        gather(0, 1, middle[:])
         cast(1, 1, 0)
         quant_low(1, 1)
         first(1, 1)
@@ -166,13 +167,28 @@ def tile_picked_wsagecat_maxrelu_l_kernel(
             nc.scalar.activation(hh[1][:, s * TH : (s + 1) * TH], hb[1, s][:], ACT.Relu)
         late = keep.tile([P, 2, T], BF16, name="late", tag="lowq11", align_bytes=64)
         gather(0, 2, late[:, 0, :])
-        largest(late[:, 1, :], early[:, 0, :], early[:, 1, :])
+        largest(late[:, 1, :], early[:], middle[:])
         quant_high(1, 1)
+
+        def largest_aside(n, dst, a, b, tags):
+            ahead = []
+            for s in range(2):
+                qs = slice(2 * s, 2 * s + 2)
+                diff = keep.tile([P, 2, QW], F32, name=f"diff{n}{s}", tag=tags[s], align_bytes=64)
+                nc.gpsimd.tensor_tensor(diff[:], quarters(a)[:, qs, :], quarters(b)[:, qs, :], ALU.subtract)
+                ahead.append(keep.tile([P, 2, QW], F32, name=f"ahead{n}{s}", tag=f"ahead{n}{s}", align_bytes=64))
+                nc.scalar.activation(ahead[s][:], diff[:], ACT.Relu)
+            for s in range(2):
+                qs = slice(2 * s, 2 * s + 2)
+                nc.gpsimd.tensor_tensor(dst[:, qs, :], ahead[s][:], quarters(b)[:, qs, :], ALU.add)
+
+        largest_aside(0, zp[:, :, 0, :], late[:, 1, :], late[:, 0, :], ("diff00", "diff01"))
         hs = keep.tile([P, PACK, T], F32, name="hs", tag="raw11", align_bytes=64)
         for c in range(2):
             own = (lo, hi)[c]
             nc.sync.dma_start(out=hs[own, 0, :], in_=hh[c][lo, 0:T])
             nc.sync.dma_start(out=hs[own, 1, :], in_=hh[c][hi, 0:T])
+        nc.sync.dma_start(out=zp[lo, :, 1, :], in_=zp[hi, :, 0, :])
         for k in range(2, PACK):
             for z in reversed(range(PASSES)):
                 first(k, z)
@@ -185,24 +201,20 @@ def tile_picked_wsagecat_maxrelu_l_kernel(
         two1 = keep.tile([P, T], BF16, name="two1", align_bytes=64)
         for d in range(LISTS):
             gather(1, d, got1[d][:])
-        sides = ((late[:, 1, :], late[:, 0, :]), (got1[0][:], got1[1][:]))
-        ahead = []
-        for n, (a, b) in enumerate(sides):
-            diff = keep.tile([P, T], F32, name=f"diff{n}", align_bytes=64)
-            nc.gpsimd.tensor_tensor(diff[:], a, b, ALU.subtract)
-            ahead.append(keep.tile([P, T], F32, name=f"ahead{n}", tag=f"ahead{n}", align_bytes=64))
-            nc.scalar.activation(ahead[n][:], diff[:], ACT.Relu)
-        nc.gpsimd.tensor_tensor(zp[:, :, 0, :], quarters(ahead[0][:]), quarters(sides[0][1]), ALU.add)
-        nc.sync.dma_start(out=zp[lo, :, 1, :], in_=zp[hi, :, 0, :])
-        nc.gpsimd.tensor_tensor(two1[:], ahead[1][:], sides[1][1], ALU.add)
+        largest_aside(1, quarters(two1[:]), got1[0][:], got1[1][:], ("ahead00", "ahead01"))
 
         work = keep.tile([P, 3, T], BF16, name="work", align_bytes=64)
-        two2 = keep.tile([P, T], BF16, name="two2", tag="ahead1", align_bytes=64)
+        two2 = keep.tile([P, T], BF16, name="two2", tag="ahead11", align_bytes=64)
         for d in range(LISTS):
             gather(2, d, work[:, d, :])
-        largest(zt[:], quarters(two1[:]), quarters(got1[2][:]))
-        nc.sync.dma_start(out=zp[hi, :, 1, :], in_=zt[hi, :, :])
-        nc.sync.dma_start(out=zp[hi, :, 0, :], in_=zt[lo, :, :])
+        lead = keep.tile([P, QW], BF16, name="lead", tag="ahead10", align_bytes=64)
+        for s in range(2):
+            qs = slice(2 * s, 2 * s + 2)
+            largest(zt[:, qs, :], quarters(two1[:])[:, qs, :], quarters(got1[2][:])[:, qs, :])
+            nc.sync.dma_start(out=zp[hi, qs, 1, :], in_=zt[hi, qs, :])
+            nc.sync.dma_start(out=zp[hi, qs, 0, :], in_=zt[lo, qs, :])
+            if s == 0:
+                gather(PACK - 1, 1, lead[:], 0, QW)
 
         h4 = keep.tile([P, T, PACK], BF16, name="h4", tag="got10", align_bytes=64)
         nc.scalar.copy(
@@ -278,7 +290,7 @@ def tile_picked_wsagecat_maxrelu_l_kernel(
                 nc.vector.tensor_copy(dst, src)
 
         t = PACK - 1
-        free = keep.tile([P, 5, QW], BF16, name="free", tag="got11", align_bytes=64)
+        free = keep.tile([P, 4, QW], BF16, name="free", tag="got11", align_bytes=64)
         afterh = keep.tile([P, 3, QW], BF16, name="afterh", tag="raw11", align_bytes=64)
         mq = keep.tile([P, NQ, QW], BF16, name="mq", align_bytes=64)
         flat = lambda ap: ap.rearrange("p a v -> p (a v)")
@@ -299,9 +311,8 @@ def tile_picked_wsagecat_maxrelu_l_kernel(
 
         largest(two2[:], work[:, 0, :], work[:, 1, :])
         gather_q(0, 0, 2, flat(free[:, 0:2, :]))
-        gather_q(1, 0, 1, free[:, 4, :])
         gather_q(2, 0, 2, flat(free[:, 2:4, :]))
-        largest(mq[:, 0, :], free[:, 0, :], free[:, 4, :])
+        largest(mq[:, 0, :], free[:, 0, :], lead[:])
         largest(zp[:, :, 2, :], quarters(two2[:]), quarters(work[:, 2, :]))
         largest(zp[:, 0, t, :], mq[:, 0, :], free[:, 2, :])
         interleave(0)

@@ -23,6 +23,33 @@ WIN = 1024
 QW = 128
 NQ = T // QW
 LISTS = 3
+SHARES = (48, 48, 32)
+LOW = PACK - 1
+COLUMNS = (
+    (0, 0, 48), (1, 0, 48), (2, 0, 32),
+    (2, 32, 32), (0, 48, 48), (1, 48, 48),
+    (0, 96, 32), (1, 96, 32), (2, 64, 64),
+    (3, 0, 128),
+)
+
+
+def column_of(lane, group):
+    col = 0
+    for run_lane, g0, count in COLUMNS:
+        if run_lane == lane and g0 <= group < g0 + count:
+            return col + group - g0
+        col = col + count
+    raise ValueError
+
+
+def runs_of(k):
+    runs = []
+    for lane, g0, count in COLUMNS[LOW * k : LOW * (k + 1)]:
+        while count:
+            piece = max(n for n in (16, 32, 64) if n <= count)
+            runs.append((column_of(lane, g0) - k * P, piece, lane, g0))
+            g0, count = g0 + piece, count - piece
+    return runs
 
 
 def tile_picked_wsagecat_maxrelu_l_kernel(
@@ -38,16 +65,15 @@ def tile_picked_wsagecat_maxrelu_l_kernel(
         w_sc = keep.tile([P, 2, N], U8, name="w_sc", align_bytes=64)
         hh = [keep.tile([P, WIN if k < PACK - 1 else T], F32, name=f"hh{k}", align_bytes=64) for k in range(PACK)]
 
-        HALF = H // 2
-        MH = HALF // PACK
         raw = {}
         x_w = []
         w1v = w1.rearrange("(z p j) c -> z p j c", z=PASSES, j=PACK)
-        poss = (pos1, pos2, pos3)
+        starts = [sum(SHARES[:c]) for c in range(len(SHARES))]
 
         def load_w1(z, c):
-            raw[z, c] = keep.tile([P, PACK, HALF], F32, name=f"raw{z}{c}", tag=f"raw{z}{c}", align_bytes=64)
-            nc.sync.dma_start(out=raw[z, c][:], in_=w1v[z, :, :, c * HALF : (c + 1) * HALF])
+            cols = slice(PACK * starts[c], PACK * (starts[c] + SHARES[c]))
+            raw[z, c] = keep.tile([P, PACK, PACK * SHARES[c]], F32, name=f"raw{z}{c}", tag=f"raw{z}{c}", align_bytes=64)
+            nc.sync.dma_start(out=raw[z, c][:], in_=w1v[z, :, :, cols])
 
         xs_v = x_scales.bitcast(I32).rearrange("z (q r) c -> r q z c", r=PACK)
         load_w1(0, 0)
@@ -55,13 +81,15 @@ def tile_picked_wsagecat_maxrelu_l_kernel(
             nc.sync.dma_start(out=x_sc[r:P:32, :, :].bitcast(I32), in_=xs_v[r])
         load_w1(1, 0)
         for z in range(PASSES):
-            x_w.append(keep.tile([P, T], U32, name=f"x_w{z}", tag=f"x_w{z}", align_bytes=64))
+            x_w.append(keep.tile([P, T], U32, name=f"x_w{z}", align_bytes=64))
             nc.sync.dma_start(out=x_w[z][:].bitcast(I32), in_=x_words[z].rearrange("p c r -> p (c r)").bitcast(I32))
         nc.sync.dma_start(lists[0][:], pos1)
         load_w1(0, 1)
-        for d in range(1, LISTS):
-            nc.sync.dma_start(lists[d][:], poss[d])
+        nc.sync.dma_start(lists[1][:], pos2)
         load_w1(1, 1)
+        for z in range(PASSES):
+            load_w1(z, 2)
+        nc.sync.dma_start(lists[2][:], pos3)
         w_w = []
         for a, (words, scales) in enumerate(((w2_words, w2_scales), (w3_words, w3_scales))):
             sv = scales[0].bitcast(I32).rearrange("(q r) c -> r q c", r=PACK)
@@ -71,40 +99,29 @@ def tile_picked_wsagecat_maxrelu_l_kernel(
             w_w.append(keep.tile([P, 2 * N], U8, name=f"w_w{a}", align_bytes=64))
             nc.sync.dma_start(out=w_w[a][:].bitcast(I32), in_=words[0].bitcast(I32))
 
-        lowq = {}
-        lowc = {}
-        lows = {}
-        for z in range(PASSES):
-            for c in range(2):
-                lowq[z, c] = keep.tile([P, 2, MH, PACK], BF16, name=f"lowq{z}{c}", tag=f"lowq{z}{c}", align_bytes=64)
-                lowc[z, c] = keep.tile([P, P], U32, name=f"lowc{z}{c}", align_bytes=64)
-                lows[z, c] = keep.tile([P, P], U8, name=f"lows{z}{c}", align_bytes=64)
-        highq = keep.tile([P, PASSES, 2, 2, MH, PACK], BF16, name="highq", align_bytes=64)
-        highc = keep.tile([P, PASSES, 2, P], U32, name="highc", tag="highc", align_bytes=64)
-        highs = keep.tile([P, PASSES, 2, P], U8, name="highs", align_bytes=64)
+        SPAN = 720
+        wq = [keep.tile([P, SPAN, PACK], BF16, name=f"wq{z}", align_bytes=64) for z in range(PASSES)]
+        wc = [keep.tile([P, H], U32, name=f"wc{z}", align_bytes=64) for z in range(PASSES)]
+        ws = [keep.tile([P, H], U8, name=f"ws{z}", align_bytes=64) for z in range(PASSES)]
 
-        def cast(z, c, u):
-            src = raw[z, c][:].rearrange("p j (m t) -> p m j t", t=PACK)[:, :, :, 2 * u : 2 * u + 2]
-            dst = (lowq[z, c][:] if u == 0 else highq[:, z, :, c, :, :]).rearrange("p t m j -> p m j t")
-            if c == 1 or u == 1:
-                nc.scalar.activation(dst, src, ACT.Copy)
-            else:
+        def cast(z, c, u, m0=0, m1=None):
+            m1 = SHARES[c] if m1 is None else m1
+            base = column_of(2 * u, starts[c] + m0)
+            step = column_of(2 * u + 1, starts[c] + m0) - base
+            src = raw[z, c][:].rearrange("p j (m t) -> p m j t", t=PACK)[:, m0:m1, :, 2 * u : 2 * u + 2]
+            dst = wq[z][:, base : base + 2 * step, :].rearrange("p (t m) j -> p m j t", t=2)[:, 0 : m1 - m0, :, :]
+            if (c, u) == (0, 0):
                 nc.vector.tensor_copy(dst, src)
+            else:
+                nc.scalar.activation(dst, src, ACT.Copy)
 
-        def quant_low(z, c):
+        def quant_w1(z, k0, k1):
+            cols = slice(k0 * P, k1 * P)
             nc.vector.quantize_mx(
-                out=lowc[z, c][:].bitcast(FP8X4),
-                scales=lows[z, c][:],
-                in_=lowq[z, c][:].rearrange("p t m j -> p (t m j)"),
+                out=wc[z][:, cols].bitcast(FP8X4),
+                scales=ws[z][:, cols],
+                in_=wq[z][:, cols, :].rearrange("p m j -> p (m j)"),
             )
-
-        def quant_high(z, c):
-            for t in range(2):
-                nc.vector.quantize_mx(
-                    out=highc[:, z, t, c * MH : (c + 1) * MH].bitcast(FP8X4),
-                    scales=highs[:, z, t, c * MH : (c + 1) * MH],
-                    in_=highq[:, z, t, c, :, :].rearrange("p m j -> p (m j)"),
-                )
 
         TH = T // 2
         hb = {(k, 0): psum.tile([P, T], F32, name=f"hb{k}", tag=f"bank{k}") for k in range(2, PACK)}
@@ -115,106 +132,104 @@ def tile_picked_wsagecat_maxrelu_l_kernel(
         def first(k, z):
             parts = 2 if k < 2 else 1
             width = T // parts
-            codes = lowc[z, k][:] if k < 2 else highc[:, z, k - 2, :]
-            scales = lows[z, k][:] if k < 2 else highs[:, z, k - 2, :]
             for s in range(parts):
                 nc.tensor.matmul_mx(
                     out=hb[k, s][:],
-                    lhsT=codes.bitcast(FP8X4),
-                    lhsT_scale=scales,
+                    lhsT=wc[z][:, k * P : (k + 1) * P].bitcast(FP8X4),
+                    lhsT_scale=ws[z][:, k * P : (k + 1) * P],
                     rhs=x_w[z][:, s * width : (s + 1) * width].bitcast(FP8X4),
                     rhs_scale=x_sc[:, z, s * width : (s + 1) * width],
-                    start=(z == (0 if k < 2 else 1)),
-                    stop=(z == (1 if k < 2 else 0)),
+                    start=(z == 0),
+                    stop=(z == PASSES - 1),
                 )
 
         zp = keep.tile([P, NQ, PACK, QW], BF16, name="zp", tag="zp", align_bytes=64)
-        HP = P // 2
-        lo, hi = slice(0, HP), slice(HP, P)
+        quarters = lambda ap: ap.rearrange("p (q v) -> p q v", q=NQ)
 
         def gather(k, d, dst, c0=0, c1=T):
             nc.vector.tensor_copy(dst, hh[k][:].indirect(lists[d][:, c0 // 16 : c1 // 16]))
 
-        for z in range(PASSES):
-            cast(z, 0, 0)
-            quant_low(z, 0)
-            cast(z, 0, 1)
-            first(0, z)
-        for s in range(2):
-            nc.scalar.activation(hh[0][:, s * TH : (s + 1) * TH], hb[0, s][:], ACT.Relu)
-        for z in range(PASSES):
-            quant_high(z, 0)
-
-        quarters = lambda ap: ap.rearrange("p (q v) -> p q v", q=NQ)
-
         def largest(dst, a, b):
             nc.vector.tensor_tensor(dst, a, b, ALU.max)
-
-        early = keep.tile([P, T], BF16, name="early", align_bytes=64)
-        gather(0, 0, early[:])
-        cast(0, 1, 0)
-        quant_low(0, 1)
-        first(1, 0)
-        cast(0, 1, 1)
-        quant_high(0, 1)
-        middle = keep.tile([P, T], BF16, name="middle", tag="raw01", align_bytes=64)
-        gather(0, 1, middle[:])
-        cast(1, 1, 0)
-        quant_low(1, 1)
-        first(1, 1)
-        cast(1, 1, 1)
-        for s in range(2):
-            nc.scalar.activation(hh[1][:, s * TH : (s + 1) * TH], hb[1, s][:], ACT.Relu)
-        late = keep.tile([P, 2, T], BF16, name="late", tag="lowq11", align_bytes=64)
-        gather(0, 2, late[:, 0, :])
-        largest(late[:, 1, :], early[:], middle[:])
-        quant_high(1, 1)
 
         def largest_aside(n, dst, a, b, tags):
             ahead = []
             for s in range(2):
-                qs = slice(2 * s, 2 * s + 2)
-                diff = keep.tile([P, 2, QW], F32, name=f"diff{n}{s}", tag=tags[s], align_bytes=64)
-                nc.gpsimd.tensor_tensor(diff[:], quarters(a)[:, qs, :], quarters(b)[:, qs, :], ALU.subtract)
-                ahead.append(keep.tile([P, 2, QW], F32, name=f"ahead{n}{s}", tag=f"ahead{n}{s}", align_bytes=64))
+                cols = slice(s * TH, (s + 1) * TH)
+                diff = keep.tile([P, TH], F32, name=f"diff{n}{s}", tag=tags[s], align_bytes=64)
+                nc.gpsimd.tensor_tensor(diff[:], a[:, cols], b[:, cols], ALU.subtract)
+                ahead.append(keep.tile([P, TH], F32, name=f"ahead{n}{s}", tag=f"ahead{n}{s}", align_bytes=64))
                 nc.scalar.activation(ahead[s][:], diff[:], ACT.Relu)
             for s in range(2):
-                qs = slice(2 * s, 2 * s + 2)
-                nc.gpsimd.tensor_tensor(dst[:, qs, :], ahead[s][:], quarters(b)[:, qs, :], ALU.add)
+                cols = slice(s * TH, (s + 1) * TH)
+                nc.gpsimd.tensor_tensor(dst[:, cols], ahead[s][:], b[:, cols], ALU.add)
 
-        largest_aside(0, zp[:, :, 0, :], late[:, 1, :], late[:, 0, :], ("diff00", "diff01"))
+        def move_h(k):
+            for p0, count, lane, g0 in runs_of(k):
+                nc.sync.dma_start(out=hs[g0 : g0 + count, lane, :], in_=hh[k][p0 : p0 + count, 0:T])
+
+        def move_z(k):
+            for p0, count, lane, g0 in runs_of(k):
+                nc.sync.dma_start(out=zp[g0 : g0 + count, :, lane, :], in_=quarters(zt[k][p0 : p0 + count, :]))
+
+        for z in range(PASSES):
+            cast(z, 0, 0)
+            cast(z, 0, 1)
+            quant_w1(z, 0, 1)
+            first(0, z)
+        for s in range(2):
+            nc.scalar.activation(hh[0][:, s * TH : (s + 1) * TH], hb[0, s][:], ACT.Relu)
+
+        early = keep.tile([P, T], BF16, name="early", align_bytes=64)
+        gather(0, 0, early[:])
+        cast(0, 1, 0)
+        cast(0, 1, 1, 0, 16)
+        quant_w1(0, 1, 2)
+        first(1, 0)
+        cast(0, 1, 1, 16)
+        middle = keep.tile([P, T], BF16, name="middle", tag="raw01", align_bytes=64)
+        gather(0, 1, middle[:])
+        cast(1, 1, 0)
+        cast(1, 1, 1, 0, 16)
+        quant_w1(1, 1, 2)
+        first(1, 1)
+        cast(1, 1, 1, 16)
+        for z in range(PASSES):
+            for u in range(2):
+                cast(z, 2, u)
+        for s in range(2):
+            nc.scalar.activation(hh[1][:, s * TH : (s + 1) * TH], hb[1, s][:], ACT.Relu)
+        quant_w1(0, 2, PACK)
+        late = keep.tile([P, T], BF16, name="late", tag="raw02", align_bytes=64)
+        gather(0, 2, late[:])
+        quant_w1(1, 2, PACK)
+        two0 = keep.tile([P, T], BF16, name="two0", tag="raw12", align_bytes=64)
+        largest(two0[:], early[:], middle[:])
+        zt = [keep.tile([P, T], BF16, name=f"zt{k}", align_bytes=64) for k in range(LOW)]
+        largest_aside(0, zt[0], two0, late, ("diff00", "diff01"))
         hs = keep.tile([P, PACK, T], F32, name="hs", tag="raw11", align_bytes=64)
-        for c in range(2):
-            own = (lo, hi)[c]
-            nc.sync.dma_start(out=hs[own, 0, :], in_=hh[c][lo, 0:T])
-            nc.sync.dma_start(out=hs[own, 1, :], in_=hh[c][hi, 0:T])
-        nc.sync.dma_start(out=zp[lo, :, 1, :], in_=zp[hi, :, 0, :])
         for k in range(2, PACK):
-            for z in reversed(range(PASSES)):
+            for z in range(PASSES):
                 first(k, z)
             nc.scalar.activation(hh[k][:, 0:T], hb[k, 0][:], ACT.Relu)
-        for k in range(2, PACK):
-            nc.scalar.activation(hs[:, k, :], hb[k, 0][:], ACT.Relu)
+        nc.scalar.activation(hs[:, LOW, :], hb[LOW, 0][:], ACT.Relu)
+        for k in range(LOW):
+            move_h(k)
 
-        zt = keep.tile([P, NQ, QW], BF16, name="zt", align_bytes=64)
         got1 = [keep.tile([P, T], BF16, name=f"got1{d}", tag=f"got1{d}", align_bytes=64) for d in range(LISTS)]
         two1 = keep.tile([P, T], BF16, name="two1", align_bytes=64)
         for d in range(LISTS):
             gather(1, d, got1[d][:])
-        largest_aside(1, quarters(two1[:]), got1[0][:], got1[1][:], ("ahead00", "ahead01"))
+        largest_aside(1, two1, got1[0][:], got1[1][:], ("ahead00", "ahead01"))
 
-        work = keep.tile([P, 3, T], BF16, name="work", align_bytes=64)
+        move_z(0)
+        work = keep.tile([P, 3, T], BF16, name="work", tag="work", align_bytes=64)
         two2 = keep.tile([P, T], BF16, name="two2", tag="ahead11", align_bytes=64)
         for d in range(LISTS):
             gather(2, d, work[:, d, :])
-        lead = keep.tile([P, QW], BF16, name="lead", tag="ahead10", align_bytes=64)
-        for s in range(2):
-            qs = slice(2 * s, 2 * s + 2)
-            largest(zt[:, qs, :], quarters(two1[:])[:, qs, :], quarters(got1[2][:])[:, qs, :])
-            nc.sync.dma_start(out=zp[hi, qs, 1, :], in_=zt[hi, qs, :])
-            nc.sync.dma_start(out=zp[hi, qs, 0, :], in_=zt[lo, qs, :])
-            if s == 0:
-                gather(PACK - 1, 1, lead[:], 0, QW)
+        largest(two2[:], work[:, 0, :], work[:, 1, :])
+        largest(zt[1][:], two1[:], got1[2][:])
+        move_z(1)
 
         h4 = keep.tile([P, T, PACK], BF16, name="h4", tag="got10", align_bytes=64)
         nc.scalar.copy(
@@ -290,9 +305,7 @@ def tile_picked_wsagecat_maxrelu_l_kernel(
                 nc.vector.tensor_copy(dst, src)
 
         t = PACK - 1
-        free = keep.tile([P, 4, QW], BF16, name="free", tag="got11", align_bytes=64)
-        afterh = keep.tile([P, 3, QW], BF16, name="afterh", tag="raw11", align_bytes=64)
-        mq = keep.tile([P, NQ, QW], BF16, name="mq", align_bytes=64)
+        free = keep.tile([P, LISTS, 2, QW], BF16, name="free", tag="got12", align_bytes=64)
         flat = lambda ap: ap.rearrange("p a v -> p (a v)")
 
         def gather_q(d, q0, q1, dst):
@@ -309,29 +322,27 @@ def tile_picked_wsagecat_maxrelu_l_kernel(
                 for b in range(2):
                     second(sums(q, b), b, q, 0)
 
-        largest(two2[:], work[:, 0, :], work[:, 1, :])
-        gather_q(0, 0, 2, flat(free[:, 0:2, :]))
-        gather_q(2, 0, 2, flat(free[:, 2:4, :]))
-        largest(mq[:, 0, :], free[:, 0, :], lead[:])
-        largest(zp[:, :, 2, :], quarters(two2[:]), quarters(work[:, 2, :]))
-        largest(zp[:, 0, t, :], mq[:, 0, :], free[:, 2, :])
+        largest(zt[2][:], two2[:], work[:, 2, :])
+        move_z(2)
+        for d in range(LISTS):
+            gather_q(d, 0, 2, flat(free[:, d, :, :]))
+        rest = keep.tile([P, 7, QW], BF16, name="rest", tag="raw11", align_bytes=64)
+        largest(rest[:, 5:7, :], free[:, 0, :, :], free[:, 1, :, :])
+        gather_q(0, 2, 4, flat(rest[:, 0:2, :]))
+        largest(zp[:, 0:2, t, :], rest[:, 5:7, :], free[:, 2, :, :])
         interleave(0)
-        gather_q(1, 1, 2, afterh[:, 2, :])
-        quant_h(0)
-        largest(mq[:, 1, :], free[:, 1, :], afterh[:, 2, :])
-        gather_q(0, 2, 4, flat(afterh[:, 0:2, :]))
-        largest(zp[:, 1, t, :], mq[:, 1, :], free[:, 3, :])
         interleave(1)
-        gather_q(1, 2, 4, flat(zp[:, 0, 0:2, :]))
+        quant_h(0)
+        gather_q(1, 2, 4, flat(rest[:, 2:4, :]))
+        gather_q(2, 2, 3, rest[:, 4, :])
+        spent = zp[:, 0, :, :]
         finish(0)
-        gather_q(2, 2, 3, zp[:, 0, 2, :])
-        largest(mq[:, 2:4, :], afterh[:, 0:2, :], zp[:, 0, 0:2, :])
-        end = z4[0][:].rearrange("p v t -> p (v t)")[:, 0:QW]
-        gather_q(2, 3, 4, end)
-        largest(zp[:, 2, t, :], mq[:, 2, :], zp[:, 0, 2, :])
+        largest(spent[:, 0:2, :], rest[:, 0:2, :], rest[:, 2:4, :])
+        gather_q(2, 3, 4, spent[:, 2, :])
+        largest(zp[:, 2, t, :], spent[:, 0, :], rest[:, 4, :])
         interleave(2)
         quant_h(1)
-        largest(zp[:, 3, t, :], mq[:, 3, :], end)
+        largest(zp[:, 3, t, :], spent[:, 1, :], spent[:, 2, :])
         finish(1)
         interleave(3)
         finish(2)

@@ -22,34 +22,20 @@ PASSES = K // (P * PACK)
 WIN = 1024
 QW = 128
 NQ = T // QW
+LAST = NQ - 1
+TA = LAST * QW
 LISTS = 3
-SHARES = (48, 48, 32)
-LOW = PACK - 1
-COLUMNS = (
-    (0, 0, 48), (1, 0, 48), (2, 0, 32),
-    (2, 32, 32), (0, 48, 48), (1, 48, 48),
-    (0, 96, 32), (1, 96, 32), (2, 64, 64),
-    (3, 0, 128),
-)
-
-
-def column_of(lane, group):
-    col = 0
-    for run_lane, g0, count in COLUMNS:
-        if run_lane == lane and g0 <= group < g0 + count:
-            return col + group - g0
-        col = col + count
-    raise ValueError
+WORDS = (32, 32, 64)
+RUN = 8
+HALVES = ((0, 256), (256, 512))
+CUTS = (((0, 256), (256, 384), (384, 512)), HALVES, HALVES, ((0, 512),))
+BANKS = ((0, 4, 7), (1, 5), (2, 6), (3,))
 
 
 def runs_of(k):
-    runs = []
-    for lane, g0, count in COLUMNS[LOW * k : LOW * (k + 1)]:
-        while count:
-            piece = max(n for n in (16, 32, 64) if n <= count)
-            runs.append((column_of(lane, g0) - k * P, piece, lane, g0))
-            g0, count = g0 + piece, count - piece
-    return runs
+    if k < 2:
+        return [(32 * t, 32, t, 32 * k) for t in range(PACK)]
+    return [(64 * u, 64, 2 * (k - 2) + u, 64) for u in range(2)]
 
 
 def tile_picked_wsagecat_maxrelu_l_kernel(
@@ -60,290 +46,290 @@ def tile_picked_wsagecat_maxrelu_l_kernel(
         keep = ctx.enter_context(tc.tile_pool(name="keep", bufs=1))
         psum = ctx.enter_context(tc.psum_pool(name="psum", bufs=1))
 
+        def tile(shape, dtype, name, on=None):
+            return keep.tile(shape, dtype, name=name, tag=on or name, align_bytes=64)
+
         lists = [keep.tile([P, T // 16], U16, name=f"list{d}") for d in range(LISTS)]
-        x_sc = keep.tile([P, PASSES, T], U8, name="x_sc", align_bytes=64)
-        w_sc = keep.tile([P, 2, N], U8, name="w_sc", align_bytes=64)
-        hh = [keep.tile([P, WIN if k < PACK - 1 else T], F32, name=f"hh{k}", align_bytes=64) for k in range(PACK)]
+        x_sc = tile([P, PASSES, T], U8, "x_sc")
+        w_sc = tile([P, 2, N], U8, "w_sc")
 
         raw = {}
-        x_w = []
         w1v = w1.rearrange("(z p j) c -> z p j c", z=PASSES, j=PACK)
-        starts = [sum(SHARES[:c]) for c in range(len(SHARES))]
+        starts = [sum(WORDS[:c]) for c in range(len(WORDS))]
 
         def load_w1(z, c):
-            cols = slice(PACK * starts[c], PACK * (starts[c] + SHARES[c]))
-            raw[z, c] = keep.tile([P, PACK, PACK * SHARES[c]], F32, name=f"raw{z}{c}", tag=f"raw{z}{c}", align_bytes=64)
+            cols = slice(PACK * starts[c], PACK * (starts[c] + WORDS[c]))
+            raw[z, c] = tile([P, PACK, PACK * WORDS[c]], F32, f"raw{z}{c}")
             nc.sync.dma_start(out=raw[z, c][:], in_=w1v[z, :, :, cols])
 
         xs_v = x_scales.bitcast(I32).rearrange("z (q r) c -> r q z c", r=PACK)
-        load_w1(0, 0)
         for r in range(PACK):
             nc.sync.dma_start(out=x_sc[r:P:32, :, :].bitcast(I32), in_=xs_v[r])
+            if r == 0:
+                load_w1(0, 0)
         load_w1(1, 0)
-        for z in range(PASSES):
-            x_w.append(keep.tile([P, T], U32, name=f"x_w{z}", align_bytes=64))
-            nc.sync.dma_start(out=x_w[z][:].bitcast(I32), in_=x_words[z].rearrange("p c r -> p (c r)").bitcast(I32))
-        nc.sync.dma_start(lists[0][:], pos1)
+        x_w = tile([P, PASSES, T], U32, "x_w")
+        xw_v = x_words.rearrange("z p c r -> p z (c r)").bitcast(I32)
+        for c0, c1 in HALVES:
+            nc.sync.dma_start(out=x_w[:, :, c0:c1].bitcast(I32), in_=xw_v[:, :, c0:c1])
         load_w1(0, 1)
-        nc.sync.dma_start(lists[1][:], pos2)
+        nc.sync.dma_start(lists[0][:], pos1)
         load_w1(1, 1)
-        for z in range(PASSES):
-            load_w1(z, 2)
+        load_w1(0, 2)
+        nc.sync.dma_start(lists[1][:], pos2)
         nc.sync.dma_start(lists[2][:], pos3)
+        load_w1(1, 2)
         w_w = []
-        for a, (words, scales) in enumerate(((w2_words, w2_scales), (w3_words, w3_scales))):
+        for a, scales in enumerate((w2_scales, w3_scales)):
             sv = scales[0].bitcast(I32).rearrange("(q r) c -> r q c", r=PACK)
             for r in range(PACK):
                 nc.sync.dma_start(out=w_sc[r:P:32, a, :].bitcast(I32), in_=sv[r])
         for a, words in enumerate((w2_words, w3_words)):
-            w_w.append(keep.tile([P, 2 * N], U8, name=f"w_w{a}", align_bytes=64))
+            w_w.append(tile([P, 2 * N], U8, f"w_w{a}"))
             nc.sync.dma_start(out=w_w[a][:].bitcast(I32), in_=words[0].bitcast(I32))
 
-        SPAN = 720
-        wq = [keep.tile([P, SPAN, PACK], BF16, name=f"wq{z}", align_bytes=64) for z in range(PASSES)]
-        wc = [keep.tile([P, H], U32, name=f"wc{z}", align_bytes=64) for z in range(PASSES)]
-        ws = [keep.tile([P, H], U8, name=f"ws{z}", align_bytes=64) for z in range(PASSES)]
+        wq = {(z, c): tile([P, PACK * WORDS[c], PACK], BF16, f"wq{z}{c}") for z in range(PASSES) for c in range(len(WORDS))}
+        wc = [tile([P, H], U32, f"wc{z}") for z in range(PASSES)]
+        ws = [tile([P, H], U8, f"ws{z}") for z in range(PASSES)]
 
-        def cast(z, c, u, m0=0, m1=None):
-            m1 = SHARES[c] if m1 is None else m1
-            base = column_of(2 * u, starts[c] + m0)
-            step = column_of(2 * u + 1, starts[c] + m0) - base
-            src = raw[z, c][:].rearrange("p j (m t) -> p m j t", t=PACK)[:, m0:m1, :, 2 * u : 2 * u + 2]
-            dst = wq[z][:, base : base + 2 * step, :].rearrange("p (t m) j -> p m j t", t=2)[:, 0 : m1 - m0, :, :]
-            if (c, u) == (0, 0):
+        def cast(z, c):
+            src = raw[z, c][:].rearrange("p j (m t) -> p m j t", t=PACK)
+            dst = wq[z, c][:].rearrange("p (t m) j -> p m j t", t=PACK)
+            if c == 0:
+                nc.vector.tensor_copy(dst[:, :, :, 0:2], src[:, :, :, 0:2])
+                nc.scalar.activation(dst[:, :, :, 2:4], src[:, :, :, 2:4], ACT.Copy)
+            elif (z, c) == (0, 1):
                 nc.vector.tensor_copy(dst, src)
             else:
                 nc.scalar.activation(dst, src, ACT.Copy)
 
-        def quant_w1(z, k0, k1):
-            cols = slice(k0 * P, k1 * P)
+        def quant_w1(z, c):
+            cols = slice(PACK * starts[c], PACK * (starts[c] + WORDS[c]))
             nc.vector.quantize_mx(
                 out=wc[z][:, cols].bitcast(FP8X4),
                 scales=ws[z][:, cols],
-                in_=wq[z][:, cols, :].rearrange("p m j -> p (m j)"),
+                in_=wq[z, c][:].rearrange("p m j -> p (m j)"),
             )
 
         TH = T // 2
-        hb = {(k, 0): psum.tile([P, T], F32, name=f"hb{k}", tag=f"bank{k}") for k in range(2, PACK)}
-        for k in range(2):
-            for s in range(2):
-                hb[k, s] = psum.tile([P, TH], F32, name=f"hb{k}{s}", tag=f"bank{k + PACK * s}")
+        hb = {}
+        for k in range(PACK):
+            for s, (c0, c1) in enumerate(CUTS[k]):
+                hb[k, s] = psum.tile([P, c1 - c0], F32, name=f"hb{k}{s}", tag=f"bank{BANKS[k][s]}")
 
-        def first(k, z):
-            parts = 2 if k < 2 else 1
-            width = T // parts
-            for s in range(parts):
+        def first(k, z, only=None):
+            for s, (c0, c1) in enumerate(CUTS[k]):
+                if only is not None and s != only:
+                    continue
                 nc.tensor.matmul_mx(
                     out=hb[k, s][:],
                     lhsT=wc[z][:, k * P : (k + 1) * P].bitcast(FP8X4),
                     lhsT_scale=ws[z][:, k * P : (k + 1) * P],
-                    rhs=x_w[z][:, s * width : (s + 1) * width].bitcast(FP8X4),
-                    rhs_scale=x_sc[:, z, s * width : (s + 1) * width],
+                    rhs=x_w[:, z, c0:c1].bitcast(FP8X4),
+                    rhs_scale=x_sc[:, z, c0:c1],
                     start=(z == 0),
                     stop=(z == PASSES - 1),
                 )
 
-        zp = keep.tile([P, NQ, PACK, QW], BF16, name="zp", tag="zp", align_bytes=64)
-        quarters = lambda ap: ap.rearrange("p (q v) -> p q v", q=NQ)
+        hh = {}
 
-        def gather(k, d, dst, c0=0, c1=T):
-            nc.vector.tensor_copy(dst, hh[k][:].indirect(lists[d][:, c0 // 16 : c1 // 16]))
+        def window(k, on=None):
+            hh[k] = tile([P, WIN], F32, f"hh{k}", on)
+            for s, (c0, c1) in enumerate(CUTS[k]):
+                nc.scalar.activation(hh[k][:, c0:c1], hb[k, s][:], ACT.Relu)
+
+        hs = tile([P, PACK, T], F32, "hs")
+        zp = tile([P, LAST, PACK, QW], BF16, "zp")
+
+        def gather(k, d, dst):
+            nc.vector.tensor_copy(dst, hh[k][:].indirect(lists[d][:, 0 : TA // 16]))
+
+        def gather_last(d, dst):
+            view = dst.rearrange("p (s t v) -> p s t v", s=2, t=PACK)
+            for t in range(PACK):
+                nc.vector.tensor_copy(view[:, :, t, :], hs[:, t, :].indirect(lists[d][:, TA // 16 : T // 16]))
 
         def largest(dst, a, b):
             nc.vector.tensor_tensor(dst, a, b, ALU.max)
 
-        def largest_aside(n, dst, a, b, tags):
-            ahead = []
-            for s in range(2):
-                cols = slice(s * TH, (s + 1) * TH)
-                diff = keep.tile([P, TH], F32, name=f"diff{n}{s}", tag=tags[s], align_bytes=64)
-                nc.gpsimd.tensor_tensor(diff[:], a[:, cols], b[:, cols], ALU.subtract)
-                ahead.append(keep.tile([P, TH], F32, name=f"ahead{n}{s}", tag=f"ahead{n}{s}", align_bytes=64))
-                nc.scalar.activation(ahead[s][:], diff[:], ACT.Relu)
-            for s in range(2):
-                cols = slice(s * TH, (s + 1) * TH)
-                nc.gpsimd.tensor_tensor(dst[:, cols], ahead[s][:], b[:, cols], ALU.add)
+        def halves():
+            return [slice(s * TA // 2, (s + 1) * TA // 2) for s in range(2)]
+
+        def lead(ahead, diffs, a, b):
+            for diff, cols in zip(diffs, halves()):
+                nc.gpsimd.tensor_tensor(diff, a[:, cols], b[:, cols], ALU.subtract)
+                nc.scalar.activation(ahead[:, cols], diff, ACT.Relu)
+
+        def top(dst, ahead, b):
+            for cols in halves():
+                nc.gpsimd.tensor_tensor(dst[:, cols], ahead[:, cols], b[:, cols], ALU.add)
 
         def move_h(k):
             for p0, count, lane, g0 in runs_of(k):
                 nc.sync.dma_start(out=hs[g0 : g0 + count, lane, :], in_=hh[k][p0 : p0 + count, 0:T])
 
-        def move_z(k):
+        def move_z(k, src):
             for p0, count, lane, g0 in runs_of(k):
-                nc.sync.dma_start(out=zp[g0 : g0 + count, :, lane, :], in_=quarters(zt[k][p0 : p0 + count, :]))
+                nc.sync.dma_start(
+                    out=zp[g0 : g0 + count, :, lane, :], in_=src[p0 : p0 + count, :].rearrange("p (q v) -> p q v", q=LAST)
+                )
 
         for z in range(PASSES):
-            cast(z, 0, 0)
-            cast(z, 0, 1)
-            quant_w1(z, 0, 1)
-            first(0, z)
-        for s in range(2):
-            nc.scalar.activation(hh[0][:, s * TH : (s + 1) * TH], hb[0, s][:], ACT.Relu)
-
-        early = keep.tile([P, T], BF16, name="early", align_bytes=64)
-        gather(0, 0, early[:])
-        cast(0, 1, 0)
-        cast(0, 1, 1, 0, 16)
-        quant_w1(0, 1, 2)
-        first(1, 0)
-        cast(0, 1, 1, 16)
-        middle = keep.tile([P, T], BF16, name="middle", tag="raw01", align_bytes=64)
-        gather(0, 1, middle[:])
-        cast(1, 1, 0)
-        cast(1, 1, 1, 0, 16)
-        quant_w1(1, 1, 2)
-        first(1, 1)
-        cast(1, 1, 1, 16)
-        for z in range(PASSES):
-            for u in range(2):
-                cast(z, 2, u)
-        for s in range(2):
-            nc.scalar.activation(hh[1][:, s * TH : (s + 1) * TH], hb[1, s][:], ACT.Relu)
-        quant_w1(0, 2, PACK)
-        late = keep.tile([P, T], BF16, name="late", tag="raw02", align_bytes=64)
-        gather(0, 2, late[:])
-        quant_w1(1, 2, PACK)
-        two0 = keep.tile([P, T], BF16, name="two0", tag="raw12", align_bytes=64)
-        largest(two0[:], early[:], middle[:])
-        zt = [keep.tile([P, T], BF16, name=f"zt{k}", align_bytes=64) for k in range(LOW)]
-        largest_aside(0, zt[0], two0, late, ("diff00", "diff01"))
-        hs = keep.tile([P, PACK, T], F32, name="hs", tag="raw11", align_bytes=64)
-        for k in range(2, PACK):
+            cast(z, 0)
+            quant_w1(z, 0)
+        for s in range(len(CUTS[0])):
             for z in range(PASSES):
-                first(k, z)
-            nc.scalar.activation(hh[k][:, 0:T], hb[k, 0][:], ACT.Relu)
-        nc.scalar.activation(hs[:, LOW, :], hb[LOW, 0][:], ACT.Relu)
-        for k in range(LOW):
-            move_h(k)
+                first(0, z, s)
+        window(0)
 
-        got1 = [keep.tile([P, T], BF16, name=f"got1{d}", tag=f"got1{d}", align_bytes=64) for d in range(LISTS)]
-        two1 = keep.tile([P, T], BF16, name="two1", align_bytes=64)
-        for d in range(LISTS):
-            gather(1, d, got1[d][:])
-        largest_aside(1, two1, got1[0][:], got1[1][:], ("ahead00", "ahead01"))
+        a0 = tile([P, TA], BF16, "a0")
+        gather(0, 0, a0[:])
+        for z in range(PASSES):
+            cast(z, 1)
+            quant_w1(z, 1)
+            first(1, z)
+        window(1)
+        b0 = tile([P, TA], BF16, "b0", "raw11")
+        gather(0, 1, b0[:])
+        c0 = tile([P, TA], BF16, "c0", "raw01")
+        gather(0, 2, c0[:])
+        cast(0, 2)
+        quant_w1(0, 2)
+        first(2, 0)
+        first(3, 0)
+        a1 = tile([P, TA], BF16, "a1", "raw02")
+        gather(1, 0, a1[:])
+        cast(1, 2)
+        quant_w1(1, 2)
+        first(2, 1)
+        first(3, 1)
+        bc1 = tile([P, 2, TA], BF16, "bc1", "raw12")
+        b1, c1 = bc1[:, 0, :], bc1[:, 1, :]
+        gather(1, 1, b1)
+        gather(1, 2, c1)
+        window(2)
+        move_h(0)
+        move_h(1)
+        move_h(2)
 
-        move_z(0)
-        work = keep.tile([P, 3, T], BF16, name="work", tag="work", align_bytes=64)
-        two2 = keep.tile([P, T], BF16, name="two2", tag="ahead11", align_bytes=64)
-        for d in range(LISTS):
-            gather(2, d, work[:, d, :])
-        largest(two2[:], work[:, 0, :], work[:, 1, :])
-        largest(zt[1][:], two1[:], got1[2][:])
-        move_z(1)
+        ahead0 = tile([P, TA], F32, "ahead0", "wq12")
+        early = [tile([P, TA // 2], F32, "diff00"), tile([P, TA // 2], F32, "diff01", "wq02")]
+        lead(ahead0, [d[:] for d in early], a0, b0)
+        m0 = tile([P, TA], BF16, "m0")
+        top(m0, ahead0, b0)
+        ahead2 = tile([P, TA], F32, "ahead2")
+        diff2 = tile([P, TA], F32, "diff2")
+        lead(ahead2, [diff2[:, cols] for cols in halves()], m0, c0)
+        ahead1 = tile([P, TA], F32, "ahead1")
+        diff1 = tile([P, TA], F32, "diff1", "raw11")
+        lead(ahead1, [diff1[:, cols] for cols in halves()], a1, b1)
+        z0 = tile([P, TA], BF16, "z0")
+        top(z0, ahead2, c0)
+        m1 = tile([P, TA], BF16, "m1", "diff2")
+        top(m1, ahead1, b1)
+        a23 = tile([P, 2, TA], BF16, "a23")
+        b23 = tile([P, 2, TA], BF16, "b23")
+        gather(2, 0, a23[:, 0, :])
+        gather(2, 1, b23[:, 0, :])
+        window(3, "wq12")
+        move_h(3)
+        move_z(0, z0)
+        c23 = tile([P, 2, TA], BF16, "c23")
+        gather(2, 2, c23[:, 0, :])
+        for d, dst in enumerate((a23, b23, c23)):
+            gather(3, d, dst[:, 1, :])
+        m23 = tile([P, 2, TA], BF16, "m23")
+        largest(m23[:], a23[:], b23[:])
+        z1 = tile([P, TA], BF16, "z1")
+        largest(z1[:], m1[:], c1)
+        z23 = tile([P, 2, TA], BF16, "z23", "ahead1")
+        largest(z23[:], m23[:], c23[:])
+        move_z(1, z1)
+        for k in range(2, PACK):
+            move_z(k, z23[:, k - 2, :])
 
-        h4 = keep.tile([P, T, PACK], BF16, name="h4", tag="got10", align_bytes=64)
-        nc.scalar.copy(
-            h4[:].rearrange("p (c i) t -> p c t i", i=4), hs[:].rearrange("p t (c i) -> p c t i", i=4)
-        )
-        hc = {}
-        hsc = keep.tile([P, T], U8, name="hsc", align_bytes=64)
-
-        outv = out.rearrange("(b p) v -> p b v", p=P)
-        zc = keep.tile([P, T - QW], U32, name="zc", align_bytes=64)
-        zsc = keep.tile([P, T], U8, name="zsc", align_bytes=64)
-        z4 = {}
-        last = NQ - 1
-
-        last_codes = []
-
-        def z_codes(q):
-            if q < last:
-                return zc[:, q * QW : (q + 1) * QW]
-            return last_codes[0][:]
-
-        def second(dst, b, q, a):
+        h4 = tile([P, T, PACK], BF16, "h4")
+        for q in range(NQ):
             cols = slice(q * QW, (q + 1) * QW)
-            codes = z_codes(q) if a == 1 else hc[q // 2][:, (q % 2) * QW : (q % 2 + 1) * QW]
-            scales = (hsc, zsc)[a][:, cols]
-            shared = q < last
-            nc.tensor.matmul_mx(
-                out=dst,
-                lhsT=w_w[a][:, 2 * P * b : 2 * P * (b + 1)].bitcast(FP4X4),
-                lhsT_scale=w_sc[:, a, P * b : P * (b + 1)],
-                rhs=codes.bitcast(FP8X4),
-                rhs_scale=scales,
-                start=(a == 0 and (b == 0 or not shared)),
-                stop=(a == 1 and (b == 1 or not shared)),
+            nc.scalar.copy(
+                h4[:, cols, :].rearrange("p (c i) t -> p c t i", i=4), hs[:, :, cols].rearrange("p t (c i) -> p c t i", i=4)
             )
+        hc = tile([P, T], U32, "hc")
+        hsc = tile([P, T], U8, "hsc")
+        zc = tile([P, T], U32, "zc")
+        zsc = tile([P, T], U8, "zsc")
+        outv = out.rearrange("(b p) v -> p b v", p=P)
 
-        def quant_z(q):
-            if q == last:
-                last_codes.append(keep.tile([P, QW], U32, name="zc_last", tag="zp", align_bytes=64))
-            nc.vector.quantize_mx(
-                out=z_codes(q).bitcast(FP8X4),
-                scales=zsc[:, q * QW : (q + 1) * QW],
-                in_=z4[q][:].rearrange("p v t -> p (v t)"),
-            )
+        pair = {q: psum.tile([P, 2, QW], F32, name=f"pair{q}", tag=f"bank{(0, 1, 4)[q]}") for q in range(LAST)}
+        lone = [psum.tile([P, QW], F32, name=f"lone{b}", tag=f"bank{(5, 7)[b]}") for b in range(2)]
 
-        pair = {q: psum.tile([P, 2, QW], F32, name=f"pair{q}", tag=f"bank{(0, 1, 4)[q]}") for q in range(last)}
-        lone = [psum.tile([P, QW], F32, name=f"lone{b}", tag=f"bank{6 + b}") for b in range(2)]
-
-        def sums(q, b):
-            return pair[q][:, b, :] if q < last else lone[b][:]
-
-        def finish(q):
-            quant_z(q)
+        def second(q, a):
+            cols = slice(q * QW, (q + 1) * QW)
+            shared = q < LAST
             for b in range(2):
-                second(sums(q, b), b, q, 1)
-            if q < last:
-                res = keep.tile([P, 2, QW], F32, name=f"res{q}")
-                nc.scalar.activation(res[:], pair[q][:], ACT.Relu)
-                nc.sync.dma_start(out=outv[:, :, q * QW : (q + 1) * QW], in_=res[:])
-            else:
-                for b in range(2):
-                    res = keep.tile([P, QW], F32, name=f"res{q}{b}")
-                    nc.vector.tensor_scalar_max(res[:], lone[b][:], 0.0)
-                    (nc.sync, nc.scalar)[b].dma_start(out=outv[:, b, q * QW : (q + 1) * QW], in_=res[:])
-
-        def interleave(q):
-            z4[q] = keep.tile([P, QW, PACK], BF16, name=f"z4_{q}", tag=f"z4_{q}", align_bytes=64)
-            dst = z4[q][:].rearrange("p (c i) t -> p c t i", i=4)
-            src = zp[:, q, :, :].rearrange("p t (c i) -> p c t i", i=4)
-            if q < last:
-                nc.scalar.copy(dst, src)
-            else:
-                nc.vector.tensor_copy(dst, src)
-
-        t = PACK - 1
-        free = keep.tile([P, LISTS, 2, QW], BF16, name="free", tag="got12", align_bytes=64)
-        flat = lambda ap: ap.rearrange("p a v -> p (a v)")
-
-        def gather_q(d, q0, q1, dst):
-            gather(t, d, dst, q0 * QW, q1 * QW)
+                nc.tensor.matmul_mx(
+                    out=pair[q][:, b, :] if shared else lone[b][:],
+                    lhsT=w_w[a][:, 2 * P * b : 2 * P * (b + 1)].bitcast(FP4X4),
+                    lhsT_scale=w_sc[:, a, P * b : P * (b + 1)],
+                    rhs=(hc, zc)[a][:, cols].bitcast(FP8X4),
+                    rhs_scale=(hsc, zsc)[a][:, cols],
+                    start=(a == 0 and (b == 0 or not shared)),
+                    stop=(a == 1 and (b == 1 or not shared)),
+                )
 
         def quant_h(s):
-            hc[s] = keep.tile([P, TH], U32, name=f"hc{s}", tag=("hc0", "raw11")[s], align_bytes=64)
+            cols = slice(s * TH, (s + 1) * TH)
             nc.vector.quantize_mx(
-                out=hc[s][:].bitcast(FP8X4),
-                scales=hsc[:, s * TH : (s + 1) * TH],
-                in_=h4[:, s * TH : (s + 1) * TH, :].rearrange("p v t -> p (v t)"),
+                out=hc[:, cols].bitcast(FP8X4), scales=hsc[:, cols], in_=h4[:, cols, :].rearrange("p v t -> p (v t)")
             )
             for q in (2 * s, 2 * s + 1):
-                for b in range(2):
-                    second(sums(q, b), b, q, 0)
+                second(q, 0)
 
-        largest(zt[2][:], two2[:], work[:, 2, :])
-        move_z(2)
-        for d in range(LISTS):
-            gather_q(d, 0, 2, flat(free[:, d, :, :]))
-        rest = keep.tile([P, 7, QW], BF16, name="rest", tag="raw11", align_bytes=64)
-        largest(rest[:, 5:7, :], free[:, 0, :, :], free[:, 1, :, :])
-        gather_q(0, 2, 4, flat(rest[:, 0:2, :]))
-        largest(zp[:, 0:2, t, :], rest[:, 5:7, :], free[:, 2, :, :])
-        interleave(0)
-        interleave(1)
-        quant_h(0)
-        gather_q(1, 2, 4, flat(rest[:, 2:4, :]))
-        gather_q(2, 2, 3, rest[:, 4, :])
-        spent = zp[:, 0, :, :]
-        finish(0)
-        largest(spent[:, 0:2, :], rest[:, 0:2, :], rest[:, 2:4, :])
-        gather_q(2, 3, 4, spent[:, 2, :])
-        largest(zp[:, 2, t, :], spent[:, 0, :], rest[:, 4, :])
-        interleave(2)
-        quant_h(1)
-        largest(zp[:, 3, t, :], spent[:, 1, :], spent[:, 2, :])
-        finish(1)
-        interleave(3)
-        finish(2)
-        finish(3)
+        def finish(q, src):
+            cols = slice(q * QW, (q + 1) * QW)
+            nc.vector.quantize_mx(out=zc[:, cols].bitcast(FP8X4), scales=zsc[:, cols], in_=src)
+            second(q, 1)
+            if q < LAST:
+                res = tile([P, 2, QW], F32, f"res{q}")
+                nc.scalar.activation(res[:], pair[q][:], ACT.Relu)
+                nc.sync.dma_start(out=outv[:, :, cols], in_=res[:])
+            else:
+                for b in range(2):
+                    res = tile([P, QW], F32, f"res{q}{b}")
+                    if b == 0:
+                        nc.scalar.activation(res[:], lone[b][:], ACT.Relu)
+                    else:
+                        nc.vector.tensor_scalar_max(res[:], lone[b][:], 0.0)
+                    (nc.scalar, nc.sync)[b].dma_start(out=outv[:, b, cols], in_=res[:])
+
+        z4 = {}
+
+        def interleave(q):
+            z4[q] = tile([P, QW, PACK], BF16, f"z4_{q}")
+            nc.scalar.copy(
+                z4[q][:].rearrange("p (c i) t -> p c t i", i=4), zp[:, q, :, :].rearrange("p t (c i) -> p c t i", i=4)
+            )
+
+        flat = lambda ap: ap.rearrange("p a v -> p (a v)")
+        ab = tile([P, 2, PACK * QW], BF16, "ab", "raw12")
+        for d in range(2):
+            gather_last(d, ab[:, d, :])
+        for s in range(2):
+            quant_h(s)
+        m_last = tile([P, PACK * QW], BF16, "m_last")
+        largest(m_last[:], ab[:, 0, :], ab[:, 1, :])
+        for q in range(LAST):
+            interleave(q)
+        finish(0, flat(z4[0][:]))
+        c_last = flat(zp[:, 0, :, :])
+        gather_last(2, c_last)
+        finish(1, flat(z4[1][:]))
+        z_last = flat(zp[:, 2, :, :])
+        runs = lambda ap: ap.rearrange("p (t c i) -> p c t i", t=PACK, i=RUN)
+        for s in range(2):
+            cols = slice(s * TH, (s + 1) * TH)
+            largest(
+                z_last[:, cols].rearrange("p (c i t) -> p c t i", t=PACK, i=RUN), runs(m_last[:, cols]), runs(c_last[:, cols])
+            )
+        finish(2, flat(z4[2][:]))
+        finish(3, z_last)

@@ -197,16 +197,16 @@ def tile_picked_wsagecat_maxrelu_l_kernel(
         quant_w1(0, 2)
         first(2, 0)
         first(3, 0)
-        a1 = tile([P, TA], BF16, "a1", "raw02")
-        gather(1, 0, a1[:])
+        first_got = tile([P, LAST, TA], BF16, "first_got", "raw02")
+        gather(1, 0, first_got[:, 0, :])
         cast(1, 2)
         quant_w1(1, 2)
         first(2, 1)
         first(3, 1)
-        bc1 = tile([P, 2, TA], BF16, "bc1", "raw12")
-        b1, c1 = bc1[:, 0, :], bc1[:, 1, :]
-        gather(1, 1, b1)
-        gather(1, 2, c1)
+        rest_got = tile([P, 2, LAST, TA], BF16, "rest_got", "raw12")
+        got = (first_got[:], rest_got[:, 0, :, :], rest_got[:, 1, :, :])
+        for d in range(1, LISTS):
+            gather(1, d, got[d][:, 0, :])
         window(2)
         move_h(0)
         move_h(1)
@@ -217,36 +217,27 @@ def tile_picked_wsagecat_maxrelu_l_kernel(
         lead(ahead0, [d[:] for d in early], a0, b0)
         m0 = tile([P, TA], BF16, "m0")
         top(m0, ahead0, b0)
-        ahead2 = tile([P, TA], F32, "ahead2")
-        diff2 = tile([P, TA], F32, "diff2")
-        lead(ahead2, [diff2[:, cols] for cols in halves()], m0, c0)
         ahead1 = tile([P, TA], F32, "ahead1")
-        diff1 = tile([P, TA], F32, "diff1", "raw11")
-        lead(ahead1, [diff1[:, cols] for cols in halves()], a1, b1)
+        diff1 = tile([P, TA], F32, "diff1")
+        lead(ahead1, [diff1[:, cols] for cols in halves()], m0, c0)
         z0 = tile([P, TA], BF16, "z0")
-        top(z0, ahead2, c0)
-        m1 = tile([P, TA], BF16, "m1", "diff2")
-        top(m1, ahead1, b1)
-        a23 = tile([P, 2, TA], BF16, "a23")
-        b23 = tile([P, 2, TA], BF16, "b23")
-        gather(2, 0, a23[:, 0, :])
-        gather(2, 1, b23[:, 0, :])
-        window(3, "wq12")
+        top(z0, ahead1, c0)
+        for d in range(LISTS):
+            gather(2, d, got[d][:, 1, :])
+        window(3)
         move_h(3)
         move_z(0, z0)
-        c23 = tile([P, 2, TA], BF16, "c23")
-        gather(2, 2, c23[:, 0, :])
-        for d, dst in enumerate((a23, b23, c23)):
-            gather(3, d, dst[:, 1, :])
-        m23 = tile([P, 2, TA], BF16, "m23")
-        largest(m23[:], a23[:], b23[:])
-        z1 = tile([P, TA], BF16, "z1")
-        largest(z1[:], m1[:], c1)
-        z23 = tile([P, 2, TA], BF16, "z23", "ahead1")
-        largest(z23[:], m23[:], c23[:])
-        move_z(1, z1)
-        for k in range(2, PACK):
-            move_z(k, z23[:, k - 2, :])
+        for d in range(LISTS):
+            gather(3, d, got[d][:, 2, :])
+        two = tile([P, LAST, TA], BF16, "two", "ahead1")
+        zt = tile([P, LAST, TA], BF16, "zt")
+        parts = (slice(0, 2), slice(2, 3))
+        for part in parts:
+            largest(two[:, part, :], got[0][:, part, :], got[1][:, part, :])
+        for part in parts:
+            largest(zt[:, part, :], two[:, part, :], got[2][:, part, :])
+        for k in range(1, PACK):
+            move_z(k, zt[:, k - 1, :])
 
         h4 = tile([P, T, PACK], BF16, "h4")
         for q in range(NQ):
@@ -311,7 +302,7 @@ def tile_picked_wsagecat_maxrelu_l_kernel(
             )
 
         flat = lambda ap: ap.rearrange("p a v -> p (a v)")
-        ab = tile([P, 2, PACK * QW], BF16, "ab", "raw12")
+        ab = tile([P, 2, PACK * QW], BF16, "ab", "raw01")
         for d in range(2):
             gather_last(d, ab[:, d, :])
         for s in range(2):

@@ -144,10 +144,13 @@ def tile_picked_wsagecat_maxrelu_l_kernel(
         def gather(k, d, dst):
             nc.vector.tensor_copy(dst, hh[k][:].indirect(lists[d][:, 0 : TA // 16]))
 
+        def gather_lane(d, t, dst):
+            nc.vector.tensor_copy(dst, hs[:, t, :].indirect(lists[d][:, TA // 16 : T // 16]))
+
         def gather_last(d, dst):
             view = dst.rearrange("p (s t v) -> p s t v", s=2, t=PACK)
             for t in range(PACK):
-                nc.vector.tensor_copy(view[:, :, t, :], hs[:, t, :].indirect(lists[d][:, TA // 16 : T // 16]))
+                gather_lane(d, t, view[:, :, t, :])
 
         def largest(dst, a, b):
             nc.vector.tensor_tensor(dst, a, b, ALU.max)
@@ -245,7 +248,7 @@ def tile_picked_wsagecat_maxrelu_l_kernel(
             nc.scalar.copy(
                 h4[:, cols, :].rearrange("p (c i) t -> p c t i", i=4), hs[:, :, cols].rearrange("p t (c i) -> p c t i", i=4)
             )
-        hc = tile([P, T], U32, "hc")
+        hc = {}
         hsc = tile([P, T], U8, "hsc")
         zc = tile([P, T], U32, "zc")
         zsc = tile([P, T], U8, "zsc")
@@ -262,18 +265,20 @@ def tile_picked_wsagecat_maxrelu_l_kernel(
                     out=pair[q][:, b, :] if shared else lone[b][:],
                     lhsT=w_w[a][:, 2 * P * b : 2 * P * (b + 1)].bitcast(FP4X4),
                     lhsT_scale=w_sc[:, a, P * b : P * (b + 1)],
-                    rhs=(hc, zc)[a][:, cols].bitcast(FP8X4),
+                    rhs=(hc[q], zc[:, cols])[a].bitcast(FP8X4),
                     rhs_scale=(hsc, zsc)[a][:, cols],
                     start=(a == 0 and (b == 0 or not shared)),
                     stop=(a == 1 and (b == 1 or not shared)),
                 )
 
-        def quant_h(s):
-            cols = slice(s * TH, (s + 1) * TH)
+        def quant_h(q0, q1, on=None):
+            cols = slice(q0 * QW, q1 * QW)
+            codes = tile([P, (q1 - q0) * QW], U32, f"hc{q0}", on)
             nc.vector.quantize_mx(
-                out=hc[:, cols].bitcast(FP8X4), scales=hsc[:, cols], in_=h4[:, cols, :].rearrange("p v t -> p (v t)")
+                out=codes[:].bitcast(FP8X4), scales=hsc[:, cols], in_=h4[:, cols, :].rearrange("p v t -> p (v t)")
             )
-            for q in (2 * s, 2 * s + 1):
+            for q in range(q0, q1):
+                hc[q] = codes[:, (q - q0) * QW : (q - q0 + 1) * QW]
                 second(q, 0)
 
         def finish(q, src):
@@ -305,22 +310,24 @@ def tile_picked_wsagecat_maxrelu_l_kernel(
         ab = tile([P, 2, PACK * QW], BF16, "ab", "raw01")
         for d in range(2):
             gather_last(d, ab[:, d, :])
-        for s in range(2):
-            quant_h(s)
-        m_last = tile([P, PACK * QW], BF16, "m_last")
-        largest(m_last[:], ab[:, 0, :], ab[:, 1, :])
+        quant_h(0, 2)
+        quant_h(2, 3)
+        m_last = tile([P, 2, PACK, QW // 2], BF16, "m_last")
+        largest(m_last[:].rearrange("p s t v -> p (s t v)"), ab[:, 0, :], ab[:, 1, :])
         for q in range(LAST):
             interleave(q)
         finish(0, flat(z4[0][:]))
         c_last = flat(zp[:, 0, :, :])
         gather_last(2, c_last)
-        finish(1, flat(z4[1][:]))
+        for q in range(1, LAST):
+            finish(q, flat(z4[q][:]))
         z_last = flat(zp[:, 2, :, :])
-        runs = lambda ap: ap.rearrange("p (t c i) -> p c t i", t=PACK, i=RUN)
+        runs = lambda ap: ap.rearrange("p t (c i) -> p c t i", i=RUN)
         for s in range(2):
-            cols = slice(s * TH, (s + 1) * TH)
             largest(
-                z_last[:, cols].rearrange("p (c i t) -> p c t i", t=PACK, i=RUN), runs(m_last[:, cols]), runs(c_last[:, cols])
+                z_last[:, s * TH : (s + 1) * TH].rearrange("p (c i t) -> p c t i", t=PACK, i=RUN),
+                runs(m_last[:, s, :, :]),
+                runs(c_last.rearrange("p (s t v) -> p s t v", s=2, t=PACK)[:, s, :, :]),
             )
-        finish(2, flat(z4[2][:]))
-        finish(3, z_last)
+        quant_h(LAST, NQ, "z4_2")
+        finish(LAST, z_last)

@@ -19,23 +19,12 @@ ALU = mybir.AluOpType
 P = 128
 PACK = 4
 PASSES = K // (P * PACK)
-WIN = 1024
-QW = 128
-NQ = T // QW
-LAST = NQ - 1
-TA = LAST * QW
-LISTS = 3
-WORDS = (32, 32, 64)
+TH = T // 2
+TQ = T // 4
+ORDER = (3, 1, 2, 0)
+PIECES = ((0, TH), (TH, TH + TQ), (TH + TQ, T))
+CAST_V = 88
 RUN = 8
-HALVES = ((0, 256), (256, 512))
-CUTS = (((0, 256), (256, 384), (384, 512)), HALVES, HALVES, ((0, 512),))
-BANKS = ((0, 4, 7), (1, 5), (2, 6), (3,))
-
-
-def runs_of(k):
-    if k < 2:
-        return [(32 * t, 32, t, 32 * k) for t in range(PACK)]
-    return [(64 * u, 64, 2 * (k - 2) + u, 64) for u in range(2)]
 
 
 def tile_picked_wsagecat_maxrelu_l_kernel(
@@ -49,285 +38,200 @@ def tile_picked_wsagecat_maxrelu_l_kernel(
         def tile(shape, dtype, name, on=None):
             return keep.tile(shape, dtype, name=name, tag=on or name, align_bytes=64)
 
-        lists = [keep.tile([P, T // 16], U16, name=f"list{d}") for d in range(LISTS)]
+        def bank(shape, name, b):
+            return psum.tile(shape, F32, name=name, tag=f"bank{b}")
+
+        lists = [keep.tile([P, T // 16], U16, name=f"list{d}") for d in range(3)]
         x_sc = tile([P, PASSES, T], U8, "x_sc")
         w_sc = tile([P, 2, N], U8, "w_sc")
 
-        raw = {}
         w1v = w1.rearrange("(z p j) c -> z p j c", z=PASSES, j=PACK)
-        starts = [sum(WORDS[:c]) for c in range(len(WORDS))]
-
-        def load_w1(z, c):
-            cols = slice(PACK * starts[c], PACK * (starts[c] + WORDS[c]))
-            raw[z, c] = tile([P, PACK, PACK * WORDS[c]], F32, f"raw{z}{c}")
-            nc.sync.dma_start(out=raw[z, c][:], in_=w1v[z, :, :, cols])
-
+        raw = [tile([P, PACK, H], F32, f"raw{z}") for z in range(PASSES)]
         xs_v = x_scales.bitcast(I32).rearrange("z (q r) c -> r q z c", r=PACK)
         for r in range(PACK):
             nc.sync.dma_start(out=x_sc[r:P:32, :, :].bitcast(I32), in_=xs_v[r])
             if r == 0:
-                load_w1(0, 0)
-        load_w1(1, 0)
-        x_w = tile([P, PASSES, T], U32, "x_w")
+                nc.sync.dma_start(out=raw[0][:], in_=w1v[0])
+        nc.sync.dma_start(out=raw[1][:], in_=w1v[1])
         xw_v = x_words.rearrange("z p c r -> p z (c r)").bitcast(I32)
-        for c0, c1 in HALVES:
-            nc.sync.dma_start(out=x_w[:, :, c0:c1].bitcast(I32), in_=xw_v[:, :, c0:c1])
-        load_w1(0, 1)
-        nc.sync.dma_start(lists[0][:], pos1)
-        load_w1(1, 1)
-        load_w1(0, 2)
-        nc.sync.dma_start(lists[1][:], pos2)
-        nc.sync.dma_start(lists[2][:], pos3)
-        load_w1(1, 2)
+        x_w = []
+        for s in range(2):
+            x_w.append(tile([P, PASSES, TH], U32, f"x_w{s}"))
+            nc.sync.dma_start(out=x_w[s][:].bitcast(I32), in_=xw_v[:, :, s * TH : (s + 1) * TH])
+        for d, pos in enumerate((pos1, pos2, pos3)):
+            nc.sync.dma_start(lists[d][:], pos)
         w_w = []
+        for a, words in enumerate((w2_words, w3_words)):
+            w_w.append(tile([P, 2 * N], U8, f"w_w{a}"))
+            nc.sync.dma_start(out=w_w[a][:].bitcast(I32), in_=words[0].bitcast(I32))
         for a, scales in enumerate((w2_scales, w3_scales)):
             sv = scales[0].bitcast(I32).rearrange("(q r) c -> r q c", r=PACK)
             for r in range(PACK):
                 nc.sync.dma_start(out=w_sc[r:P:32, a, :].bitcast(I32), in_=sv[r])
-        for a, words in enumerate((w2_words, w3_words)):
-            w_w.append(tile([P, 2 * N], U8, f"w_w{a}"))
-            nc.sync.dma_start(out=w_w[a][:].bitcast(I32), in_=words[0].bitcast(I32))
 
-        wq = {(z, c): tile([P, PACK * WORDS[c], PACK], BF16, f"wq{z}{c}") for z in range(PASSES) for c in range(len(WORDS))}
-        wc = [tile([P, H], U32, f"wc{z}") for z in range(PASSES)]
-        ws = [tile([P, H], U8, f"ws{z}") for z in range(PASSES)]
+        wq = [tile([P, H, PACK], BF16, f"wq{z}") for z in range(PASSES)]
+        wc, ws = {}, {}
 
-        def cast(z, c):
-            src = raw[z, c][:].rearrange("p j (m t) -> p m j t", t=PACK)
-            dst = wq[z, c][:].rearrange("p (t m) j -> p m j t", t=PACK)
-            if c == 0:
-                nc.vector.tensor_copy(dst[:, :, :, 0:2], src[:, :, :, 0:2])
-                nc.scalar.activation(dst[:, :, :, 2:4], src[:, :, :, 2:4], ACT.Copy)
-            elif (z, c) == (0, 1):
+        def cast(z):
+            src = raw[z][:].rearrange("p j (m t) -> p m j t", t=PACK)
+            dst = wq[z][:].rearrange("p (t m) j -> p m j t", t=PACK)
+            nc.vector.tensor_copy(dst[:, 0:CAST_V], src[:, 0:CAST_V])
+            nc.scalar.activation(dst[:, CAST_V:P], src[:, CAST_V:P], ACT.Copy)
+
+        def quantise(codes, scales, src):
+            nc.vector.quantize_mx(out=codes.bitcast(FP8X4), scales=scales, in_=src.rearrange("p m j -> p (m j)"))
+
+        cast(0)
+        wc0 = tile([P, H], U32, "wc0")
+        ws0 = tile([P, H], U8, "ws0")
+        quantise(wc0[:], ws0[:], wq[0][:])
+        cast(1)
+        for t in ORDER:
+            wc[0, t], ws[0, t] = wc0[:, t * P : (t + 1) * P], ws0[:, t * P : (t + 1) * P]
+            wc[1, t] = tile([P, P], U32, f"wc1{t}")[:]
+            ws[1, t] = tile([P, P], U8, f"ws1{t}")[:]
+            quantise(wc[1, t], ws[1, t], wq[1][:, t * P : (t + 1) * P, :])
+
+        def first(t, dst, c0, c1, z, start, stop):
+            s = c0 // TH
+            nc.tensor.matmul_mx(
+                out=dst,
+                lhsT=wc[z, t].bitcast(FP8X4),
+                lhsT_scale=ws[z, t],
+                rhs=x_w[s][:, z, c0 - s * TH : c1 - s * TH].bitcast(FP8X4),
+                rhs_scale=x_sc[:, z, c0:c1],
+                start=start,
+                stop=stop,
+            )
+
+        lead = []
+        for b, (c0, c1) in enumerate(PIECES):
+            lead.append(bank([P, c1 - c0], f"lead{b}", b))
+            for z in range(PASSES):
+                first(ORDER[0], lead[b][:], c0, c1, z, z == 0, z == 1)
+        hb = {}
+        for n, t in enumerate(ORDER[1:]):
+            hb[t] = bank([P, T], f"hb{t}", 3 + n)
+            for s in range(2):
+                for z in range(PASSES):
+                    first(t, hb[t][:, s * TH : (s + 1) * TH], s * TH, (s + 1) * TH, z, z == 0, z == 1)
+
+        win = {t: tile([P, 2 * T], F32, f"win{t}") for t in ORDER[:2]}
+        hs = tile([P, PACK * T], F32, "hs")
+        lane = lambda t: hs[:, t * T : (t + 1) * T]
+        window = {3: win[3][:], 1: win[1][:], 2: hs[:, 2 * T : 4 * T], 0: hs[:]}
+
+        def gather(eng, t, d, dst, c0, c1):
+            src = window[t].indirect(lists[d][:, c0 // 16 : c1 // 16])
+            if eng == "v":
                 nc.vector.tensor_copy(dst, src)
             else:
                 nc.scalar.activation(dst, src, ACT.Copy)
 
-        def quant_w1(z, c):
-            cols = slice(PACK * starts[c], PACK * (starts[c] + WORDS[c]))
-            nc.vector.quantize_mx(
-                out=wc[z][:, cols].bitcast(FP8X4),
-                scales=ws[z][:, cols],
-                in_=wq[z, c][:].rearrange("p m j -> p (m j)"),
-            )
-
-        TH = T // 2
-        hb = {}
-        for k in range(PACK):
-            for s, (c0, c1) in enumerate(CUTS[k]):
-                hb[k, s] = psum.tile([P, c1 - c0], F32, name=f"hb{k}{s}", tag=f"bank{BANKS[k][s]}")
-
-        def first(k, z, only=None):
-            for s, (c0, c1) in enumerate(CUTS[k]):
-                if only is not None and s != only:
-                    continue
-                nc.tensor.matmul_mx(
-                    out=hb[k, s][:],
-                    lhsT=wc[z][:, k * P : (k + 1) * P].bitcast(FP8X4),
-                    lhsT_scale=ws[z][:, k * P : (k + 1) * P],
-                    rhs=x_w[:, z, c0:c1].bitcast(FP8X4),
-                    rhs_scale=x_sc[:, z, c0:c1],
-                    start=(z == 0),
-                    stop=(z == PASSES - 1),
-                )
-
-        hh = {}
-
-        def window(k, on=None):
-            hh[k] = tile([P, WIN], F32, f"hh{k}", on)
-            for s, (c0, c1) in enumerate(CUTS[k]):
-                nc.scalar.activation(hh[k][:, c0:c1], hb[k, s][:], ACT.Relu)
-
-        hs = tile([P, PACK, T], F32, "hs")
-        zp = tile([P, LAST, PACK, QW], BF16, "zp")
-
-        def gather(k, d, dst):
-            nc.vector.tensor_copy(dst, hh[k][:].indirect(lists[d][:, 0 : TA // 16]))
-
-        def gather_lane(d, t, dst):
-            nc.vector.tensor_copy(dst, hs[:, t, :].indirect(lists[d][:, TA // 16 : T // 16]))
-
-        def gather_last(d, dst):
-            view = dst.rearrange("p (s t v) -> p s t v", s=2, t=PACK)
-            for t in range(PACK):
-                gather_lane(d, t, view[:, :, t, :])
+        def relu(eng, dst, src):
+            if eng == "v":
+                nc.vector.tensor_scalar_max(dst, src, 0.0)
+            else:
+                nc.scalar.activation(dst, src, ACT.Relu)
 
         def largest(dst, a, b):
             nc.vector.tensor_tensor(dst, a, b, ALU.max)
 
-        def halves():
-            return [slice(s * TA // 2, (s + 1) * TA // 2) for s in range(2)]
+        for eng, b in (("s", 0), ("s", 1), ("v", 2)):
+            c0, c1 = PIECES[b]
+            relu(eng, win[3][:, c0:c1], lead[b][:])
+        nc.sync.dma_start(out=lane(3), in_=win[3][:, 0:T])
 
-        def lead(ahead, diffs, a, b):
-            for diff, cols in zip(diffs, halves()):
-                nc.gpsimd.tensor_tensor(diff, a[:, cols], b[:, cols], ALU.subtract)
-                nc.scalar.activation(ahead[:, cols], diff, ACT.Relu)
+        third = tile([P, 2, PACK, TH], BF16, "third")
+        two = tile([P, 2, PACK, TH], BF16, "two")
+        halves = lambda ap: ap.rearrange("p (h v) -> p h v", h=2)
 
-        def top(dst, ahead, b):
-            for cols in halves():
-                nc.gpsimd.tensor_tensor(dst[:, cols], ahead[:, cols], b[:, cols], ALU.add)
-
-        def move_h(k):
-            for p0, count, lane, g0 in runs_of(k):
-                nc.sync.dma_start(out=hs[g0 : g0 + count, lane, :], in_=hh[k][p0 : p0 + count, 0:T])
-
-        def move_z(k, src):
-            for p0, count, lane, g0 in runs_of(k):
-                nc.sync.dma_start(
-                    out=zp[g0 : g0 + count, :, lane, :], in_=src[p0 : p0 + count, :].rearrange("p (q v) -> p q v", q=LAST)
-                )
-
-        for z in range(PASSES):
-            cast(z, 0)
-            quant_w1(z, 0)
-        for s in range(len(CUTS[0])):
-            for z in range(PASSES):
-                first(0, z, s)
-        window(0)
-
-        a0 = tile([P, TA], BF16, "a0")
-        gather(0, 0, a0[:])
-        for z in range(PASSES):
-            cast(z, 1)
-            quant_w1(z, 1)
-            first(1, z)
-        window(1)
-        b0 = tile([P, TA], BF16, "b0", "raw11")
-        gather(0, 1, b0[:])
-        c0 = tile([P, TA], BF16, "c0", "raw01")
-        gather(0, 2, c0[:])
-        cast(0, 2)
-        quant_w1(0, 2)
-        first(2, 0)
-        first(3, 0)
-        first_got = tile([P, LAST, TA], BF16, "first_got", "raw02")
-        gather(1, 0, first_got[:, 0, :])
-        cast(1, 2)
-        quant_w1(1, 2)
-        first(2, 1)
-        first(3, 1)
-        rest_got = tile([P, 2, LAST, TA], BF16, "rest_got", "raw12")
-        got = (first_got[:], rest_got[:, 0, :, :], rest_got[:, 1, :, :])
-        for d in range(1, LISTS):
-            gather(1, d, got[d][:, 0, :])
-        window(2)
-        move_h(0)
-        move_h(1)
-        move_h(2)
-
-        ahead0 = tile([P, TA], F32, "ahead0", "wq12")
-        early = [tile([P, TA // 2], F32, "diff00"), tile([P, TA // 2], F32, "diff01", "wq02")]
-        lead(ahead0, [d[:] for d in early], a0, b0)
-        m0 = tile([P, TA], BF16, "m0")
-        top(m0, ahead0, b0)
-        ahead1 = tile([P, TA], F32, "ahead1")
-        diff1 = tile([P, TA], F32, "diff1")
-        lead(ahead1, [diff1[:, cols] for cols in halves()], m0, c0)
-        z0 = tile([P, TA], BF16, "z0")
-        top(z0, ahead1, c0)
-        for d in range(LISTS):
-            gather(2, d, got[d][:, 1, :])
-        window(3)
-        move_h(3)
-        move_z(0, z0)
-        for d in range(LISTS):
-            gather(3, d, got[d][:, 2, :])
-        two = tile([P, LAST, TA], BF16, "two", "ahead1")
-        zt = tile([P, LAST, TA], BF16, "zt")
-        parts = (slice(0, 2), slice(2, 3))
-        for part in parts:
-            largest(two[:, part, :], got[0][:, part, :], got[1][:, part, :])
-        for part in parts:
-            largest(zt[:, part, :], two[:, part, :], got[2][:, part, :])
-        for k in range(1, PACK):
-            move_z(k, zt[:, k - 1, :])
+        a3 = tile([P, T], BF16, "a3")
+        b3 = tile([P, T], BF16, "b3", "wc11")
+        gather("s", 3, 0, a3[:], 0, T)
+        gather("v", 3, 2, third[:, :, 3, :], 0, T)
+        relu("s", win[1][:, 0:T], hb[1][:])
+        nc.sync.dma_start(out=lane(1), in_=win[1][:, 0:T])
+        gather("v", 3, 1, b3[:, 0:TH], 0, TH)
+        gather("s", 3, 1, b3[:, TH:T], TH, T)
+        gather("v", 1, 2, third[:, :, 1, :], 0, T)
+        relu("s", lane(2), hb[2][:])
+        relu("s", lane(0), hb[0][:])
+        largest(two[:, :, 3, :], halves(a3[:]), halves(b3[:]))
 
         h4 = tile([P, T, PACK], BF16, "h4")
-        for q in range(NQ):
-            cols = slice(q * QW, (q + 1) * QW)
-            nc.scalar.copy(
-                h4[:, cols, :].rearrange("p (c i) t -> p c t i", i=4), hs[:, :, cols].rearrange("p t (c i) -> p c t i", i=4)
-            )
-        hc = {}
+        hv = hs[:].rearrange("p (t v) -> p v t", t=PACK)
+        for c0, c1 in PIECES:
+            nc.gpsimd.tensor_scalar(h4[:, c0:c1, :], hv[:, c0:c1, :], 1.0, 0.0, ALU.mult, ALU.add)
+
+        a12 = tile([P, 2, 2, TH], BF16, "a12", "wc10")
+        b12 = tile([P, 2, 2, TH], BF16, "b12", "ws10")
+        gather("v", 2, 2, third[:, :, 2, :], 0, T)
+        for d, dst in enumerate((a12, b12)):
+            gather("v", 2, d, dst[:, :, 1, :], 0, T)
+            for s in range(2):
+                gather("s", 1, d, dst[:, s, 0, :], s * TH, (s + 1) * TH)
+        largest(two[:, :, 1:3, :], a12[:], b12[:])
+
+        a0 = tile([P, T], BF16, "a0")
+        b0 = tile([P, T], BF16, "b0")
+        for c0, c1 in PIECES:
+            s = c0 // TH
+            gather("s", 0, 0, a0[:, c0:c1], c0, c1)
+            gather("s", 0, 1, b0[:, c0:c1], c0, c1)
+            gather("s", 0, 2, third[:, s, 0, c0 - s * TH : c1 - s * TH], c0, c1)
+
+        hc = tile([P, T], U32, "hc")
         hsc = tile([P, T], U8, "hsc")
         zc = tile([P, T], U32, "zc")
         zsc = tile([P, T], U8, "zsc")
+        z4 = tile([P, T, PACK], BF16, "z4")
         outv = out.rearrange("(b p) v -> p b v", p=P)
-
-        pair = {q: psum.tile([P, 2, QW], F32, name=f"pair{q}", tag=f"bank{(0, 1, 4)[q]}") for q in range(LAST)}
-        lone = [psum.tile([P, QW], F32, name=f"lone{b}", tag=f"bank{(5, 7)[b]}") for b in range(2)]
+        last = len(PIECES) - 1
+        acc = {}
+        for q, (c0, c1) in enumerate(PIECES[:last]):
+            both = bank([P, 2, c1 - c0], f"both{q}", 6 + q)
+            acc[q] = both
+        lone = [bank([P, TQ], f"lone{b}", b) for b in range(2)]
 
         def second(q, a):
-            cols = slice(q * QW, (q + 1) * QW)
-            shared = q < LAST
+            c0, c1 = PIECES[q]
+            shared = q < last
             for b in range(2):
                 nc.tensor.matmul_mx(
-                    out=pair[q][:, b, :] if shared else lone[b][:],
+                    out=acc[q][:, b, :] if shared else lone[b][:],
                     lhsT=w_w[a][:, 2 * P * b : 2 * P * (b + 1)].bitcast(FP4X4),
                     lhsT_scale=w_sc[:, a, P * b : P * (b + 1)],
-                    rhs=(hc[q], zc[:, cols])[a].bitcast(FP8X4),
-                    rhs_scale=(hsc, zsc)[a][:, cols],
+                    rhs=(hc, zc)[a][:, c0:c1].bitcast(FP8X4),
+                    rhs_scale=(hsc, zsc)[a][:, c0:c1],
                     start=(a == 0 and (b == 0 or not shared)),
                     stop=(a == 1 and (b == 1 or not shared)),
                 )
 
-        def quant_h(q0, q1, on=None):
-            cols = slice(q0 * QW, q1 * QW)
-            codes = tile([P, (q1 - q0) * QW], U32, f"hc{q0}", on)
-            nc.vector.quantize_mx(
-                out=codes[:].bitcast(FP8X4), scales=hsc[:, cols], in_=h4[:, cols, :].rearrange("p v t -> p (v t)")
-            )
-            for q in range(q0, q1):
-                hc[q] = codes[:, (q - q0) * QW : (q - q0 + 1) * QW]
-                second(q, 0)
-
-        def finish(q, src):
-            cols = slice(q * QW, (q + 1) * QW)
-            nc.vector.quantize_mx(out=zc[:, cols].bitcast(FP8X4), scales=zsc[:, cols], in_=src)
-            second(q, 1)
-            if q < LAST:
-                res = tile([P, 2, QW], F32, f"res{q}")
-                nc.scalar.activation(res[:], pair[q][:], ACT.Relu)
-                nc.sync.dma_start(out=outv[:, :, cols], in_=res[:])
-            else:
-                for b in range(2):
-                    res = tile([P, QW], F32, f"res{q}{b}")
-                    if b == 0:
-                        nc.scalar.activation(res[:], lone[b][:], ACT.Relu)
-                    else:
-                        nc.vector.tensor_scalar_max(res[:], lone[b][:], 0.0)
-                    (nc.scalar, nc.sync)[b].dma_start(out=outv[:, b, cols], in_=res[:])
-
-        z4 = {}
-
-        def interleave(q):
-            z4[q] = tile([P, QW, PACK], BF16, f"z4_{q}")
-            nc.scalar.copy(
-                z4[q][:].rearrange("p (c i) t -> p c t i", i=4), zp[:, q, :, :].rearrange("p t (c i) -> p c t i", i=4)
-            )
-
-        flat = lambda ap: ap.rearrange("p a v -> p (a v)")
-        ab = tile([P, 2, PACK * QW], BF16, "ab", "raw01")
-        for d in range(2):
-            gather_last(d, ab[:, d, :])
-        quant_h(0, 2)
-        quant_h(2, 3)
-        m_last = tile([P, 2, PACK, QW // 2], BF16, "m_last")
-        largest(m_last[:].rearrange("p s t v -> p (s t v)"), ab[:, 0, :], ab[:, 1, :])
-        for q in range(LAST):
-            interleave(q)
-        finish(0, flat(z4[0][:]))
-        c_last = flat(zp[:, 0, :, :])
-        gather_last(2, c_last)
-        for q in range(1, LAST):
-            finish(q, flat(z4[q][:]))
-        z_last = flat(zp[:, 2, :, :])
-        runs = lambda ap: ap.rearrange("p t (c i) -> p c t i", i=RUN)
         for s in range(2):
+            cols = slice(s * TH, (s + 1) * TH)
+            quantise(hc[:, cols], hsc[:, cols], h4[:, cols, :])
+        for q in range(len(PIECES)):
+            second(q, 0)
+
+        runs = lambda ap: ap.rearrange("p t (c i) -> p c t i", i=RUN)
+        for q, (c0, c1) in enumerate(PIECES):
+            s = c0 // TH
+            part = slice(c0 - s * TH, c1 - s * TH)
+            largest(two[:, s, 0, part], a0[:, c0:c1], b0[:, c0:c1])
             largest(
-                z_last[:, s * TH : (s + 1) * TH].rearrange("p (c i t) -> p c t i", t=PACK, i=RUN),
-                runs(m_last[:, s, :, :]),
-                runs(c_last.rearrange("p (s t v) -> p s t v", s=2, t=PACK)[:, s, :, :]),
+                z4[:, c0:c1, :].rearrange("p (c i) t -> p c t i", i=RUN),
+                runs(two[:, s, :, part]),
+                runs(third[:, s, :, part]),
             )
-        quant_h(LAST, NQ, "z4_2")
-        finish(LAST, z_last)
+            quantise(zc[:, c0:c1], zsc[:, c0:c1], z4[:, c0:c1, :])
+            second(q, 1)
+            if q < last:
+                res = tile([P, 2, c1 - c0], F32, f"res{q}")
+                relu("s", res[:], acc[q][:])
+                nc.sync.dma_start(out=outv[:, :, c0:c1], in_=res[:])
+            else:
+                for b, eng in enumerate("sv"):
+                    res = tile([P, TQ], F32, f"res{q}{b}")
+                    relu(eng, res[:], lone[b][:])
+                    (nc.scalar, nc.sync)[b].dma_start(out=outv[:, b, c0:c1], in_=res[:])

@@ -23,7 +23,8 @@ TH = T // 2
 TQ = T // 4
 ORDER = (3, 1, 2, 0)
 PIECES = ((0, TH), (TH, TH + TQ), (TH + TQ, T))
-CAST_V = 88
+CAST_V = 44
+WIN = 2 * T
 RUN = 8
 
 
@@ -46,18 +47,24 @@ def tile_picked_wsagecat_maxrelu_l_kernel(
         w_sc = tile([P, 2, N], U8, "w_sc")
 
         w1v = w1.rearrange("(z p j) c -> z p j c", z=PASSES, j=PACK)
-        raw = [tile([P, PACK, H], F32, f"raw{z}") for z in range(PASSES)]
+        raw0 = tile([P, PACK, H], F32, "raw0")
+        raw1 = [tile([P, PACK, H // 2], F32, f"raw1{u}") for u in range(2)]
+        x_w = tile([P, PASSES, T], U32, "x_w")
         xs_v = x_scales.bitcast(I32).rearrange("z (q r) c -> r q z c", r=PACK)
+        xw_v = x_words.rearrange("z p c r -> p z (c r)").bitcast(I32)
+
+        def load_x(s):
+            cols = slice(s * TH, (s + 1) * TH)
+            nc.sync.dma_start(out=x_w[:, :, cols].bitcast(I32), in_=xw_v[:, :, cols])
+
         for r in range(PACK):
             nc.sync.dma_start(out=x_sc[r:P:32, :, :].bitcast(I32), in_=xs_v[r])
             if r == 0:
-                nc.sync.dma_start(out=raw[0][:], in_=w1v[0])
-        nc.sync.dma_start(out=raw[1][:], in_=w1v[1])
-        xw_v = x_words.rearrange("z p c r -> p z (c r)").bitcast(I32)
-        x_w = []
-        for s in range(2):
-            x_w.append(tile([P, PASSES, TH], U32, f"x_w{s}"))
-            nc.sync.dma_start(out=x_w[s][:].bitcast(I32), in_=xw_v[:, :, s * TH : (s + 1) * TH])
+                nc.sync.dma_start(out=raw0[:], in_=w1v[0])
+        load_x(0)
+        for u in range(2):
+            nc.sync.dma_start(out=raw1[u][:], in_=w1v[1, :, :, u * H // 2 : (u + 1) * H // 2])
+        load_x(1)
         for d, pos in enumerate((pos1, pos2, pos3)):
             nc.sync.dma_start(lists[d][:], pos)
         w_w = []
@@ -72,20 +79,22 @@ def tile_picked_wsagecat_maxrelu_l_kernel(
         wq = [tile([P, H, PACK], BF16, f"wq{z}") for z in range(PASSES)]
         wc, ws = {}, {}
 
-        def cast(z):
-            src = raw[z][:].rearrange("p j (m t) -> p m j t", t=PACK)
-            dst = wq[z][:].rearrange("p (t m) j -> p m j t", t=PACK)
-            nc.vector.tensor_copy(dst[:, 0:CAST_V], src[:, 0:CAST_V])
-            nc.scalar.activation(dst[:, CAST_V:P], src[:, CAST_V:P], ACT.Copy)
+        def cast(z, src, m0, m1):
+            src = src.rearrange("p j (m t) -> p m j t", t=PACK)
+            dst = wq[z][:].rearrange("p (t m) j -> p m j t", t=PACK)[:, m0:m1]
+            cut = CAST_V * (m1 - m0) // 64
+            nc.vector.tensor_copy(dst[:, 0:cut], src[:, 0:cut])
+            nc.scalar.activation(dst[:, cut : m1 - m0], src[:, cut : m1 - m0], ACT.Copy)
 
         def quantise(codes, scales, src):
             nc.vector.quantize_mx(out=codes.bitcast(FP8X4), scales=scales, in_=src.rearrange("p m j -> p (m j)"))
 
-        cast(0)
+        cast(0, raw0[:], 0, P)
         wc0 = tile([P, H], U32, "wc0")
         ws0 = tile([P, H], U8, "ws0")
         quantise(wc0[:], ws0[:], wq[0][:])
-        cast(1)
+        for u in range(2):
+            cast(1, raw1[u][:], u * P // 2, (u + 1) * P // 2)
         for t in ORDER:
             wc[0, t], ws[0, t] = wc0[:, t * P : (t + 1) * P], ws0[:, t * P : (t + 1) * P]
             wc[1, t] = tile([P, P], U32, f"wc1{t}")[:]
@@ -93,33 +102,33 @@ def tile_picked_wsagecat_maxrelu_l_kernel(
             quantise(wc[1, t], ws[1, t], wq[1][:, t * P : (t + 1) * P, :])
 
         def first(t, dst, c0, c1, z, start, stop):
-            s = c0 // TH
             nc.tensor.matmul_mx(
                 out=dst,
                 lhsT=wc[z, t].bitcast(FP8X4),
                 lhsT_scale=ws[z, t],
-                rhs=x_w[s][:, z, c0 - s * TH : c1 - s * TH].bitcast(FP8X4),
+                rhs=x_w[:, z, c0:c1].bitcast(FP8X4),
                 rhs_scale=x_sc[:, z, c0:c1],
                 start=start,
                 stop=stop,
             )
 
-        lead = []
-        for b, (c0, c1) in enumerate(PIECES):
-            lead.append(bank([P, c1 - c0], f"lead{b}", b))
+        lead = [bank([P, c1 - c0], f"lead{b}", b) for b, (c0, c1) in enumerate(PIECES)]
+        hb = {t: bank([P, T], f"hb{t}", 3 + n) for n, t in enumerate(ORDER[1:])}
+        first(ORDER[0], lead[0][:], 0, TH, 0, True, False)
+        for t in ORDER[1:]:
+            first(t, hb[t][:, 0:TH], 0, TH, 0, True, False)
+        first(ORDER[0], lead[0][:], 0, TH, 1, False, True)
+        for b in (1, 2):
             for z in range(PASSES):
-                first(ORDER[0], lead[b][:], c0, c1, z, z == 0, z == 1)
-        hb = {}
-        for n, t in enumerate(ORDER[1:]):
-            hb[t] = bank([P, T], f"hb{t}", 3 + n)
-            for s in range(2):
-                for z in range(PASSES):
-                    first(t, hb[t][:, s * TH : (s + 1) * TH], s * TH, (s + 1) * TH, z, z == 0, z == 1)
+                first(ORDER[0], lead[b][:], *PIECES[b], z, z == 0, z == 1)
+        for t in ORDER[1:]:
+            first(t, hb[t][:, TH:T], TH, T, 0, False, False)
+            first(t, hb[t][:], 0, T, 1, False, True)
 
-        win = {t: tile([P, 2 * T], F32, f"win{t}") for t in ORDER[:2]}
-        hs = tile([P, PACK * T], F32, "hs")
-        lane = lambda t: hs[:, t * T : (t + 1) * T]
-        window = {3: win[3][:], 1: win[1][:], 2: hs[:, 2 * T : 4 * T], 0: hs[:]}
+        win3 = tile([P, WIN], F32, "win3")
+        hs = tile([P, PACK * WIN], F32, "hs")
+        lane = lambda t: hs[:, t * WIN : t * WIN + T]
+        window = {3: win3[:], 1: hs[:, WIN : 2 * WIN], 2: hs[:, 2 * WIN : 3 * WIN], 0: hs[:]}
 
         def gather(eng, t, d, dst, c0, c1):
             src = window[t].indirect(lists[d][:, c0 // 16 : c1 // 16])
@@ -139,59 +148,64 @@ def tile_picked_wsagecat_maxrelu_l_kernel(
 
         for eng, b in (("s", 0), ("s", 1), ("v", 2)):
             c0, c1 = PIECES[b]
-            relu(eng, win[3][:, c0:c1], lead[b][:])
-        nc.sync.dma_start(out=lane(3), in_=win[3][:, 0:T])
+            relu(eng, win3[:, c0:c1], lead[b][:])
+        nc.sync.dma_start(out=lane(3), in_=win3[:, 0:T])
 
-        third = tile([P, 2, PACK, TH], BF16, "third")
-        two = tile([P, 2, PACK, TH], BF16, "two")
-        halves = lambda ap: ap.rearrange("p (h v) -> p h v", h=2)
-
+        third = [tile([P, PACK, TH], F32, f"third{s}", ("wc12", "win3")[s]) for s in range(2)]
+        two = tile([P, PACK, T], BF16, "two")
         a3 = tile([P, T], BF16, "a3")
-        b3 = tile([P, T], BF16, "b3", "wc11")
-        gather("s", 3, 0, a3[:], 0, T)
-        gather("v", 3, 2, third[:, :, 3, :], 0, T)
-        relu("s", win[1][:, 0:T], hb[1][:])
-        nc.sync.dma_start(out=lane(1), in_=win[1][:, 0:T])
-        gather("v", 3, 1, b3[:, 0:TH], 0, TH)
-        gather("s", 3, 1, b3[:, TH:T], TH, T)
-        gather("v", 1, 2, third[:, :, 1, :], 0, T)
-        relu("s", lane(2), hb[2][:])
-        relu("s", lane(0), hb[0][:])
-        largest(two[:, :, 3, :], halves(a3[:]), halves(b3[:]))
-
-        h4 = tile([P, T, PACK], BF16, "h4")
-        hv = hs[:].rearrange("p (t v) -> p v t", t=PACK)
-        for c0, c1 in PIECES:
-            nc.gpsimd.tensor_scalar(h4[:, c0:c1, :], hv[:, c0:c1, :], 1.0, 0.0, ALU.mult, ALU.add)
-
-        a12 = tile([P, 2, 2, TH], BF16, "a12", "wc10")
-        b12 = tile([P, 2, 2, TH], BF16, "b12", "ws10")
-        gather("v", 2, 2, third[:, :, 2, :], 0, T)
-        for d, dst in enumerate((a12, b12)):
-            gather("v", 2, d, dst[:, :, 1, :], 0, T)
-            for s in range(2):
-                gather("s", 1, d, dst[:, s, 0, :], s * TH, (s + 1) * TH)
-        largest(two[:, :, 1:3, :], a12[:], b12[:])
-
+        b3 = [tile([P, TH], BF16, f"b3{s}", (None, "wc10")[s]) for s in range(2)]
+        a12 = tile([P, 2, 2, TH], BF16, "a12")
+        b12 = tile([P, 2, 2, TH], BF16, "b12")
         a0 = tile([P, T], BF16, "a0")
         b0 = tile([P, T], BF16, "b0")
+
+        def third_of(eng, t, c0, c1):
+            s = c0 // TH
+            gather(eng, t, 2, third[s][:, t, c0 - s * TH : c1 - s * TH], c0, c1)
+
+        gather("s", 3, 0, a3[:], 0, T)
+        gather("v", 3, 1, b3[0][:], 0, TH)
+        relu("v", lane(1), hb[1][:])
+        relu("s", lane(2), hb[2][:])
+        third_of("s", 3, 0, TH)
+        relu("s", lane(0), hb[0][:])
+        gather("s", 3, 1, b3[1][:], TH, T)
+        for t in (1, 2):
+            for d, dst in enumerate((a12, b12)):
+                gather("v", t, d, dst[:, :, t - 1, :], 0, T)
+
+        window[3] = hs[:, 3 * WIN : 4 * WIN]
+        third_of("v", 3, TH, T)
+        h4 = [tile([P, TH, PACK], BF16, f"h4{s}") for s in range(2)]
+        hv = hs[:].rearrange("p (t v) -> p v t", t=PACK)
         for c0, c1 in PIECES:
             s = c0 // TH
-            gather("s", 0, 0, a0[:, c0:c1], c0, c1)
-            gather("s", 0, 1, b0[:, c0:c1], c0, c1)
-            gather("s", 0, 2, third[:, s, 0, c0 - s * TH : c1 - s * TH], c0, c1)
+            nc.gpsimd.tensor_scalar(h4[s][:, c0 - s * TH : c1 - s * TH, :], hv[:, c0:c1, :], 1.0, 0.0, ALU.mult, ALU.add)
+
+        for t in (1, 2):
+            third_of("s", t, 0, TH)
+        gather("s", 0, 0, a0[:, 0:TH], 0, TH)
+        gather("s", 0, 1, b0[:, 0:TH], 0, TH)
+        third_of("s", 0, 0, TH)
+        gather("s", 0, 0, a0[:, TH:T], TH, T)
+        gather("s", 0, 1, b0[:, TH:T], TH, T)
+        for t in (1, 2):
+            third_of("s", t, TH, T)
+        for c0, c1 in PIECES[1:]:
+            third_of("s", 0, c0, c1)
+
+        largest(two[:, 1:3, :].rearrange("p l (h v) -> p h l v", h=2), a12[:], b12[:])
+        for s in range(2):
+            largest(two[:, 3, s * TH : (s + 1) * TH], a3[:, s * TH : (s + 1) * TH], b3[s][:])
 
         hc = tile([P, T], U32, "hc")
         hsc = tile([P, T], U8, "hsc")
         zc = tile([P, T], U32, "zc")
         zsc = tile([P, T], U8, "zsc")
-        z4 = tile([P, T, PACK], BF16, "z4")
         outv = out.rearrange("(b p) v -> p b v", p=P)
         last = len(PIECES) - 1
-        acc = {}
-        for q, (c0, c1) in enumerate(PIECES[:last]):
-            both = bank([P, 2, c1 - c0], f"both{q}", 6 + q)
-            acc[q] = both
+        acc = [bank([P, 2, c1 - c0], f"both{q}", 6 + q) for q, (c0, c1) in enumerate(PIECES[:last])]
         lone = [bank([P, TQ], f"lone{b}", b) for b in range(2)]
 
         def second(q, a):
@@ -208,23 +222,28 @@ def tile_picked_wsagecat_maxrelu_l_kernel(
                     stop=(a == 1 and (b == 1 or not shared)),
                 )
 
-        for s in range(2):
+        def quant_h(s):
             cols = slice(s * TH, (s + 1) * TH)
-            quantise(hc[:, cols], hsc[:, cols], h4[:, cols, :])
-        for q in range(len(PIECES)):
-            second(q, 0)
+            quantise(hc[:, cols], hsc[:, cols], h4[s][:])
+            for q in ((0,), (1, 2))[s]:
+                second(q, 0)
 
+        z4 = [tile([P, TH, PACK], BF16, f"z4{s}", f"h4{s}") for s in range(2)]
         runs = lambda ap: ap.rearrange("p t (c i) -> p c t i", i=RUN)
-        for q, (c0, c1) in enumerate(PIECES):
+
+        def z_part(q):
+            c0, c1 = PIECES[q]
             s = c0 // TH
-            part = slice(c0 - s * TH, c1 - s * TH)
-            largest(two[:, s, 0, part], a0[:, c0:c1], b0[:, c0:c1])
-            largest(
-                z4[:, c0:c1, :].rearrange("p (c i) t -> p c t i", i=RUN),
-                runs(two[:, s, :, part]),
-                runs(third[:, s, :, part]),
-            )
-            quantise(zc[:, c0:c1], zsc[:, c0:c1], z4[:, c0:c1, :])
+            return z4[s][:, c0 - s * TH : c1 - s * TH, :]
+
+        def top(q):
+            c0, c1 = PIECES[q]
+            s = c0 // TH
+            largest(z_part(q).rearrange("p (c i) t -> p c t i", i=RUN), runs(two[:, :, c0:c1]), runs(third[s][:, :, c0 - s * TH : c1 - s * TH]))
+
+        def finish(q):
+            c0, c1 = PIECES[q]
+            quantise(zc[:, c0:c1], zsc[:, c0:c1], z_part(q))
             second(q, 1)
             if q < last:
                 res = tile([P, 2, c1 - c0], F32, f"res{q}")
@@ -235,3 +254,14 @@ def tile_picked_wsagecat_maxrelu_l_kernel(
                     res = tile([P, TQ], F32, f"res{q}{b}")
                     relu(eng, res[:], lone[b][:])
                     (nc.scalar, nc.sync)[b].dma_start(out=outv[:, b, c0:c1], in_=res[:])
+
+        largest(two[:, 0, 0:TH], a0[:, 0:TH], b0[:, 0:TH])
+        quant_h(0)
+        top(0)
+        quant_h(1)
+        largest(two[:, 0, TH:T], a0[:, TH:T], b0[:, TH:T])
+        finish(0)
+        top(1)
+        top(2)
+        finish(1)
+        finish(2)

@@ -22,6 +22,7 @@ PASSES = K // (P * PACK)
 TH = T // 2
 TQ = T // 4
 ORDER = (3, 1, 2, 0)
+EMPTIES = "svsv"
 PIECES = ((0, TH), (TH, TH + TQ), (TH + TQ, T))
 CAST_V = 44
 WIN = 2 * T
@@ -49,13 +50,12 @@ def tile_picked_wsagecat_maxrelu_l_kernel(
         w1v = w1.rearrange("(z p j) c -> z p j c", z=PASSES, j=PACK)
         raw0 = tile([P, PACK, H], F32, "raw0")
         raw1 = [tile([P, PACK, H // 2], F32, f"raw1{u}") for u in range(2)]
-        x_w = tile([P, PASSES, T], U32, "x_w")
+        x_w = [tile([P, T], U32, f"x_w{z}") for z in range(PASSES)]
         xs_v = x_scales.bitcast(I32).rearrange("z (q r) c -> r q z c", r=PACK)
-        xw_v = x_words.rearrange("z p c r -> p z (c r)").bitcast(I32)
+        xw_v = x_words.rearrange("z p c r -> z p (c r)").bitcast(I32)
 
-        def load_x(s):
-            cols = slice(s * TH, (s + 1) * TH)
-            nc.sync.dma_start(out=x_w[:, :, cols].bitcast(I32), in_=xw_v[:, :, cols])
+        def load_x(z):
+            nc.sync.dma_start(out=x_w[z][:].bitcast(I32), in_=xw_v[z])
 
         for r in range(PACK):
             nc.sync.dma_start(out=x_sc[r:P:32, :, :].bitcast(I32), in_=xs_v[r])
@@ -92,7 +92,8 @@ def tile_picked_wsagecat_maxrelu_l_kernel(
         cast(0, raw0[:], 0, P)
         wc0 = tile([P, H], U32, "wc0")
         ws0 = tile([P, H], U8, "ws0")
-        quantise(wc0[:], ws0[:], wq[0][:])
+        for cols in (slice(H // 2, H), slice(0, H // 2)):
+            quantise(wc0[:, cols], ws0[:, cols], wq[0][:, cols, :])
         for u in range(2):
             cast(1, raw1[u][:], u * P // 2, (u + 1) * P // 2)
         for t in ORDER:
@@ -101,34 +102,23 @@ def tile_picked_wsagecat_maxrelu_l_kernel(
             ws[1, t] = tile([P, P], U8, f"ws1{t}")[:]
             quantise(wc[1, t], ws[1, t], wq[1][:, t * P : (t + 1) * P, :])
 
-        def first(t, dst, c0, c1, z, start, stop):
-            nc.tensor.matmul_mx(
-                out=dst,
-                lhsT=wc[z, t].bitcast(FP8X4),
-                lhsT_scale=ws[z, t],
-                rhs=x_w[:, z, c0:c1].bitcast(FP8X4),
-                rhs_scale=x_sc[:, z, c0:c1],
-                start=start,
-                stop=stop,
-            )
-
-        lead = [bank([P, c1 - c0], f"lead{b}", b) for b, (c0, c1) in enumerate(PIECES)]
-        hb = {t: bank([P, T], f"hb{t}", 3 + n) for n, t in enumerate(ORDER[1:])}
-        first(ORDER[0], lead[0][:], 0, TH, 0, True, False)
-        for t in ORDER[1:]:
-            first(t, hb[t][:, 0:TH], 0, TH, 0, True, False)
-        first(ORDER[0], lead[0][:], 0, TH, 1, False, True)
-        for b in (1, 2):
-            for z in range(PASSES):
-                first(ORDER[0], lead[b][:], *PIECES[b], z, z == 0, z == 1)
-        for t in ORDER[1:]:
-            first(t, hb[t][:, TH:T], TH, T, 0, False, False)
-            first(t, hb[t][:], 0, T, 1, False, True)
+        hb = {t: bank([P, T], f"hb{t}", t) for t in ORDER}
+        for z in range(PASSES):
+            for t in ORDER:
+                nc.tensor.matmul_mx(
+                    out=hb[t][:],
+                    lhsT=wc[z, t].bitcast(FP8X4),
+                    lhsT_scale=ws[z, t],
+                    rhs=x_w[z][:].bitcast(FP8X4),
+                    rhs_scale=x_sc[:, z, :],
+                    start=(z == 0),
+                    stop=(z == PASSES - 1),
+                )
 
         win3 = tile([P, WIN], F32, "win3")
         hs = tile([P, PACK * WIN], F32, "hs")
         lane = lambda t: hs[:, t * WIN : t * WIN + T]
-        window = {3: win3[:], 1: hs[:, WIN : 2 * WIN], 2: hs[:, 2 * WIN : 3 * WIN], 0: hs[:]}
+        window = {0: hs[:], 1: hs[:, WIN : 2 * WIN], 2: hs[:, 2 * WIN : 3 * WIN], 3: win3[:]}
 
         def gather(eng, t, d, dst, c0, c1):
             src = window[t].indirect(lists[d][:, c0 // 16 : c1 // 16])
@@ -146,89 +136,78 @@ def tile_picked_wsagecat_maxrelu_l_kernel(
         def largest(dst, a, b):
             nc.vector.tensor_tensor(dst, a, b, ALU.max)
 
-        for eng, b in (("s", 0), ("s", 1), ("v", 2)):
-            c0, c1 = PIECES[b]
-            relu(eng, win3[:, c0:c1], lead[b][:])
-        nc.sync.dma_start(out=lane(3), in_=win3[:, 0:T])
+        for eng, t in zip(EMPTIES, ORDER):
+            relu(eng, win3[:, 0:T] if t == 3 else lane(t), hb[t][:])
+        nc.gpsimd.tensor_scalar(lane(3), win3[:, 0:T], 1.0, 0.0, ALU.mult, ALU.add)
 
-        third = [tile([P, PACK, TH], F32, f"third{s}", ("wc12", "win3")[s]) for s in range(2)]
+        h4 = [tile([P, TH, PACK], BF16, f"h4{s}") for s in range(2)]
+        hv = hs[:].rearrange("p (t v) -> p v t", t=PACK)
+        for s in range(2):
+            nc.gpsimd.tensor_scalar(h4[s][:], hv[:, s * TH : (s + 1) * TH, :], 1.0, 0.0, ALU.mult, ALU.add)
+
+        third = tile([P, PACK, T], F32, "third")
         two = tile([P, PACK, T], BF16, "two")
-        a3 = tile([P, T], BF16, "a3")
-        b3 = [tile([P, TH], BF16, f"b3{s}", (None, "wc10")[s]) for s in range(2)]
+        ab = {(t, d): tile([P, T], BF16, f"ab{t}{d}") for t in (3, 0) for d in range(2)}
         a12 = tile([P, 2, 2, TH], BF16, "a12")
         b12 = tile([P, 2, 2, TH], BF16, "b12")
-        a0 = tile([P, T], BF16, "a0")
-        b0 = tile([P, T], BF16, "b0")
 
         def third_of(eng, t, c0, c1):
-            s = c0 // TH
-            gather(eng, t, 2, third[s][:, t, c0 - s * TH : c1 - s * TH], c0, c1)
+            gather(eng, t, 2, third[:, t, c0:c1], c0, c1)
 
-        gather("s", 3, 0, a3[:], 0, T)
-        gather("v", 3, 1, b3[0][:], 0, TH)
-        relu("v", lane(1), hb[1][:])
-        relu("s", lane(2), hb[2][:])
-        third_of("s", 3, 0, TH)
-        relu("s", lane(0), hb[0][:])
-        gather("s", 3, 1, b3[1][:], TH, T)
         for t in (1, 2):
             for d, dst in enumerate((a12, b12)):
                 gather("v", t, d, dst[:, :, t - 1, :], 0, T)
+        third_of("v", 3, 0, TH)
 
-        window[3] = hs[:, 3 * WIN : 4 * WIN]
-        third_of("v", 3, TH, T)
-        h4 = [tile([P, TH, PACK], BF16, f"h4{s}") for s in range(2)]
-        hv = hs[:].rearrange("p (t v) -> p v t", t=PACK)
-        for c0, c1 in PIECES:
-            s = c0 // TH
-            nc.gpsimd.tensor_scalar(h4[s][:, c0 - s * TH : c1 - s * TH, :], hv[:, c0:c1, :], 1.0, 0.0, ALU.mult, ALU.add)
-
-        for t in (1, 2):
+        for t in (3, 0):
+            for d in range(2):
+                gather("s", t, d, ab[t, d][:], 0, T)
+        for t in (1, 2, 0):
             third_of("s", t, 0, TH)
-        gather("s", 0, 0, a0[:, 0:TH], 0, TH)
-        gather("s", 0, 1, b0[:, 0:TH], 0, TH)
-        third_of("s", 0, 0, TH)
-        gather("s", 0, 0, a0[:, TH:T], TH, T)
-        gather("s", 0, 1, b0[:, TH:T], TH, T)
-        for t in (1, 2):
+        for t in (1, 2, 3):
             third_of("s", t, TH, T)
         for c0, c1 in PIECES[1:]:
             third_of("s", 0, c0, c1)
 
         largest(two[:, 1:3, :].rearrange("p l (h v) -> p h l v", h=2), a12[:], b12[:])
-        for s in range(2):
-            largest(two[:, 3, s * TH : (s + 1) * TH], a3[:, s * TH : (s + 1) * TH], b3[s][:])
+        for t in (3, 0):
+            largest(two[:, t, :], ab[t, 0][:], ab[t, 1][:])
 
-        hc = tile([P, T], U32, "hc")
+        hc = [tile([P, TH], U32, f"hc{s}", (None, "ab00")[s]) for s in range(2)]
         hsc = tile([P, T], U8, "hsc")
         zc = tile([P, T], U32, "zc")
         zsc = tile([P, T], U8, "zsc")
         outv = out.rearrange("(b p) v -> p b v", p=P)
-        last = len(PIECES) - 1
-        acc = [bank([P, 2, c1 - c0], f"both{q}", 6 + q) for q, (c0, c1) in enumerate(PIECES[:last])]
-        lone = [bank([P, TQ], f"lone{b}", b) for b in range(2)]
+        SHARED = 1
+        acc = {}
+        for q, (c0, c1) in enumerate(PIECES):
+            if q == SHARED:
+                both = bank([P, 2, c1 - c0], "both", 0)
+                acc[q, 0], acc[q, 1] = both[:, 0, :], both[:, 1, :]
+            else:
+                for b in range(2):
+                    acc[q, b] = bank([P, c1 - c0], f"lone{q}{b}", 4 + q + b)[:]
 
         def second(q, a):
             c0, c1 = PIECES[q]
-            shared = q < last
             for b in range(2):
                 nc.tensor.matmul_mx(
-                    out=acc[q][:, b, :] if shared else lone[b][:],
+                    out=acc[q, b],
                     lhsT=w_w[a][:, 2 * P * b : 2 * P * (b + 1)].bitcast(FP4X4),
                     lhsT_scale=w_sc[:, a, P * b : P * (b + 1)],
-                    rhs=(hc, zc)[a][:, c0:c1].bitcast(FP8X4),
+                    rhs=(hc[c0 // TH][:, c0 % TH : c0 % TH + c1 - c0], zc[:, c0:c1])[a].bitcast(FP8X4),
                     rhs_scale=(hsc, zsc)[a][:, c0:c1],
-                    start=(a == 0 and (b == 0 or not shared)),
-                    stop=(a == 1 and (b == 1 or not shared)),
+                    start=(a == 0 and (b == 0 or q != SHARED)),
+                    stop=(a == 1 and (b == 1 or q != SHARED)),
                 )
 
         def quant_h(s):
             cols = slice(s * TH, (s + 1) * TH)
-            quantise(hc[:, cols], hsc[:, cols], h4[s][:])
+            quantise(hc[s][:], hsc[:, cols], h4[s][:])
             for q in ((0,), (1, 2))[s]:
                 second(q, 0)
 
-        z4 = [tile([P, TH, PACK], BF16, f"z4{s}", f"h4{s}") for s in range(2)]
+        z4 = [tile([P, TH, PACK], BF16, f"z4{s}", "h40") for s in range(2)]
         runs = lambda ap: ap.rearrange("p t (c i) -> p c t i", i=RUN)
 
         def z_part(q):
@@ -238,28 +217,25 @@ def tile_picked_wsagecat_maxrelu_l_kernel(
 
         def top(q):
             c0, c1 = PIECES[q]
-            s = c0 // TH
-            largest(z_part(q).rearrange("p (c i) t -> p c t i", i=RUN), runs(two[:, :, c0:c1]), runs(third[s][:, :, c0 - s * TH : c1 - s * TH]))
+            largest(z_part(q).rearrange("p (c i) t -> p c t i", i=RUN), runs(two[:, :, c0:c1]), runs(third[:, :, c0:c1]))
 
         def finish(q):
             c0, c1 = PIECES[q]
             quantise(zc[:, c0:c1], zsc[:, c0:c1], z_part(q))
             second(q, 1)
-            if q < last:
+            if q == SHARED:
                 res = tile([P, 2, c1 - c0], F32, f"res{q}")
-                relu("s", res[:], acc[q][:])
+                relu("s", res[:], both[:])
                 nc.sync.dma_start(out=outv[:, :, c0:c1], in_=res[:])
             else:
-                for b, eng in enumerate("sv"):
-                    res = tile([P, TQ], F32, f"res{q}{b}")
-                    relu(eng, res[:], lone[b][:])
-                    (nc.scalar, nc.sync)[b].dma_start(out=outv[:, b, c0:c1], in_=res[:])
+                for b, eng in enumerate("sv" if q else "ss"):
+                    res = tile([P, c1 - c0], F32, f"res{q}{b}")
+                    relu(eng, res[:], acc[q, b])
+                    (nc.scalar if q and b == 0 else nc.sync).dma_start(out=outv[:, b, c0:c1], in_=res[:])
 
-        largest(two[:, 0, 0:TH], a0[:, 0:TH], b0[:, 0:TH])
         quant_h(0)
         top(0)
         quant_h(1)
-        largest(two[:, 0, TH:T], a0[:, TH:T], b0[:, TH:T])
         finish(0)
         top(1)
         top(2)

@@ -21,10 +21,10 @@ PACK = 4
 PASSES = K // (P * PACK)
 TH = T // 2
 TQ = T // 4
-ORDER = (3, 1, 2, 0)
+ORDER = (3, 2, 1, 0)
 EMPTIES = "svsv"
 PIECES = ((0, TH), (TH, TH + TQ), (TH + TQ, T))
-CAST_V = 44
+CAST_V = 88
 WIN = 2 * T
 RUN = 8
 
@@ -48,8 +48,7 @@ def tile_picked_wsagecat_maxrelu_l_kernel(
         w_sc = tile([P, 2, N], U8, "w_sc")
 
         w1v = w1.rearrange("(z p j) c -> z p j c", z=PASSES, j=PACK)
-        raw0 = tile([P, PACK, H], F32, "raw0")
-        raw1 = [tile([P, PACK, H // 2], F32, f"raw1{u}") for u in range(2)]
+        raw = [tile([P, PACK, H], F32, f"raw{z}") for z in range(PASSES)]
         x_w = [tile([P, T], U32, f"x_w{z}") for z in range(PASSES)]
         xs_v = x_scales.bitcast(I32).rearrange("z (q r) c -> r q z c", r=PACK)
         xw_v = x_words.rearrange("z p c r -> z p (c r)").bitcast(I32)
@@ -60,10 +59,9 @@ def tile_picked_wsagecat_maxrelu_l_kernel(
         for r in range(PACK):
             nc.sync.dma_start(out=x_sc[r:P:32, :, :].bitcast(I32), in_=xs_v[r])
             if r == 0:
-                nc.sync.dma_start(out=raw0[:], in_=w1v[0])
+                nc.sync.dma_start(out=raw[0][:], in_=w1v[0])
         load_x(0)
-        for u in range(2):
-            nc.sync.dma_start(out=raw1[u][:], in_=w1v[1, :, :, u * H // 2 : (u + 1) * H // 2])
+        nc.sync.dma_start(out=raw[1][:], in_=w1v[1])
         load_x(1)
         for d, pos in enumerate((pos1, pos2, pos3)):
             nc.sync.dma_start(lists[d][:], pos)
@@ -79,23 +77,22 @@ def tile_picked_wsagecat_maxrelu_l_kernel(
         wq = [tile([P, H, PACK], BF16, f"wq{z}") for z in range(PASSES)]
         wc, ws = {}, {}
 
-        def cast(z, src, m0, m1):
-            src = src.rearrange("p j (m t) -> p m j t", t=PACK)
-            dst = wq[z][:].rearrange("p (t m) j -> p m j t", t=PACK)[:, m0:m1]
-            cut = CAST_V * (m1 - m0) // 64
-            nc.vector.tensor_copy(dst[:, 0:cut], src[:, 0:cut])
-            nc.scalar.activation(dst[:, cut : m1 - m0], src[:, cut : m1 - m0], ACT.Copy)
+        def cast(z):
+            src = raw[z][:].rearrange("p j (m t) -> p m j t", t=PACK)
+            dst = wq[z][:].rearrange("p (t m) j -> p m j t", t=PACK)
+            for pair in (slice(2, 4), slice(0, 2)):
+                nc.vector.tensor_copy(dst[:, 0:CAST_V, :, pair], src[:, 0:CAST_V, :, pair])
+                nc.scalar.activation(dst[:, CAST_V:P, :, pair], src[:, CAST_V:P, :, pair], ACT.Copy)
 
         def quantise(codes, scales, src):
             nc.vector.quantize_mx(out=codes.bitcast(FP8X4), scales=scales, in_=src.rearrange("p m j -> p (m j)"))
 
-        cast(0, raw0[:], 0, P)
+        cast(0)
         wc0 = tile([P, H], U32, "wc0")
         ws0 = tile([P, H], U8, "ws0")
         for cols in (slice(H // 2, H), slice(0, H // 2)):
             quantise(wc0[:, cols], ws0[:, cols], wq[0][:, cols, :])
-        for u in range(2):
-            cast(1, raw1[u][:], u * P // 2, (u + 1) * P // 2)
+        cast(1)
         for t in ORDER:
             wc[0, t], ws[0, t] = wc0[:, t * P : (t + 1) * P], ws0[:, t * P : (t + 1) * P]
             wc[1, t] = tile([P, P], U32, f"wc1{t}")[:]
@@ -154,7 +151,7 @@ def tile_picked_wsagecat_maxrelu_l_kernel(
         def third_of(eng, t, c0, c1):
             gather(eng, t, 2, third[:, t, c0:c1], c0, c1)
 
-        for t in (1, 2):
+        for t in (2, 1):
             for d, dst in enumerate((a12, b12)):
                 gather("v", t, d, dst[:, :, t - 1, :], 0, T)
         third_of("v", 3, 0, TH)

@@ -22,11 +22,10 @@ PASSES = K // (P * PACK)
 TH = T // 2
 TQ = T // 4
 ORDER = (3, 2, 1, 0)
-EMPTIES = "svsv"
 PIECES = ((0, TH), (TH, TH + TQ), (TH + TQ, T))
 CAST_V = 88
 WIN = 2 * T
-RUN = 8
+RUN = 4
 
 
 def tile_picked_wsagecat_maxrelu_l_kernel(
@@ -56,11 +55,10 @@ def tile_picked_wsagecat_maxrelu_l_kernel(
         def load_x(z):
             nc.sync.dma_start(out=x_w[z][:].bitcast(I32), in_=xw_v[z])
 
+        nc.sync.dma_start(out=raw[0][:], in_=w1v[0])
+        load_x(0)
         for r in range(PACK):
             nc.sync.dma_start(out=x_sc[r:P:32, :, :].bitcast(I32), in_=xs_v[r])
-            if r == 0:
-                nc.sync.dma_start(out=raw[0][:], in_=w1v[0])
-        load_x(0)
         nc.sync.dma_start(out=raw[1][:], in_=w1v[1])
         load_x(1)
         for d, pos in enumerate((pos1, pos2, pos3)):
@@ -99,15 +97,16 @@ def tile_picked_wsagecat_maxrelu_l_kernel(
             ws[1, t] = tile([P, P], U8, f"ws1{t}")[:]
             quantise(wc[1, t], ws[1, t], wq[1][:, t * P : (t + 1) * P, :])
 
-        hb = {t: bank([P, T], f"hb{t}", t) for t in ORDER}
+        parts = [(3, 0, T, "s"), (2, 0, T, "v"), (1, 0, T, "s"), (0, 0, TH, "v"), (0, TH, T, "s")]
+        hb = [bank([P, c1 - c0], f"hb{b}", b) for b, (t, c0, c1, eng) in enumerate(parts)]
         for z in range(PASSES):
-            for t in ORDER:
+            for b, (t, c0, c1, eng) in enumerate(parts):
                 nc.tensor.matmul_mx(
-                    out=hb[t][:],
+                    out=hb[b][:],
                     lhsT=wc[z, t].bitcast(FP8X4),
                     lhsT_scale=ws[z, t],
-                    rhs=x_w[z][:].bitcast(FP8X4),
-                    rhs_scale=x_sc[:, z, :],
+                    rhs=x_w[z][:, c0:c1].bitcast(FP8X4),
+                    rhs_scale=x_sc[:, z, c0:c1],
                     start=(z == 0),
                     stop=(z == PASSES - 1),
                 )
@@ -133,8 +132,8 @@ def tile_picked_wsagecat_maxrelu_l_kernel(
         def largest(dst, a, b):
             nc.vector.tensor_tensor(dst, a, b, ALU.max)
 
-        for eng, t in zip(EMPTIES, ORDER):
-            relu(eng, win3[:, 0:T] if t == 3 else lane(t), hb[t][:])
+        for b, (t, c0, c1, eng) in enumerate(parts):
+            relu(eng, (win3[:, 0:T] if t == 3 else lane(t))[:, c0:c1], hb[b][:])
         nc.gpsimd.tensor_scalar(lane(3), win3[:, 0:T], 1.0, 0.0, ALU.mult, ALU.add)
 
         h4 = [tile([P, TH, PACK], BF16, f"h4{s}") for s in range(2)]
@@ -183,7 +182,7 @@ def tile_picked_wsagecat_maxrelu_l_kernel(
                 acc[q, 0], acc[q, 1] = both[:, 0, :], both[:, 1, :]
             else:
                 for b in range(2):
-                    acc[q, b] = bank([P, c1 - c0], f"lone{q}{b}", 4 + q + b)[:]
+                    acc[q, b] = bank([P, c1 - c0], f"lone{q}{b}", ((5, 6), (), (7, 1))[q][b])[:]
 
         def second(q, a):
             c0, c1 = PIECES[q]

@@ -47,7 +47,13 @@ def tile_picked_wsagecat_maxrelu_l_kernel(
         w_sc = tile([P, 2, N], U8, "w_sc")
 
         w1v = w1.rearrange("(z p j) c -> z p j c", z=PASSES, j=PACK)
-        raw = [tile([P, PACK, H], F32, f"raw{z}") for z in range(PASSES)]
+        rows = {0: [(0, PACK)], 1: [(0, 2), (2, PACK)]}
+        raw = {(z, j0): tile([P, j1 - j0, H], F32, f"raw{z}{j0}") for z in rows for j0, j1 in rows[z]}
+
+        def load_w1(z):
+            for j0, j1 in rows[z]:
+                nc.sync.dma_start(out=raw[z, j0][:], in_=w1v[z, :, j0:j1, :])
+
         x_w = [tile([P, T], U32, f"x_w{z}") for z in range(PASSES)]
         xs_v = x_scales.bitcast(I32).rearrange("z (q r) c -> r q z c", r=PACK)
         xw_v = x_words.rearrange("z p c r -> z p (c r)").bitcast(I32)
@@ -55,11 +61,11 @@ def tile_picked_wsagecat_maxrelu_l_kernel(
         def load_x(z):
             nc.sync.dma_start(out=x_w[z][:].bitcast(I32), in_=xw_v[z])
 
-        nc.sync.dma_start(out=raw[0][:], in_=w1v[0])
+        load_w1(0)
         load_x(0)
         for r in range(PACK):
             nc.sync.dma_start(out=x_sc[r:P:32, :, :].bitcast(I32), in_=xs_v[r])
-        nc.sync.dma_start(out=raw[1][:], in_=w1v[1])
+        load_w1(1)
         load_x(1)
         for d, pos in enumerate((pos1, pos2, pos3)):
             nc.sync.dma_start(lists[d][:], pos)
@@ -76,11 +82,15 @@ def tile_picked_wsagecat_maxrelu_l_kernel(
         wc, ws = {}, {}
 
         def cast(z):
-            src = raw[z][:].rearrange("p j (m t) -> p m j t", t=PACK)
-            dst = wq[z][:].rearrange("p (t m) j -> p m j t", t=PACK)
-            for pair in (slice(2, 4), slice(0, 2)):
-                nc.vector.tensor_copy(dst[:, 0:CAST_V, :, pair], src[:, 0:CAST_V, :, pair])
-                nc.scalar.activation(dst[:, CAST_V:P, :, pair], src[:, CAST_V:P, :, pair], ACT.Copy)
+            for j0, j1 in rows[z]:
+                src = raw[z, j0][:].rearrange("p j (m t) -> p m t j", t=PACK)
+                dst = wq[z][:, :, j0:j1].rearrange("p (t m) j -> p m t j", t=PACK)
+                if j1 - j0 == PACK:
+                    src, dst = (ap.rearrange("p m t j -> p m j t") for ap in (src, dst))
+                for t0 in (2, 0):
+                    pair = (lambda ap: ap[:, :, :, t0 : t0 + 2]) if j1 - j0 == PACK else (lambda ap: ap[:, :, t0 : t0 + 2, :])
+                    nc.vector.tensor_copy(pair(dst[:, 0:CAST_V]), pair(src[:, 0:CAST_V]))
+                    nc.scalar.activation(pair(dst[:, CAST_V:P]), pair(src[:, CAST_V:P]), ACT.Copy)
 
         def quantise(codes, scales, src):
             nc.vector.quantize_mx(out=codes.bitcast(FP8X4), scales=scales, in_=src.rearrange("p m j -> p (m j)"))

@@ -107,7 +107,7 @@ def tile_picked_wsagecat_maxrelu_l_kernel(
             ws[1, t] = tile([P, P], U8, f"ws1{t}")[:]
             quantise(wc[1, t], ws[1, t], wq[1][:, t * P : (t + 1) * P, :])
 
-        parts = [(3, 0, T, "s"), (2, 0, T, "v"), (1, 0, T, "s"), (0, 0, TH, "v"), (0, TH, T, "s")]
+        parts = [(t, s * TH, (s + 1) * TH, "sv"[s] if t else "s") for t in ORDER for s in range(2)]
         hb = [bank([P, c1 - c0], f"hb{b}", b) for b, (t, c0, c1, eng) in enumerate(parts)]
         for z in range(PASSES):
             for b, (t, c0, c1, eng) in enumerate(parts):
@@ -151,11 +151,11 @@ def tile_picked_wsagecat_maxrelu_l_kernel(
         for s in range(2):
             nc.gpsimd.tensor_scalar(h4[s][:], hv[:, s * TH : (s + 1) * TH, :], 1.0, 0.0, ALU.mult, ALU.add)
 
-        third = tile([P, PACK, T], F32, "third")
+        third = tile([P, PACK, T], F32, "third", "x_w1")
         two = tile([P, PACK, T], BF16, "two")
-        ab = {(t, d): tile([P, T], BF16, f"ab{t}{d}") for t in (3, 0) for d in range(2)}
-        a12 = tile([P, 2, 2, TH], BF16, "a12")
-        b12 = tile([P, 2, 2, TH], BF16, "b12")
+        ab = {(t, d): tile([P, T], BF16, f"ab{t}{d}", ("wc10", "ws10")[d] if t == 3 else None) for t in (3, 0) for d in range(2)}
+        a12 = tile([P, 2, 2, TH], BF16, "a12", "wc11")
+        b12 = tile([P, 2, 2, TH], BF16, "b12", "ws11")
 
         def third_of(eng, t, c0, c1):
             gather(eng, t, 2, third[:, t, c0:c1], c0, c1)
@@ -192,7 +192,7 @@ def tile_picked_wsagecat_maxrelu_l_kernel(
                 acc[q, 0], acc[q, 1] = both[:, 0, :], both[:, 1, :]
             else:
                 for b in range(2):
-                    acc[q, b] = bank([P, c1 - c0], f"lone{q}{b}", ((5, 6), (), (7, 1))[q][b])[:]
+                    acc[q, b] = bank([P, c1 - c0], f"lone{q}{b}", ((1, 2), (), (3, 4))[q][b])[:]
 
         def second(q, a):
             c0, c1 = PIECES[q]

@@ -85,10 +85,9 @@ def tile_picked_wsagecat_maxrelu_l_kernel(
             for j0, j1 in rows[z]:
                 src = raw[z, j0][:].rearrange("p j (m t) -> p m t j", t=PACK)
                 dst = wq[z][:, :, j0:j1].rearrange("p (t m) j -> p m t j", t=PACK)
-                if j1 - j0 == PACK:
-                    src, dst = (ap.rearrange("p m t j -> p m j t") for ap in (src, dst))
+                src, dst = (ap.rearrange("p m t j -> p m j t") for ap in (src, dst))
                 for t0 in (2, 0):
-                    pair = (lambda ap: ap[:, :, :, t0 : t0 + 2]) if j1 - j0 == PACK else (lambda ap: ap[:, :, t0 : t0 + 2, :])
+                    pair = lambda ap: ap[:, :, :, t0 : t0 + 2]
                     nc.vector.tensor_copy(pair(dst[:, 0:CAST_V]), pair(src[:, 0:CAST_V]))
                     nc.scalar.activation(pair(dst[:, CAST_V:P]), pair(src[:, CAST_V:P]), ACT.Copy)
 

@@ -236,7 +236,7 @@ def tile_picked_wsagecat_maxrelu_l_kernel(
                 for b, eng in enumerate("sv" if q else "ss"):
                     res = tile([P, c1 - c0], F32, f"res{q}{b}")
                     relu(eng, res[:], acc[q, b])
-                    (nc.scalar if q and b == 0 else nc.sync).dma_start(out=outv[:, b, c0:c1], in_=res[:])
+                    nc.sync.dma_start(out=outv[:, b, c0:c1], in_=res[:])
 
         quant_h(0)
         top(0)

from contextlib import ExitStack

import concourse.mybir as mybir

K, T, H, N = 1024, 512, 512, 256
FLOPS = 2 * K * H * T + 2 * 2 * H * N * T

F32 = mybir.dt.float32
BF16 = mybir.dt.bfloat16
I32 = mybir.dt.int32
U32 = mybir.dt.uint32
U16 = mybir.dt.uint16
U8 = mybir.dt.uint8
FP8X4 = mybir.dt.float8_e4m3fn_x4
FP4X4 = mybir.dt.float4_e2m1fn_x4
ACT = mybir.ActivationFunctionType
ALU = mybir.AluOpType

P = 128
PACK = 4
PASSES = K // (P * PACK)
TH = T // 2
TQ = T // 4
ORDER = (3, 2, 1, 0)
PIECES = ((0, TH), (TH, TH + TQ), (TH + TQ, T))
CAST_V = 88
WIN = 2 * T
RUN = 4


def tile_picked_wsagecat_maxrelu_l_kernel(
    tc, x_words, x_scales, w1, w2_words, w2_scales, w3_words, w3_scales, pos1, pos2, pos3, out
):
    nc = tc.nc
    with ExitStack() as ctx:
        keep = ctx.enter_context(tc.tile_pool(name="keep", bufs=1))
        psum = ctx.enter_context(tc.psum_pool(name="psum", bufs=1))

        def tile(shape, dtype, name, on=None):
            return keep.tile(shape, dtype, name=name, tag=on or name, align_bytes=64)

        def bank(shape, name, b):
            return psum.tile(shape, F32, name=name, tag=f"bank{b}")

        lists = [keep.tile([P, T // 16], U16, name=f"list{d}") for d in range(3)]
        x_sc = tile([P, PASSES, T], U8, "x_sc")
        w_sc = tile([P, 2, N], U8, "w_sc")

        w1v = w1.rearrange("(z p j) c -> z p j c", z=PASSES, j=PACK)
        rows = {0: [(0, PACK)], 1: [(0, 2), (2, PACK)]}
        raw = {(z, j0): tile([P, j1 - j0, H], F32, f"raw{z}{j0}") for z in rows for j0, j1 in rows[z]}

        def load_w1(z):
            for j0, j1 in rows[z]:
                nc.sync.dma_start(out=raw[z, j0][:], in_=w1v[z, :, j0:j1, :])

        x_w = [tile([P, T], U32, f"x_w{z}") for z in range(PASSES)]
        xs_v = x_scales.bitcast(I32).rearrange("z (q r) c -> r q z c", r=PACK)
        xw_v = x_words.rearrange("z p c r -> z p (c r)").bitcast(I32)

        def load_x(z):
            nc.sync.dma_start(out=x_w[z][:].bitcast(I32), in_=xw_v[z])

        load_w1(0)
        load_x(0)
        for r in range(PACK):
            nc.sync.dma_start(out=x_sc[r:P:32, :, :].bitcast(I32), in_=xs_v[r])
        load_w1(1)
        load_x(1)
        for d, pos in enumerate((pos1, pos2, pos3)):
            nc.sync.dma_start(lists[d][:], pos)
        w_w = []
        for a, words in enumerate((w2_words, w3_words)):
            w_w.append(tile([P, 2 * N], U8, f"w_w{a}"))
            nc.sync.dma_start(out=w_w[a][:].bitcast(I32), in_=words[0].bitcast(I32))
        for a, scales in enumerate((w2_scales, w3_scales)):
            sv = scales[0].bitcast(I32).rearrange("(q r) c -> r q c", r=PACK)
            for r in range(PACK):
                nc.sync.dma_start(out=w_sc[r:P:32, a, :].bitcast(I32), in_=sv[r])

        wq = [tile([P, H, PACK], BF16, f"wq{z}") for z in range(PASSES)]
        wc, ws = {}, {}

        def cast(z):
            for j0, j1 in rows[z]:
                src = raw[z, j0][:].rearrange("p j (m t) -> p m t j", t=PACK)
                dst = wq[z][:, :, j0:j1].rearrange("p (t m) j -> p m t j", t=PACK)
                src, dst = (ap.rearrange("p m t j -> p m j t") for ap in (src, dst))
                for t0 in (2, 0):
                    pair = lambda ap: ap[:, :, :, t0 : t0 + 2]
                    nc.vector.tensor_copy(pair(dst[:, 0:CAST_V]), pair(src[:, 0:CAST_V]))
                    nc.scalar.activation(pair(dst[:, CAST_V:P]), pair(src[:, CAST_V:P]), ACT.Copy)

        def quantise(codes, scales, src):
            nc.vector.quantize_mx(out=codes.bitcast(FP8X4), scales=scales, in_=src.rearrange("p m j -> p (m j)"))

        cast(0)
        wc0 = tile([P, H], U32, "wc0")
        ws0 = tile([P, H], U8, "ws0")
        for cols in (slice(H // 2, H), slice(0, H // 2)):
            quantise(wc0[:, cols], ws0[:, cols], wq[0][:, cols, :])
        cast(1)
        for t in ORDER:
            wc[0, t], ws[0, t] = wc0[:, t * P : (t + 1) * P], ws0[:, t * P : (t + 1) * P]
            wc[1, t] = tile([P, P], U32, f"wc1{t}")[:]
            ws[1, t] = tile([P, P], U8, f"ws1{t}")[:]
            quantise(wc[1, t], ws[1, t], wq[1][:, t * P : (t + 1) * P, :])

        parts = [(t, s * TH, (s + 1) * TH, "sv"[s] if t else "s") for t in ORDER for s in range(2)]
        hb = [bank([P, c1 - c0], f"hb{b}", b) for b, (t, c0, c1, eng) in enumerate(parts)]
        for z in range(PASSES):
            for b, (t, c0, c1, eng) in enumerate(parts):
                nc.tensor.matmul_mx(
                    out=hb[b][:],
                    lhsT=wc[z, t].bitcast(FP8X4),
                    lhsT_scale=ws[z, t],
                    rhs=x_w[z][:, c0:c1].bitcast(FP8X4),
                    rhs_scale=x_sc[:, z, c0:c1],
                    start=(z == 0),
                    stop=(z == PASSES - 1),
                )

        win3 = tile([P, WIN], F32, "win3")
        hs = tile([P, PACK * WIN], F32, "hs")
        lane = lambda t: hs[:, t * WIN : t * WIN + T]
        window = {0: hs[:], 1: hs[:, WIN : 2 * WIN], 2: hs[:, 2 * WIN : 3 * WIN], 3: win3[:]}

        def gather(eng, t, d, dst, c0, c1):
            src = window[t].indirect(lists[d][:, c0 // 16 : c1 // 16])
            if eng == "v":
                nc.vector.tensor_copy(dst, src)
            else:
                nc.scalar.activation(dst, src, ACT.Copy)

        def relu(eng, dst, src):
            if eng == "v":
                nc.vector.tensor_scalar_max(dst, src, 0.0)
            else:
                nc.scalar.activation(dst, src, ACT.Relu)

        def largest(dst, a, b):
            nc.vector.tensor_tensor(dst, a, b, ALU.max)

        for b, (t, c0, c1, eng) in enumerate(parts):
            relu(eng, (win3[:, 0:T] if t == 3 else lane(t))[:, c0:c1], hb[b][:])
        nc.gpsimd.tensor_scalar(lane(3), win3[:, 0:T], 1.0, 0.0, ALU.mult, ALU.add)

        h4 = [tile([P, TH, PACK], BF16, f"h4{s}") for s in range(2)]
        hv = hs[:].rearrange("p (t v) -> p v t", t=PACK)
        for s in range(2):
            nc.gpsimd.tensor_scalar(h4[s][:], hv[:, s * TH : (s + 1) * TH, :], 1.0, 0.0, ALU.mult, ALU.add)

        third = tile([P, PACK, T], F32, "third", "x_w1")
        two = tile([P, PACK, T], BF16, "two")
        ab = {(t, d): tile([P, T], BF16, f"ab{t}{d}", ("wc10", "ws10")[d] if t == 3 else None) for t in (3, 0) for d in range(2)}
        a12 = tile([P, 2, 2, TH], BF16, "a12", "wc11")
        b12 = tile([P, 2, 2, TH], BF16, "b12", "ws11")

        def third_of(eng, t, c0, c1):
            gather(eng, t, 2, third[:, t, c0:c1], c0, c1)

        for t in (2, 1):
            for d, dst in enumerate((a12, b12)):
                gather("v", t, d, dst[:, :, t - 1, :], 0, T)
        third_of("v", 3, 0, TH)

        for t in (3, 0):
            for d in range(2):
                gather("s", t, d, ab[t, d][:], 0, T)
        for t in (1, 2, 0):
            third_of("s", t, 0, TH)
        for t in (1, 2, 3):
            third_of("s", t, TH, T)
        for c0, c1 in PIECES[1:]:
            third_of("s", 0, c0, c1)

        largest(two[:, 1:3, :].rearrange("p l (h v) -> p h l v", h=2), a12[:], b12[:])
        for t in (3, 0):
            largest(two[:, t, :], ab[t, 0][:], ab[t, 1][:])

        hc = [tile([P, TH], U32, f"hc{s}", (None, "ab00")[s]) for s in range(2)]
        hsc = tile([P, T], U8, "hsc")
        zc = tile([P, T], U32, "zc")
        zsc = tile([P, T], U8, "zsc")
        outv = out.rearrange("(b p) v -> p b v", p=P)
        SHARED = 1
        acc = {}
        for q, (c0, c1) in enumerate(PIECES):
            if q == SHARED:
                both = bank([P, 2, c1 - c0], "both", 0)
                acc[q, 0], acc[q, 1] = both[:, 0, :], both[:, 1, :]
            else:
                for b in range(2):
                    acc[q, b] = bank([P, c1 - c0], f"lone{q}{b}", ((1, 2), (), (3, 4))[q][b])[:]

        def second(q, a):
            c0, c1 = PIECES[q]
            for b in range(2):
                nc.tensor.matmul_mx(
                    out=acc[q, b],
                    lhsT=w_w[a][:, 2 * P * b : 2 * P * (b + 1)].bitcast(FP4X4),
                    lhsT_scale=w_sc[:, a, P * b : P * (b + 1)],
                    rhs=(hc[c0 // TH][:, c0 % TH : c0 % TH + c1 - c0], zc[:, c0:c1])[a].bitcast(FP8X4),
                    rhs_scale=(hsc, zsc)[a][:, c0:c1],
                    start=(a == 0 and (b == 0 or q != SHARED)),
                    stop=(a == 1 and (b == 1 or q != SHARED)),
                )

        def quant_h(s):
            cols = slice(s * TH, (s + 1) * TH)
            quantise(hc[s][:], hsc[:, cols], h4[s][:])
            for q in ((0,), (1, 2))[s]:
                second(q, 0)

        z4 = [tile([P, TH, PACK], BF16, f"z4{s}", "h40") for s in range(2)]
        runs = lambda ap: ap.rearrange("p t (c i) -> p c t i", i=RUN)

        def z_part(q):
            c0, c1 = PIECES[q]
            s = c0 // TH
            return z4[s][:, c0 - s * TH : c1 - s * TH, :]

        def top(q):
            c0, c1 = PIECES[q]
            largest(z_part(q).rearrange("p (c i) t -> p c t i", i=RUN), runs(two[:, :, c0:c1]), runs(third[:, :, c0:c1]))

        def finish(q):
            c0, c1 = PIECES[q]
            quantise(zc[:, c0:c1], zsc[:, c0:c1], z_part(q))
            second(q, 1)
            if q == SHARED:
                res = tile([P, 2, c1 - c0], F32, f"res{q}")
                relu("s", res[:], both[:])
                nc.sync.dma_start(out=outv[:, :, c0:c1], in_=res[:])
            else:
                for b, eng in enumerate("sv" if q else "ss"):
                    res = tile([P, c1 - c0], F32, f"res{q}{b}")
                    relu(eng, res[:], acc[q, b])
                    nc.sync.dma_start(out=outv[:, b, c0:c1], in_=res[:])

        quant_h(0)
        top(0)
        quant_h(1)
        finish(0)
        top(1)
        top(2)
        finish(1)
        finish(2)
